import numpy as np, ml_dtypes
CORES = [2,6,10,14,18,22,26,30]
N = 8
BF = ml_dtypes.bfloat16
W, C, H, CAP, RO = 2048, 1024, 1024, 96, 4
L = C >> 2
S16 = np.arange(16)
def owner(m):
    mb = np.zeros((8, W + 1), np.int32); mb[np.arange(8)[:, None, None], m] = np.arange(C)[None, :, None]
    return mb[:, :W]
def tight(m):
    return np.take_along_axis(m, np.argsort(m >= W, axis=-1, kind="stable"), -1)
def pick(a, j):
    return np.take_along_axis(a, j[:, :, None], 2)[:, :, 0]
def fill(n, order, s):
    s = np.minimum(s, 16 - n[order]); c = np.add.accumulate(s); left = W - np.add.reduce(n); n = n.copy()
    n[order] = n[order] + np.clip(left - (c - s), 0, s)
    return n
def sizes(rng):
    a = (W // C) * rng.choice(np.array([0.5, 1.0, 1.5]))
    n = fill(np.zeros(C, np.int64), rng.permutation(C), 1 + rng.poisson(a, C))
    return fill(n, rng.permutation(C), np.full(C, 16))
def seat(rng, n):
    m = np.full((C, 16), W, np.int64); m[S16 < n[:, None]] = rng.permutation(W)
    return m
def seats(rng):
    return np.stack([np.stack([seat(rng, sizes(rng)) for g in range(8)]) for q in range(N)])
def people(rng, m):
    typ = rng.integers(0, 16, (8, 24, 16)); own = np.take_along_axis(rng.integers(0, 24, (8, C)), owner(m), 1)
    ty = np.where(rng.random((8, W)) < rng.choice(np.array([0.3, 0.7, 0.95]), (8, 1)), own, rng.integers(0, 24, (8, W)))
    v = typ[np.arange(8)[:, None], ty]
    return np.clip(v + rng.integers(-3, 4, (8, W, 16)), 0, 15)
def wrap(x, a, m, li, w):
    def turn(v): return np.ascontiguousarray(v.transpose(0, 1, 3, 2)).reshape(N, 128, -1)
    return {"x0": turn(x).astype(np.float32).astype(BF), "ac": turn(a).astype(np.int32), "ml": turn(m).astype(np.int32),
            "lims": np.repeat(li, 16, axis=1).astype(np.int32), "wt": w.reshape(N, 128, 1).astype(np.int32)}
def setup_inputs(rng):
    m = seats(rng); x = np.stack([people(rng, b) for b in m])
    li = np.stack([rng.integers(30, 130, (N, 8)), rng.integers(20, 110, (N, 8))], axis=2)
    return wrap(x, rng.integers(0, W, (N, 8, H, 16)), m, li, rng.integers(0, 256, (N, 8, 16)))
def setup_inputs_ends(rng):
    ms, xs, as_, ls = [], [], [], []
    for q in range(N):
        m = []
        for g in range(8):
            n = np.zeros(C, np.int64); n[:4] = 16; n[C - 4:] = 16; o = 4 + rng.permutation(C - 8)
            n = fill(n, o, rng.choice(np.array([1, 1, 1, 16, 16, 8]), C - 8)); n = fill(n, o, np.full(C - 8, 16)); b = seat(rng, n)
            c = C - 4 + (g + q) % 4
            for v, k in ((0, 0), (W - 1, 15)):
                at = np.argwhere(b == v)[0]; b[at[0], at[1]] = b[c, k]; b[c, k] = v
            m.append(b)
        m = np.stack(m); ty = rng.integers(0, 5, (8, C, 1, 1)); ty[:, :4] = 4; ty[:, C - 4:] = 4
        edge = ((S16 != 2) & (S16 != 15))[None, None, :, None]
        val = np.where(ty == 0, True, np.where(ty == 1, False, np.where(ty == 2, rng.random((8, C, 16, 1)) < 0.5, np.where(ty == 3, rng.random((8, C, 16, 16)) < 0.5, edge))))
        x = np.zeros((8, W + 1, 16), np.int64); x[np.arange(8)[:, None, None], m] = 15 * val
        far = rng.random((8, H, 16)) < np.where(rng.random((8, H, 1)) < 0.4, 1.1, 0.55)
        ms.append(m); xs.append(x[:, :W]); as_.append(np.where(far, (W - 1) * rng.integers(0, 2, (8, H, 16)), rng.integers(0, W, (8, H, 16))))
        ls.append(np.array([[0, 0], [0, 240], [240, 0], [240, 240]])[(np.arange(8) // 2 + q) % 4])
    w = 255 * rng.integers(0, 2, (N, 8, 16)); w[:, 3::4] = 255; w[:, 1] = 0
    return wrap(np.stack(xs), np.stack(as_), np.stack(ms), np.stack(ls), w)
def setup_inputs_corners(rng):
    ms, xs, as_, ls = [], [], [], []
    for q in range(N):
        m = []; l = []; x = rng.integers(0, 16, (8, W, 16))
        for g in range(8):
            k = (g + q) & 7; n = np.zeros(C, np.int64); o = rng.permutation(C); z = 4 * rng.permutation(L); u = o[(o & 3) != 0]
            if k < 2:
                n[z[:CAP + k]] = 16; n = fill(n, u, rng.choice(np.array([1, 4, 8, 16]), len(u))); n = fill(n, u, np.full(len(u), 16))
            elif k == 2: n[:] = W // C
            elif k == 3:
                n[:] = W // C; n[o[:3]] = 0; n[o[3:6]] = 2 * (W // C)
            elif k == 4:
                n[z[:L // 2]] = 8; n = fill(n, u, rng.choice(np.array([8, 9]), len(u)))
            elif k == 5: n = fill(n, o, np.full(C, 16))
            elif k == 6:
                n[z] = 1; n = fill(n, u, rng.choice(np.array([15, 16]), len(u)))
            else:
                n = sizes(rng); x[g] = rng.integers(0, 2, (W, 16))
            m.append(seat(rng, n)); l.append(((0, 240), (0, 240), (240, 0), (0, 0), (240, 240), (240, 0), (240, 0), (int(rng.integers(2, 14)), int(rng.integers(2, 9))))[k])
        m = np.stack(m); mb = owner(m); mode = rng.integers(0, 6, (8, H, 1)); a = rng.integers(0, W, (8, H, 16)); zero = []
        for g in range(8):
            c0 = np.nonzero((mb[g] & 3) == 0)[0]
            if len(c0) == 0: c0 = np.arange(W)
            zero.append(c0[rng.integers(0, len(c0), (H, 16))])
        a = np.where(mode == 1, a[:, :, :1], np.where(mode == 2, (W - 1) * rng.integers(0, 2, (8, H, 16)), np.where(mode == 3, np.arange(H)[None, :, None] + H * rng.integers(0, W // H, (8, H, 16)),
            np.where(mode == 4, np.stack(zero), np.where(mode == 5, a[:, :, S16 & 1], a)))))
        ms.append(m); xs.append(x); as_.append(a); ls.append(np.array(l))
    w = np.where(rng.random((N, 8, 16)) < 0.5, rng.integers(0, 256, (N, 8, 16)), rng.choice(np.array([0, 1, 255]), (N, 8, 16)))
    return wrap(np.stack(xs), np.stack(as_), np.stack(ms), np.stack(ls), w)
def setup_inputs_brim(rng):
    ms, xs, as_, ls = [], [], [], []
    for q in range(N):
        m = []; l = []; x = rng.integers(0, 16, (8, W, 16)); a = rng.integers(0, W, (8, H, 16))
        for g in range(8):
            k = (g + q) & 3; n = np.zeros(C, np.int64); o = rng.permutation(C); z = 4 * rng.permutation(L); u = o[(o & 3) != 0][:L]
            if k == 1:
                n[z] = 1; n[u] = 2; n = fill(n, o, rng.choice(np.array([0, 2, 4, 6]), C)); n = fill(n, o, 8 - n[o])
            else:
                n[z] = 4; n = fill(n, rng.permutation(np.concatenate([z, u])), rng.choice(np.array([0, 1, 4, 8, 12]), 2 * L)); n = fill(n, rng.permutation(z), np.full(L, 12))
            b = seat(rng, n)
            if k == 1:
                old = b[z, rng.integers(0, n[z])]; h = rng.permutation(H)[:L]; new = h + H * rng.integers(0, W // H, L); p = np.full(W + 1, W)
                p[old] = new; p[np.setdiff1d(np.arange(W), old)] = rng.permutation(np.setdiff1d(np.arange(W), new)); b = p[b]
                x[g] = rng.integers(1, 16, (W, 16)); x[g, new] = 0
                x[g, b[u, 0]] = np.where(S16 == rng.integers(0, 16, (L, 1)), 0, 12); x[g, b[u, 1]] = np.where(S16 == rng.integers(0, 16, (L, 1)), 1, 12)
                a[g, h] = np.where((rng.random((L, 16)) < 0.25) & (S16 > 1), new[rng.integers(0, L, (L, 16))], np.where((S16 & 1) == 1, b[u, 0][:, None], b[np.roll(u, -1), 1][:, None]))
            elif k == 2:
                p = np.argsort(rng.random((L, 16)), axis=1); j = np.argsort(rng.random((L, 4)), axis=1); x[g] = rng.integers(1, 10, (W, 16))
                x[g, b[z, j[:, 0]]] = 0; x[g, b[z, j[:, 1]]] = np.where(p < 10, 15, np.where(p == 10, 1, 0)); x[g, b[z, j[:, 2]]] = np.where(p >= 6, 15, np.where(p < 2, 1, 0))
            elif k == 3:
                ty = rng.integers(0, 3, (W, 1)); x[g] = np.where(ty == 0, 15, np.where((ty == 1) & (S16 == rng.integers(0, 16, (W, 1))), 1, 0))
            m.append(b); l.append(((0, 0), (240, 0), (0, 0), (0, 239 + (g >> 2)))[k])
        ms.append(np.stack(m)); xs.append(x); as_.append(a); ls.append(np.array(l))
    return wrap(np.stack(xs), np.stack(as_), np.stack(ms), np.stack(ls), rng.integers(0, 256, (N, 8, 16)))
def setup_inputs_ties(rng):
    m = seats(rng); two = np.array([[0, 1], [7, 8], [0, 15], [3, 6]])[(np.arange(8)[None, :] + np.arange(N)[:, None]) & 3]
    pool = rng.integers(0, 2, (N, 8, 12, 16)); pool = np.where(pool == 1, two[:, :, None, 1:], two[:, :, None, :1])
    kind = rng.integers(0, 12, (N, 8, W)); x = pool[np.arange(N)[:, None, None], np.arange(8)[None, :, None], kind]
    step = two[:, :, 1] - two[:, :, 0]; li = np.stack([step * rng.integers(5, 14, (N, 8)), step * rng.integers(3, 11, (N, 8))], axis=2)
    known = rng.integers(0, W, (N, 8, 40)); k = rng.integers(0, 40, (N, 8, H * 16))
    a = np.where(rng.random((N, 8, H, 1)) < 0.5, np.take_along_axis(known, k, 2).reshape(N, 8, H, 16), rng.integers(0, W, (N, 8, H, 16)))
    return wrap(x, a, m, np.minimum(li, 240), rng.integers(0, 256, (N, 8, 16)))
def setup_inputs_spread(rng):
    x = rng.integers(0, 2 ** rng.integers(0, 5, (N, 8, W, 1)), (N, 8, W, 16)); m = []
    for q in range(N):
        for g in range(8):
            n = fill(np.zeros(C, np.int64), rng.permutation(C), rng.choice(np.array([0, 1, 1, 2, 3, 5, 16]), C)); m.append(seat(rng, fill(n, rng.permutation(C), np.full(C, 16))))
    a = np.minimum((W * rng.random((N, 8, H, 16)) ** 3).astype(np.int64), W - 1); w = np.minimum((np.exp2(8 * rng.random((N, 8, 16))) - 1).astype(np.int64), 255)
    return wrap(x, a, np.stack(m).reshape(N, 8, C, 16), rng.integers(0, 241, (N, 8, 2)), w)
def check_inputs(d):
    bad = []
    for k, lo, hi in (("x0", 0, 15), ("ac", 0, W - 1), ("ml", 0, W), ("lims", 0, 240), ("wt", 0, 255)):
        a = np.asarray(d[k]).astype(np.float64)
        if not (np.min(a) >= lo and np.max(a) <= hi): bad.append("range of " + k)
    a = np.asarray(d["x0"]).astype(np.float64)
    if np.any(a != np.floor(a)): bad.append("whole numbers in x0")
    m = np.asarray(d["ml"]).astype(np.int64).reshape(N, 8, 16, C)
    if np.any(np.sort(m.reshape(N, 8, 16 * C), axis=-1) != np.minimum(np.arange(16 * C), W)): bad.append("every agent once in ml")
    if np.any((m[:, :, 1:] < W) & (m[:, :, :-1] >= W)): bad.append("members before empty slots in ml")
    l = np.asarray(d["lims"]).reshape(N, 8, 16, 2)
    if np.any(l != l[:, :, :1]): bad.append("lims alike in a group")
    return bad
def reference(x0, ac, ml, lims, wt):
    X = np.zeros((N, 8, W + 1, 16), np.int32)
    X[:, :, :W] = x0.astype(np.float32).astype(np.int32).reshape(N, 8, 16, W).transpose(0, 1, 3, 2)
    A = ac.reshape(N, 8, 16, H).transpose(0, 1, 3, 2); M = np.array(ml.reshape(N, 8, 16, C).transpose(0, 1, 3, 2))
    lim = lims.reshape(N, 8, 16, 2)[:, :, 0].astype(np.int64); wv = wt.reshape(N, 8, 16).astype(np.int64)
    G = np.arange(8)[:, None]; G3 = G[:, :, None]; low = np.tri(L, L, -1, dtype=bool); z = np.zeros(N, np.int64)
    for t in range(RO):
        cl = t & 3; lane = 4 * np.arange(L) + cl; M2 = M.copy(); X2 = X.copy(); z2 = np.zeros(N, np.int64); go = []
        for r in range(N):
            x, m, mb = X[r], M[r], owner(M[r])
            own = m[:, lane]; here = own < W; live = here[:, :, 0]; tx = x[G3, own]; U = np.max(tx, axis=2)
            gr = np.where(here, np.sum(U[:, :, None] - tx, axis=3), -1); s = pick(own, np.argmax(gr, axis=2)); xs = x[G, s]
            ds = np.where(here, np.sum((tx - xs[:, :, None]) ** 2, axis=3), -1)
            an = A[r][G, s & (H - 1)]; ad = mb[G3, an]; fit = live[:, :, None] & ((ad & 3) != cl); has = np.any(fit, axis=2)
            d = pick(ad, np.argmin(np.where(fit, np.sum((x[G3, an] - xs[:, :, None]) ** 2, axis=3), 2 ** 20), axis=2))
            first = ~np.any((d[:, :, None] == d[:, None, :]) & has[:, None, :] & low, axis=2)
            dm = m[G, d]; dh = dm < W; td = x[G3, dm]; V = np.maximum(U, np.max(td, axis=2))[:, :, None]
            worst = np.maximum(np.max(np.where(here, np.sum(V - tx, axis=3), 0), axis=2), np.max(np.where(dh, np.sum(V - td, axis=3), 0), axis=2))
            mer = has & first & (np.sum(here, axis=2) + np.sum(dh, axis=2) <= 16) & (worst <= lim[r, :, :1] + (z[r] & 15))
            want = live & ~mer & (np.max(gr, axis=2) > lim[r, :, 1:])
            xg = x[G, pick(own, np.argmax(ds, axis=2))]; away = here & (np.sum((tx - xg[:, :, None]) ** 2, axis=3) < ds)
            vacant = m[:, :, 0] >= W; free = np.argsort(~vacant, axis=1, kind="stable")
            k = np.add.accumulate(want.astype(np.int64), axis=1) - want.astype(np.int64)
            spl = want & (k < np.sum(vacant, axis=1)[:, None]); e = np.take_along_axis(free, k, 1)
            both = tight(np.concatenate([own, dm], axis=2))[:, :, :16]
            M2[r][:, lane] = np.where(mer[:, :, None], both, np.where(spl[:, :, None], tight(np.where(away, W, own)), own))
            a, b = np.nonzero(mer); M2[r][a, d[a, b]] = W
            a, b = np.nonzero(spl); M2[r][a, e[a, b]] = tight(np.where(away, own, W))[a, b]
            idle = live & ~mer & ~spl; a, b = np.nonzero(idle & (np.add.accumulate(idle.astype(np.int64), axis=1) <= CAP))
            go.append((a, s[a, b], xs[a, b])); z2[r] = np.sum(mer)
        for r in range(N):
            q = (r + 1 + t % (N - 1)) % N; a, sa, xa = go[r]
            v = np.sum(wv[q][a] * xa, axis=1) & (W - 1); mm = M2[q][a, owner(M2[q])[a, v]]; y = X[q][a[:, None], mm]
            j = np.argmin(np.where(mm < W, np.sum((y - xa[:, None]) ** 2, axis=2), 2 ** 20), axis=1)
            X2[r][a, sa] = (xa + y[np.arange(len(a)), j]) >> 1
        X, M, z = X2, M2, z2
    return {"ym": np.ascontiguousarray(M.transpose(0, 1, 3, 2)).reshape(N, 128, C).astype(np.float32),
            "yx": np.ascontiguousarray(X[:, :, :W].transpose(0, 1, 3, 2)).reshape(N, 128, W).astype(np.float32).astype(BF)}

@@ -1,0 +1,906 @@
+from concourse.mybir import AluOpType as O, ActivationFunctionType as AF, AxisListType as AX
+
+F4, B2, H2, I4, U2 = "float32", "bfloat16", "float16", "int32", "uint16"
+SCRATCH = {}
+for _n, _w, _d in [
+        ("xa", 2304, B2), ("xc", 2304, B2), ("xs", 2304, B2), ("ra", 2048, F4), ("rb", 2048, F4), ("r16", 2064, H2),
+        ("at", 2048, F4), ("bt", 1536, F4), ("sz", 1536, F4), ("el", 1280, F4), ("ks", 4128, F4),
+        ("gt", 2048, F4), ("g16", 2048, H2), ("df", 2048, B2), ("xr", 2048, B2), ("zb", 2048, B2), ("sqs", 2048, B2),
+        ("eq", 1024, B2), ("bw", 2048, B2), ("sets", 14336, H2), ("wts", 2048, B2), ("orp", 2048, H2),
+        ("mlt", 1024, I4), ("act", 1024, I4), ("d0", 1024, B2), ("ck16", 1024, H2),
+        ("mr", 1536, B2), ("ones", 512, B2), ("us", 2048, B2), ("rl", 2048, B2), ("m0", 2048, B2), ("rk", 2048, H2),
+        ("bt16", 1024, H2), ("xl", 1024, B2), ("xb", 1024, B2), ("wm", 3968, H2), ("wb", 1664, B2),
+        ("xsb", 256, B2), ("xbb", 256, B2), ("uc", 256, B2), ("ud", 256, B2), ("uv", 256, B2), ("acq", 256, U2), ("ai", 512, I4),
+        ("ahl", 512, F4), ("mrb", 512, B2), ("tg", 512, F4), ("tt", 512, F4),
+        ("ag16", 256, H2), ("eg16", 256, H2), ("drep", 256, H2), ("x16", 1024, H2), ("bl16", 256, H2), ("lt16", 256, H2),
+        ("dvt", 256, F4), ("lft", 256, F4), ("sze", 256, F4), ("zd", 256, F4), ("ctr", 256, F4),
+        ("vs", 352, B2), ("res", 352, B2), ("vag", 96, H2), ("yv", 96, B2), ("ri", 96, I4), ("nx", 256, B2),
+        ("sm", 2800, F4), ("si", 416, I4), ("su", 1120, U2), ("sh", 288, H2), ("sb", 160, B2), ("lim", 2, I4), ("wtc", 1, I4)]:
+    SCRATCH[_n] = ("sbuf", [128, _w], _d)
+for _t in range(4):
+    SCRATCH["in%d" % _t] = ("sbuf", [128, 96], B2)
+    SCRATCH["ry%d" % _t] = ("sbuf", [128, 96], B2)
+SCRATCH["psA"] = ("psum", [128, 2048], F4)
+SCRATCH["psB"] = ("psum", [128, 2048], F4)
+SEMAPHORES = ["sv", "ss", "st", "sg"] + ["d%d" % i for i in range(12)]
+for _t in range(4):
+    SEMAPHORES += ["ra%d" % _t, "rb%d" % _t, "la%d" % _t, "lb%d" % _t]
+BIG = 33554432.0
+
+
+def rank_program(g, core, T, topo):
+    rank = T.rank_of(core)
+    if rank is None:
+        return
+    Q = {"v": g.vector, "s": g.scalar, "t": g.tensor, "g": g, "y": g.sync}
+    SEM = {"v": "sv", "s": "ss", "t": "st", "g": "sg"}
+    cnt = {"v": 0, "s": 0, "t": 0, "g": 0}
+    know = {e: {} for e in Q}
+    hist = {}
+    recs = {}
+
+    def A(n, a=0, b=None, s=1):
+        return (n, a, SCRATCH[n][1][1] if b is None else b, s)
+
+    def X(w, o):
+        return ("X", w, o, 0)
+
+    def ap(x):
+        if not isinstance(x, tuple):
+            return x
+        if x[0] == "X":
+            return ap(x[1]).indirect(ap(x[2]))
+        n, a, b, s = x
+        return T[n][:, a:b] if s == 1 else T[n][:, a:b:s]
+
+    def sub(x, a, b, s=1):
+        return (x[0], x[1] + a, x[1] + b, s)
+
+    def touch(e, outs, ins, seq_e):
+        acc = []
+        for x, w in [(o, True) for o in outs] + [(i, False) for i in ins]:
+            if not isinstance(x, tuple):
+                continue
+            for y, ww in ([(x[1], w), (x[2], False)] if x[0] == "X" else [(x, w)]):
+                n, a, b, s = y
+                if n[:2] == "ps":
+                    for k in range(a // 512, (b - 1) // 512 + 1):
+                        acc.append((n, 512 * k, 512 * k + 512, True, True))
+                else:
+                    acc.append((n, a, b, ww, False))
+        need = {}
+        for n, a, b, w, ps in acc:
+            for r in recs.get(n, []):
+                if r[0] < b and a < r[1] and (w or r[4]) and not (r[2] == seq_e[0] and r[2][0] == "D") and not (ps and r[2] == e and e == "t"):
+                    need[r[2]] = max(need.get(r[2], 0), r[3])
+        for x in sorted(need):
+            if know[e].get(x, 0) < need[x]:
+                Q[e].wait_ge(T.sem[SEM[x]], need[x])
+                for k, v in hist[(x, need[x])].items():
+                    know[e][k] = max(know[e].get(k, 0), v)
+                know[e][x] = need[x]
+        who, seq = seq_e
+        hist[(who, seq)] = dict(know[e])
+        for n, a, b, w, ps in acc:
+            L = recs.setdefault(n, [])
+            if w:
+                L[:] = [r for r in L if not (a <= r[0] and r[1] <= b)]
+                L.append([a, b, who, seq, True])
+            else:
+                for r in L:
+                    if r[0] == a and r[1] == b and r[2] == who and not r[4]:
+                        r[3] = seq
+                        break
+                else:
+                    L.append([a, b, who, seq, False])
+
+    def emit(e, fn, outs, ins):
+        cnt[e] += 1
+        touch(e, outs, ins, (e, cnt[e]))
+        fn().then_inc(T.sem[SEM[e]], 1)
+
+    def cp(out, i, e="v"):
+        if e == "s":
+            act(out, i, AF.Copy)
+        else:
+            emit("v", lambda: g.vector.tensor_copy(ap(out), ap(i)), [out], [i])
+
+    def tt(out, a, b, op):
+        emit("v", lambda: g.vector.tensor_tensor(ap(out), ap(a), ap(b), op), [out], [a, b])
+
+    def ts(out, a, s1, op0, s2=None, op1=None):
+        if op1 is None:
+            emit("v", lambda: g.vector.tensor_scalar(ap(out), ap(a), ap(s1), None, op0), [out], [a, s1])
+        else:
+            emit("v", lambda: g.vector.tensor_scalar(ap(out), ap(a), ap(s1), ap(s2), op0, op1), [out], [a, s1, s2])
+
+    def scan(out, d0, d1, op0, op1):
+        emit("v", lambda: g.vector.tensor_tensor_scan(ap(out), ap(d0), ap(d1), 0.0, op0, op1), [out], [d0, d1])
+
+    def vtr(out, i):
+        emit("v", lambda: g.vector.transpose(ap(out), ap(i)), [out], [i])
+
+    def ms(out, c):
+        emit("v", lambda: g.vector.memset(ap(out), c), [out], [])
+
+    def act(out, i, f, scale=1.0):
+        emit("s", lambda: g.scalar.activation(ap(out), ap(i), f, scale=ap(scale)), [out], [i, scale])
+
+    def mm(out, l, r, start=True, stop=True):
+        emit("t", lambda: g.tensor.matmul(ap(out), ap(l), ap(r), start, stop), [out], [l, r])
+
+    def mms(out, pairs):
+        for k, (l, r) in enumerate(pairs):
+            mm(out, l, r, k == 0, k == len(pairs) - 1)
+
+    def asel(out, i, pat, op, base, cm):
+        emit("g", lambda: g.affine_select(ap(out), ap(i), pat, op, 0.0, base, cm), [out], [i])
+
+    def iota(out, pat, base, cm):
+        emit("g", lambda: g.iota(ap(out), pat, base, cm, allow_small_or_imprecise_dtypes=True), [out], [])
+
+    nd = [0]
+
+    def dmas(e, pairs):
+        who = "D%d" % nd[0]
+        SEM[who] = "d%d" % nd[0]
+        nd[0] += 1
+        for k, (o, i, oa, ia) in enumerate(pairs):
+            touch(e, [o] if o else [], [i] if i else [], (who, 16 * len(pairs)))
+            Q[e].dma_start(oa, ia).then_inc(T.sem[SEM[who]], 16)
+        return who, 16 * len(pairs)
+
+    fin = []
+    slots = {}
+    used = {"sm": 0, "si": 0, "su": 0, "sh": 0, "sb": 0}
+
+    def S(buf, name, w=16):
+        if (buf, name) not in slots:
+            slots[(buf, name)] = A(buf, used[buf], used[buf] + w)
+            used[buf] += (w + 15) // 16 * 16
+        return slots[(buf, name)]
+
+    def F(name, w=16):
+        return S("sm", name, w)
+
+    for n, src in (("mlt", T.ml), ("xa", T.x0), ("act", T.ac), ("lim", T.lims), ("wtc", T.wt)):
+        w = src.shape[1]
+        fin.append(dmas("y" if n != "act" else "s", [(A(n, 0, w), None, T[n][:, 0:w], src[:, 0:w])]))
+
+    ms(A("ones"), 1.0)
+    ms(A("rl"), 1.0)
+    iota(F("i16"), [[1, 16]], 0, 0)
+    iota(F("pi", 1), [[0, 1]], 0, 1)
+    cp1 = A("el", 0, 1024)
+    iota(cp1, [[1, 1024]], 1, 0)
+    iota(F("l16"), [[16, 16]], 0, 0)
+    iota(F("c64", 64), [[16, 64]], 0, 0)
+    m8 = A("tg", 384, 512)
+    iota(m8, [[1, 128]], 0, 0)
+    wb = {}
+
+    def W1(name, buf="wb"):
+        k = (buf, name)
+        if k not in wb:
+            i = len([1 for z in wb if z[0] == buf])
+            wb[k] = A(buf, 128 * i, 128 * i + 128)
+        return wb[k]
+
+    o128 = A("ones", 0, 128)
+    BB, ID, SP, SN, TW = W1("BB"), W1("ID"), W1("SP"), W1("SN"), W1("TW")
+    asel(BB, o128, [[-16, 8], [0, 16]], O.is_ge, 0, 1)
+    asel(BB, BB, [[16, 8], [0, 16]], O.is_ge, 15, -1)
+    asel(ID, o128, [[-1, 128]], O.is_equal, 0, 1)
+    asel(A("bw"), A("rl"), [[1, 16], [0, 8], [-1, 16]], O.is_equal, 0, 0)
+    asel(A("bw"), A("bw"), [[0, 16], [-16, 8], [0, 16]], O.is_ge, 0, 1)
+    asel(A("bw"), A("bw"), [[0, 16], [16, 8], [0, 16]], O.is_ge, 15, -1)
+    asel(SP, o128, [[-1, 128]], O.is_equal, 16, 1)
+    asel(SN, o128, [[-1, 128]], O.is_equal, -16, 1)
+    asel(TW, BB, [[1, 128]], O.is_gt, 0, -1)
+    iota(A("rb"), [[1, 2048]], 0, 0)
+    pi = S("si", "pi", 1)
+    kcol, mO, mE = F("kcol", 1), F("mO", 1), F("mE", 1)
+    cp(pi, F("pi", 1))
+    ts(S("si", "p2", 1), pi, 15, O.bitwise_and)
+    cp(kcol, S("si", "p2", 1))
+    ts(S("si", "p2", 1), pi, 4, O.arith_shift_right, 1, O.bitwise_and)
+    cp(mO, S("si", "p2", 1))
+    ts(mE, mO, -1.0, O.mult, 1.0, O.add)
+    ts(F("mE4", 1), mE, 4096.0, O.mult)
+    ts(F("mO4", 1), mO, 4096.0, O.mult)
+    ts(F("k128", 1), kcol, 128.0, O.mult)
+    ts(F("k11", 1), kcol, -11.0, O.add)
+    rm = F("rm")
+    ts(rm, F("i16"), kcol, O.is_equal)
+
+    def RM(r):
+        return sub(rm, r, r + 1)
+
+    def coef(name, terms):
+        c = F("c_" + name, 1)
+        r0, w0 = terms[0]
+        ts(c, RM(r0), float(w0), O.mult)
+        for r, w in terms[1:]:
+            ts(F("c_t", 1), RM(r), float(w), O.mult)
+            tt(c, c, F("c_t", 1), O.add)
+        return c
+
+    lane, c4 = F("lane"), F("c4", 64)
+    ts(lane, F("l16"), kcol, O.add)
+    ts(c4, F("c64", 64), kcol, O.add)
+    ts(S("sb", "tri"), F("i16"), kcol, O.is_gt)
+    ci, ck0, ck1 = A("ai"), A("ks", 0, 512), A("ks", 512, 1024)
+    for h in (0, 1):
+        cpart = A("el", 512 * h, 512 * h + 512)
+        ts(ck0, cpart, -1.0, O.add)
+        cp(ci, ck0)
+        ts(ci, ci, 3, O.bitwise_and)
+        ts(ck1, ci, F("k11", 1), O.is_equal)
+        ts(ck0, ck0, RM(8), O.mult)
+        tt(A("ck16", 512 * h, 512 * h + 512), ck0, ck1, O.add)
+    ts(A("d0"), A("rl", 0, 1024), RM(2), O.mult)
+
+    def mk(name, src, col, w=1.0, buf="wm"):
+        m = W1(name, buf)
+        ts(m, src, col, O.mult, float(w), O.mult)
+        return m
+
+    one = F("one1", 1)
+    ms(one, 1.0)
+    I16 = mk("I16", ID, one)
+    mi = S("si", "mi", 128)
+    par, ta, tb = A("tg", 256, 384), A("tg", 0, 128), A("tg", 128, 256)
+    cp(mi, m8)
+    ts(mi, mi, 15, O.bitwise_and)
+    ts(ta, mi, 2.0, O.is_equal)
+    for r in (3.0, 7.0):
+        ts(tb, mi, r, O.is_equal)
+        tt(ta, ta, tb, O.add)
+    BB237 = W1("BB237", "wb")
+    tt(BB237, BB, ta, O.mult)
+    ts(A("us", 0, 1024), A("mlt"), 2048.0, O.is_lt)
+    for k in range(2):
+        mms(A("psB", 512 * k, 512 * k + 512), [(BB237, A("us", 512 * k, 512 * k + 512)), (I16, A("ck16", 512 * k, 512 * k + 512))])
+    cp(A("sz", 0, 1024), A("psB", 0, 1024))
+    scan(A("bt", 0, 1024), A("d0"), A("sz", 0, 1024), O.mult, O.add)
+    cp(A("bt16"), A("bt", 0, 1024))
+    cp(A("lt16"), A("bt", 0, 1024, 4))
+    ms(A("ks", 0, 2048), 0.0)
+    names = ["E", "n", "r8", "cid", "P", "np", "st"]
+    terms = [[(2, 1), (3, -1), (6, 1), (7, 1)], [(7, 1)], [(8, 1)], [(1, 1)], [(0, 16), (10, 1)], [(2, 1), (3, -1), (5, 1)], [(2, 1), (3, -1), (6, 1)]]
+    ccol = {}
+
+    def setof(name):
+        i = names.index(name)
+        return lambda w: A("sets", 2048 * i + 128 * w, 2048 * i + 128 * w + 128)
+    for i, nm in enumerate(names):
+        ccol[nm] = coef(nm, terms[i])
+    for nm in ("np", "n", "cid", "P", "E", "r8", "st"):
+        i = names.index(nm)
+        act(A("sets", 2048 * i, 2048 * i + 2048), A("bw"), AF.Copy, ccol[nm])
+    wf = F("wf", 1)
+    cp(wf, A("wtc"))
+    act(A("wts"), A("bw"), AF.Copy, wf)
+
+    def bws(w):
+        return A("bw", 128 * w, 128 * w + 128)
+
+    s0s = setof("cid")
+
+    def wtw(w):
+        return A("wts", 128 * w, 128 * w + 128)
+
+    def ors(w):
+        return A("orp", 128 * w, 128 * w + 128)
+    for w in range(16):
+        ts(ors(w), BB, RM(w), O.mult)
+
+    PE_, PO_, P01, P10 = mk("PE", ID, mE), mk("PO", ID, mO), mk("P01", SP, mE), mk("P10", SN, mO)
+    BBK, BBS, BBN = mk("BBK", BB, one, 2048.0, "wb"), mk("BBS", BB, one, -8.0, "wb"), mk("BBN", BB, one, -1.0, "wb")
+    RKS, RKB = mk("RKS", BB, RM(0), -0.5), mk("RKB", BB, RM(0), -128.0)
+    BB16 = mk("BB16", BB, one)
+    RPS = mk("RPS", BB, coef("ks", [(0, 2.0 ** -8), (10, 2.0 ** -12), (9, 2048)]))
+    CDP, CDN = mk("CDP", BB, RM(1)), mk("CDN", BB, RM(1), -1.0)
+    STR, NRP = mk("STR", BB, ccol["st"]), mk("NRP", BB, ccol["n"])
+    CLS = [mk("CLS%d" % m, BB, RM(11 + m), 64.0, "wb") for m in range(4)]
+    ts(mi, mi, 1, O.bitwise_and)
+    cp(par, mi)
+    RPB = W1("RPB", "wm")
+    ts(ta, BB, coef("kb1", [(10, 1.0), (0, -1.0)]), O.mult)
+    tt(ta, ta, par, O.mult)
+    ts(tb, BB, coef("kb2", [(0, 1.0), (9, 2048.0)]), O.mult)
+    tt(RPB, ta, tb, O.add)
+
+    def rowmap(name, src, rows, w=1.0):
+        m = W1(name, "wm")
+        ts(ta, bws(rows[0]), RM(src), O.mult, float(w), O.mult)
+        for r in rows[1:]:
+            ts(tb, bws(r), RM(src), O.mult, float(w), O.mult)
+            tt(ta, ta, tb, O.add)
+        cp(m, ta)
+        return m
+    M237, M237N, M7N = rowmap("M237", 0, [2, 3, 7]), rowmap("M237N", 0, [2, 3, 7], -1), rowmap("M7N", 0, [7], -1)
+    M5, M1N, M81, M81N, M56 = rowmap("M5", 0, [5]), rowmap("M1N", 0, [1], -1), rowmap("M81", 8, [1]), rowmap("M81N", 8, [1], -1), rowmap("M56", 0, [5, 6])
+    M567 = W1("M567", "wm")
+    tt(M567, M7N, M56, O.add)
+    ts(M567, M567, -1.0, O.mult)
+    I23 = mk("I23", ID, coef("i23", [(2, 1), (3, 1)]))
+    IX = W1("IX", "wm")
+    tt(IX, I16, M81, O.add)
+    RPP = mk("RPP", BB, ccol["P"])
+    H0, PX10, H10, C1 = rowmap("H0", 0, [0]), W1("PX10", "wm"), rowmap("H10", 0, [10], -16), rowmap("C1", 0, [1])
+    cp(PX10, bws(10))
+    ms(A("mr"), 1.0)
+    ms(A("mr", 0, 1536, 16), 0.0)
+    ms(A("mrb"), 0.0)
+    ms(A("mrb", 0, 512, 16), BIG)
+    for n in ("zb", "eq", "xl", "xb"):
+        ms(A(n), 0.0)
+    ms(A("vs"), 0.0)
+    ms(A("zd"), 0.0)
+    ms(F("neg"), -1.0)
+    cp(A("r16", 0, 16), F("neg"))
+    lims = F("lims", 2)
+    cp(lims, A("lim"))
+    limz = F("limz", 1)
+    cp(limz, sub(lims, 0, 1))
+
+    def gathO(src, a, n, st, out):
+        for w in range(16):
+            mm(out, st(w), A(src, a + w, a + n, 16), w == 0, w == 15)
+
+    def s2o(r1, out, n):
+        mms(sub(out, 0, n, 2), [(PE_, sub(r1, 0, n, 2)), (P01, sub(r1, 1, n, 2))])
+        mms(sub(out, 1, n, 2), [(P10, sub(r1, 0, n, 2)), (PO_, sub(r1, 1, n, 2))])
+
+    def lanes_of(win, dup):
+        cp(A("tg"), X(win, dup))
+        vtr(A("tt"), A("tg"))
+
+    def sel(out, r, me=mE, mo=mO):
+        ts(F("selA"), A("tt", r, 512, 32), me, O.mult)
+        ts(F("selB"), A("tt", 16 + r, 512, 32), mo, O.mult)
+        tt(out, F("selA"), F("selB"), O.add)
+
+    def prefix(ind, n, out, tag, ps):
+        mm(sub(ps, 0, n), TW, ind)
+        mm(sub(ps, n, 2 * n), BB, ind)
+        cp(F(tag + "tot", n), sub(ps, n, 2 * n))
+        inc = F(tag + "inc", n)
+        scan(inc, A("ones", 0, n), F(tag + "tot", n), O.mult, O.add)
+        tt(out, inc, F(tag + "tot", n), O.subtract)
+        tt(out, out, sub(ps, 0, n), O.add)
+        return sub(inc, n - 1, n)
+
+    def lt(name):
+        return F(name)
+
+    def choose(out, cond, a, b, tmp="chT", w=16):
+        d = F(tmp + str(w), w)
+        tt(d, a, b, O.subtract)
+        tt(d, d, cond, O.mult)
+        tt(out, d, b, O.add)
+
+    B0, B1, B2_, B3 = [A("psB", 512 * k, 512 * k + 512) for k in range(4)]
+    PO, CQ, CQF = S("su", "po", 128), S("su", "cq", 128), F("cqf", 128)
+
+    def chunks(off, k, n):
+        w = (off[2] - off[1]) // n
+        return sub(off, k * w, k * w + w)
+
+    def order_tables(R, last):
+        for k in range(4):
+            act(A("r16", 16 + 512 * k, 528 + 512 * k), A(R, 512 * k, 512 * k + 512), AF.Copy)
+        gathO("r16", 16, 2048, setof("P"), sub(B1, 0, 128))
+        cp(PO, sub(B1, 0, 128))
+        gather_xs()
+        if last:
+            return
+        for k in range(4):
+            c = (B0, B2_)[k % 2]
+            mms(c, [(CDP, A("r16", 16 + 512 * k, 528 + 512 * k)), (CDN, A("r16", 15 + 512 * k, 527 + 512 * k))])
+            ts(A("m0", 512 * k, 512 * k + 512), c, 0.0, O.is_equal)
+        gathO("r16", 16, 2048, setof("cid"), sub(B2_, 0, 128))
+        cp(CQF, sub(B2_, 0, 128))
+        cp(CQ, CQF)
+        scan(A("rk"), A("m0"), A("m0"), O.mult, O.add)
+
+    def gather_xs():
+        cp(A("xs", 1024, 2048), X(A("xa", 0, 2048), chunks(PO, 1, 2)))
+        for k in range(2):
+            act(A("xs", 512 * k, 512 * k + 512), X(A("xa", 0, 2048), chunks(PO, k, 4)), AF.Copy)
+
+    POS = S("su", "pos", 128)
+
+    def agents():
+        for k in range(4):
+            act(A("at", 512 * k, 512 * k + 512), X(A("gt", 0, 2048), chunks(POS, k, 4)), AF.Copy)
+
+    def build_xc(m):
+        act(A("rl"), A("at"), AF.Copy)
+        for k in range(4):
+            c = (B0, B3)[k % 2]
+            mms(c, [(ID, A("xa", 512 * k, 512 * k + 512)), (CLS[m], A("rl", 512 * k, 512 * k + 512))])
+            act(A("xc", 512 * k, 512 * k + 512), c, AF.Copy)
+
+    def new_pos():
+        for k in range(4):
+            act(A("gt", 512 * k, 512 * k + 512), X(A("ks", 2080, 4128), chunks(POS, k, 4)), AF.Copy)
+            act(A("g16", 512 * k, 512 * k + 512), A("gt", 512 * k, 512 * k + 512), AF.Copy)
+
+    def s_keys():
+        for k in range(4):
+            mm(A("psA", 512 * k, 512 * k + 512), RKS, A("rk", 512 * k, 512 * k + 512), True, False)
+            mm(A("psA", 512 * k, 512 * k + 512), RPS, A("r16", 16 + 512 * k, 528 + 512 * k), False, False)
+        for k in range(4):
+            mm(A("psA", 512 * k, 512 * k + 512), BBS, A("xs", 512 * k, 512 * k + 512), False, True)
+
+    def u_scan():
+        scan(A("us"), A("m0"), A("xs", 0, 2048), O.mult, O.max)
+
+    def k_scan():
+        scan(A("ks", 0, 2048), A("m0"), A("psA"), O.mult, O.max)
+
+    def empties():
+        act(A("bt16"), A("sz", 0, 1024), AF.Copy)
+        gathO("bt16", 0, 1024, setof("n"), sub(B2_, 0, 64))
+        e64, r64 = F("e64", 64), F("r64", 64)
+        ts(e64, sub(B2_, 0, 64), 0.5, O.is_lt)
+        cp(S("sb", "e64", 64), e64)
+        e = prefix(S("sb", "e64", 64), 64, r64, "pe", sub(B2_, 64, 192))
+        cp(F("ecnt", 1), e)
+        ts(F("t64", 64), c4, 256.0, O.add)
+        ts(F("u64", 64), r64, 255.5, O.is_lt)
+        tt(e64, e64, F("u64", 64), O.mult)
+        choose(r64, e64, r64, F("t64", 64), "ch64", 64)
+        cp(S("su", "l64", 64), r64)
+        cp(X(A("el"), S("su", "l64", 64)), A("ck16"))
+
+    def send(dst, out, src, rs, ls):
+        rid, pid, _ = topo.addr(dst)
+        es = topo.engines(core, dst)[:4]
+        m = 0
+        for e in es:
+            m |= 1 << e
+        SEM[ls] = ls
+        touch("g", [], [src], (ls, len(es)))
+        g.remote_dma(out_ap=T[out][:], in_ap=ap(src), remote_sem=T.sem[rs], local_sem=T.sem[ls], pid=pid, routing_id=rid, dma_engine_mask=m)
+        fin.append((ls, len(es)))
+
+    def arrived(buf, rs, src):
+        n = len(topo.engines(src, core)[:4])
+        SEM[rs] = rs
+        hist[(rs, n)] = {}
+        recs.setdefault(buf, []).append([0, 96, rs, n, True])
+        fin.append((rs, n))
+
+    def visits(t, q, h):
+        IN = "in%d" % t
+        arrived(IN, "ra%d" % t, h)
+        for w in range(16):
+            mm(sub(B3, 0, 6), wtw(w), A(IN, w, 96, 16), w == 0, w == 15)
+        vi = S("si", "vi", 6)
+        cp(vi, sub(B3, 0, 6))
+        ts(vi, vi, 2047, O.bitwise_and)
+        cp(S("su", "vi", 6), vi)
+        cp(A("vag"), X(A("at"), S("su", "vi", 6)))
+        mm(sub(B3, 16, 112), STR, A("vag"))
+        mm(sub(B3, 112, 208), NRP, A("vag"))
+        cp(A("zb", 0, 1536, 16), A(IN))
+        scan(A("xr", 0, 1536), A("mr", 0, 1536), A("zb", 0, 1536), O.mult, O.add)
+        yield
+        hl = F("hl", 96)
+        ts(hl, sub(B3, 112, 208), -1.0, O.add, kcol, O.min)
+        tt(hl, hl, sub(B3, 16, 112), O.add)
+        cp(S("su", "hl", 96), hl)
+        hx = A("sqs", 0, 1536)
+        tt(hx, X(A("xs", 0, 2048), S("su", "hl", 96)), A("xr", 0, 1536), O.subtract)
+        act(hx, hx, AF.Square)
+        for w in range(16):
+            mm(sub(B3, 208, 214), setof("st")(w), A("vag", w, 96, 16), w == 0, w == 15)
+        for i in range(16):
+            mm(sub(B0, 256, 352), bws(i), A("sqs", i, 1536, 16), i == 0, i == 15)
+        yield
+        ts(A("tg", 0, 96), sub(B0, 256, 352), 16.0, O.mult, kcol, O.add)
+        vtr(A("tt", 0, 96), A("tg", 0, 96))
+        scan(A("tg", 0, 96), A("mrb", 0, 96), A("tt", 0, 96), O.max, O.min)
+        k6 = S("si", "k6", 6)
+        cp(k6, A("tg", 15, 96, 16))
+        ts(k6, k6, 15, O.bitwise_and)
+        cp(S("sh", "k6", 6), k6)
+        s2o(S("sh", "k6", 6), sub(B3, 224, 230), 6)
+        yield
+        y6 = F("y6", 6)
+        cp(y6, sub(B3, 224, 230))
+        tt(y6, y6, sub(B3, 208, 214), O.add)
+        cp(S("su", "y6", 6), y6)
+        cp(A("yv"), X(A("xs", 0, 2048), S("su", "y6", 6)))
+        send(h, "ry%d" % t, A("yv"), "rb%d" % t, "lb%d" % t)
+        yield
+        arrived("ry%d" % t, "rb%d" % t, q)
+        tt(A("ri"), A("ry%d" % t), A("vs", 0, 96), O.add)
+        ts(A("ri"), A("ri"), 1, O.arith_shift_right)
+        cp(A("res", 0, 96), A("ri"))
+        cp(A("nx"), X(A("res"), S("su", "vL")))
+        cp(X(A("xa"), S("su", "vA")), A("nx"))
+        if t < 3:
+            cp(X(A("xs"), S("su", "vP")), A("nx"))
+            cp(X(A("xc"), S("su", "vA")), A("nx"))
+        yield
+
+    gathO("bt16", 0, 1024, setof("np"), sub(B2_, 0, 64))
+    gathO("bt16", 0, 1024, setof("n"), sub(B2_, 64, 128))
+    t64, u64 = F("t64", 64), F("u64", 64)
+    ts(t64, c4, 2048.0, O.add)
+    ts(u64, sub(B2_, 64, 128), 0.5, O.is_gt)
+    s64 = F("s64", 64)
+    cp(s64, sub(B2_, 0, 64))
+    choose(s64, u64, s64, t64, "ch64", 64)
+    cp(S("su", "l64", 64), s64)
+    cp(X(A("ks", 0, 3072), S("su", "l64", 64)), cp1)
+    ts(A("m0"), A("ks", 0, 2048), 0.0, O.is_equal)
+    scan(A("g16"), A("m0"), A("ks", 0, 2048), O.mult, O.add)
+    ms(A("el"), 0.0)
+    r91 = coef("r91", [(9, 1), (1, -1)])
+    gathO("g16", 0, 2048, s0s, sub(B2_, 0, 128))
+    ts(CQF, sub(B2_, 0, 128), -1.0, O.add)
+    cp(CQ, CQF)
+    scan(A("rk"), A("m0"), A("m0"), O.mult, O.add)
+    ts(A("rl"), A("rk"), kcol, O.is_equal)
+    for k in range(4):
+        c = (512 * k, 512 * k + 512)
+        px = A("r16", 16 + 512 * k, 528 + 512 * k)
+        tt(px, X(A("mlt"), chunks(CQ, k, 4)), A("rl", *c), O.mult)
+        mm(A("psA", *c), BB16, px)
+        ts(A("ai"), A("psA", *c), 0.0625, O.mult, -0.46875, O.add)
+        cp(A("bt16", 0, 512), A("ai"))
+        mms(A("psB", *c), [(H0, A("bt16", 0, 512)), (PX10, px), (H10, A("bt16", 0, 512)), (C1, A("g16", *c))])
+        ts(A("ra", *c), A("psB", *c), r91, O.add)
+    for k in range(4):
+        act(A("r16", 16 + 512 * k, 528 + 512 * k), A("ra", 512 * k, 512 * k + 512), AF.Copy)
+    gathO("r16", 16, 2048, setof("P"), sub(B1, 0, 128))
+    empties()
+    cp(PO, sub(B1, 0, 128))
+    gather_xs()
+    cp(X(A("at"), PO), A("rb"))
+    for k in range(4):
+        act(A("gt", 512 * k, 512 * k + 512), X(A("bt", 0, 1024), chunks(CQ, k, 4)), AF.Copy)
+    act(A("g16"), A("at"), AF.Copy)
+    gathO("g16", 0, 2048, s0s, sub(B2_, 256, 384))
+    R = ["ra", "rb"]
+    gens = []
+
+    def vstep():
+        if gens:
+            next(gens[0])
+
+    for t in range(4):
+        cl = t
+        lanes = (cl, 1024, 4)
+        gathO("lt16", 0, 256, setof("E"), sub(B1, 0, 16))
+        gathO("lt16", 0, 256, setof("n"), sub(B1, 16, 32))
+        EU, ED2 = S("su", "eu"), S("su", "ed2", 32)
+        nc = F("nc")
+        for o in (EU, sub(ED2, 0, 32, 2), sub(ED2, 1, 32, 2)):
+            ts(o, sub(B1, 0, 16), -1.0, O.add)
+        cp(nc, sub(B1, 16, 32))
+        s_keys()
+        u_scan()
+        vstep()
+        cp(A("uc"), X(A("us"), EU))
+        k_scan()
+        for w in range(16):
+            mm(sub(B1, 32, 48), bws(w), A("uc", w, 256, 16), w == 0, w == 15)
+        lanes_of(A("ks", 0, 2048), ED2)
+        sel(F("key"), 0, F("mE4", 1), F("mO4", 1))
+        ki, k2 = S("si", "ki"), S("si", "k2")
+        sf, hf, sig, rnk = F("sf"), F("hf"), F("sig"), F("rnk")
+        cp(ki, F("key"))
+        ts(k2, ki, 2047, O.bitwise_and)
+        cp(sf, k2)
+        cp(S("su", "sU"), k2)
+        ts(k2, ki, 1023, O.bitwise_and)
+        cp(S("su", "hU"), k2)
+        cp(A("acq"), X(A("act"), S("su", "hU")))
+        cp(A("xsb"), X(A("xa", 0, 2048), S("su", "sU")))
+        cp(A("xl", *lanes), A("xsb"))
+        for k in range(4):
+            c = (512 * k, 512 * k + 512)
+            mm(A("psA", *c), RKB, A("rk", *c), True, False)
+            mm(A("psA", *c), RPB, A("r16", 16 + 512 * k, 528 + 512 * k), False, False)
+            tt(A("df", *c), X(A("xl"), chunks(CQ, k, 4)), A("xs", *c), O.subtract)
+            act(A("sqs", *c), A("df", *c), AF.Square)
+        vstep()
+        for k in range(4):
+            mm(A("psA", 512 * k, 512 * k + 512), BBK, A("sqs", 512 * k, 512 * k + 512), False, True)
+        ts(k2, ki, 11, O.arith_shift_right)
+        ts(F("y"), k2, -1.0, O.mult, 4096.0, O.add)
+        cp(ki, F("y"))
+        ts(k2, ki, 4, O.arith_shift_right)
+        cp(sig, k2)
+        ts(k2, ki, 15, O.bitwise_and)
+        cp(rnk, k2)
+        vstep()
+        if t == 0:
+            cp(POS, sub(B2_, 256, 384))
+            agents()
+        build_xc(cl)
+        gr, live, want0 = F("gr"), F("live"), F("want0")
+        tt(gr, sub(B1, 32, 48), sig, O.subtract)
+        ts(live, nc, 0.5, O.is_gt)
+        ts(want0, gr, sub(lims, 1, 2), O.is_gt)
+        tt(want0, want0, live, O.mult)
+        ai0, ai1 = A("ai", 0, 256), A("ai", 256, 512)
+        cp(ai0, A("acq"))
+        ts(ai1, ai0, 15, O.bitwise_and)
+        ts(ai0, ai0, 4, O.arith_shift_right)
+        ts(A("ahl"), A("ai"), F("k128", 1), O.add, 1.0 / 2048, O.mult)
+        scan(A("gt", 0, 2048), A("m0"), A("psA"), O.mult, O.max)
+        lanes_of(A("gt", 0, 2048), ED2)
+        vstep()
+        if t:
+            s_keys()
+        for k in range(4):
+            z0 = 1024 * (k % 2)
+            c = (z0, z0 + 1024)
+            cp(A("zb", z0, z0 + 1024, 16), A("xsb", 64 * k, 64 * k + 64))
+            scan(A("xr", *c), A("mr", 0, 1024), A("zb", *c), O.mult, O.add)
+            tt(A("df", *c), X(A("xc", 0, 2048), A("acq", 64 * k, 64 * k + 64)), A("xr", *c), O.subtract)
+            act(A("df", *c), A("df", *c), AF.Square)
+            for i in range(16):
+                mm(A("psB", 64 * k, 64 * k + 64), bws(i), A("df", z0 + i, z0 + 1024, 16), i == 0, i == 15)
+        if t:
+            new_pos()
+        sel(F("kb0"), 0)
+        sel(F("kb1"), 1)
+        cp(ki, F("kb0"))
+        ts(ki, ki, 127, O.bitwise_and)
+        cp(k2, F("kb1"))
+        ts(k2, k2, 15, O.bitwise_and)
+        bf = F("bf")
+        ts(bf, ki, 16.0, O.mult)
+        tt(bf, bf, k2, O.add)
+        for h in (0, 1):
+            tt(A("tg", 256 * h, 256 * h + 256), sub(B0, 0, 256), A("ahl", 256 * h, 256 * h + 256), O.add)
+        vtr(A("tt"), A("tg"))
+        scan(A("tg"), A("mrb"), A("tt"), O.max, O.min)
+        r32 = S("si", "r32", 32)
+        ts(r32, A("tg", 15, 512, 16), 2048.0, O.mult)
+        ts(S("si", "rh"), sub(r32, 0, 16), 127, O.bitwise_and)
+        ts(S("si", "rl"), sub(r32, 16, 32), 15, O.bitwise_and)
+        ts(F("ah"), S("si", "rh"), 16.0, O.mult, -2048.0, O.add)
+        tt(F("ah"), F("ah"), S("si", "rl"), O.add)
+        ts(F("fit"), A("tg", 15, 256, 16), 4096.0, O.is_lt)
+        tt(F("ah"), F("ah"), F("fit"), O.mult)
+        ts(S("sh", "a16"), F("ah"), 2048.0, O.add)
+        s2o(S("sh", "a16"), sub(B1, 48, 64), 16)
+        has = F("has")
+        ts(has, sub(B1, 48, 64), 2047.5, O.is_lt)
+        tt(has, has, live, O.mult)
+        ts(S("su", "aU"), sub(B1, 48, 64), 2047.0, O.min)
+        cp(A("ag16"), X(A("at"), S("su", "aU")))
+        gathO("ag16", 0, 256, setof("E"), sub(B1, 64, 80))
+        gathO("ag16", 0, 256, setof("r8"), sub(B3, 480, 496))
+        gathO("ag16", 0, 256, setof("n"), sub(B3, 496, 512))
+        if t:
+            u_scan()
+            k_scan()
+        DU, DD2 = S("su", "du"), S("su", "dd2", 32)
+        for o in (DU, sub(DD2, 0, 32, 2), sub(DD2, 1, 32, 2)):
+            ts(o, sub(B1, 64, 80), -1.0, O.add)
+        dn, df_, d47 = F("dn"), F("d"), F("d47")
+        cp(A("ud"), X(A("us"), DU))
+        cp(dn, sub(B3, 496, 512))
+        cp(df_, sub(B3, 480, 496))
+        ts(d47, df_, -2047.0, O.add)
+        tt(d47, d47, has, O.mult)
+        ts(d47, d47, 2047.0, O.add)
+        cp(S("sh", "d16"), d47)
+        for w in range(16):
+            mm(sub(B3, w, 256, 16), ors(w), S("sh", "d16"))
+        tt(A("uv"), A("uc"), A("ud"), O.max)
+        cp(A("drep"), sub(B3, 0, 256))
+        for w in range(16):
+            mm(sub(B1, 112, 128), bws(w), A("uv", w, 256, 16), w == 0, w == 15)
+        for u in range(16):
+            q0 = 256 * (u % 4)
+            if u % 4 == u:
+                if u:
+                    ms(A("eq", q0, q0 + 16 * u), 0.0)
+            else:
+                ms(A("eq", q0 + 16 * (u - 4), q0 + 16 * u), 0.0)
+            ts(A("eq", q0 + 16 * u, q0 + 256), A("drep", 16 * u, 256), sub(d47, u, u + 1), O.is_equal)
+            tt(A("eq", q0 + 16 * u, q0 + 16 * u + 16), A("eq", q0 + 16 * u, q0 + 16 * u + 16), S("sb", "tri"), O.mult)
+            mm(sub(B3, 256, 512), BB, A("eq", q0, q0 + 256), u == 0, u == 15)
+        lanes_of(A("ks", 0, 2048), DD2)
+        sel(F("key"), 0, F("mE4", 1), F("mO4", 1))
+        cp(ki, F("key"))
+        ts(k2, ki, 11, O.arith_shift_right)
+        ts(F("y"), k2, -1.0, O.mult, 4096.0, O.add)
+        cp(ki, F("y"))
+        ts(k2, ki, 4, O.arith_shift_right)
+        cp(F("sigd"), k2)
+        mer, tmp = F("mer"), F("tmp")
+        tt(tmp, F("sigd"), sig, O.min)
+        tt(tmp, sub(B1, 112, 128), tmp, O.subtract)
+        ts(mer, tmp, limz, O.is_le)
+        tt(tmp, nc, dn, O.add)
+        ts(tmp, tmp, 16.5, O.is_lt)
+        tt(mer, mer, tmp, O.mult)
+        tt(mer, mer, has, O.mult)
+        vtr(A("ctr"), sub(B3, 256, 512))
+        cp(S("sh", "ct"), A("ctr", 0, 256, 16))
+        s2o(S("sh", "ct"), sub(B1, 128, 144), 16)
+        ts(tmp, sub(B1, 128, 144), 0.5, O.is_lt)
+        tt(mer, mer, tmp, O.mult)
+        want, spl, wk = F("want"), F("spl"), F("wk")
+        ts(tmp, mer, -1.0, O.mult, 1.0, O.add)
+        tt(want, want0, tmp, O.mult)
+        cp(S("sb", "wb"), want)
+        prefix(S("sb", "wb"), 16, wk, "pw", sub(B1, 144, 176))
+        ts(tmp, wk, F("ecnt", 1), O.is_lt)
+        tt(spl, want, tmp, O.mult)
+        cp(S("su", "kU"), wk)
+        cp(A("eg16"), X(A("el"), S("su", "kU")))
+        choose(bf, spl, bf, sf)
+        cp(S("su", "bU"), bf)
+        cp(A("xbb"), X(A("xa", 0, 2048), S("su", "bU")))
+        cp(A("xb", *lanes), A("xbb"))
+        idle, visit, vk = F("idle"), F("visit"), F("vk")
+        tt(tmp, mer, spl, O.add)
+        tt(idle, live, tmp, O.subtract)
+        cp(S("sb", "ib"), idle)
+        prefix(S("sb", "ib"), 16, vk, "pv", sub(B1, 208, 240))
+        x1, x2 = S("sh", "x1", 48), S("sh", "x2")
+        tt(tmp, mer, dn, O.mult)
+        tt(sub(x1, 0, 16), nc, tmp, O.add)
+        cp(sub(x1, 16, 32), nc)
+        cp(sub(x1, 32, 48), df_)
+        for w in range(16):
+            mm(A("psA", w, 512, 16), ors(w), sub(x1, 0, 32))
+            mm(A("psA", 512 + w, 768, 16), ors(w), sub(x1, 32, 48))
+        act(A("x16", 0, 768), A("psA", 0, 768), AF.Copy)
+        xr_, xn_, xd_, xl_ = [A("x16", 256 * k, 256 * k + 256) for k in range(4)]
+        ckl = A("ck16", cl, 1024, 4)
+        p0, p1, p2 = sub(B0, 0, 256), sub(B0, 256, 512), sub(B3, 0, 256)
+        mms(p0, [(M237, xr_), (I16, ckl)])
+        gathO("eg16", 0, 256, setof("r8"), sub(B1, 176, 192))
+        if t:
+            gathO("g16", 0, 2048, s0s, sub(B2_, 0, 128))
+        gathO("rk", 0, 2048, s0s, sub(B2_, 384, 512))
+        for k in range(4):
+            c = (512 * k, 512 * k + 512)
+            tt(A("df", *c), X(A("xb"), chunks(CQ, k, 4)), A("xs", *c), O.subtract)
+            act(A("df", *c), A("df", *c), AF.Square)
+            mms(A("psA", *c), [(BBN, A("sqs", *c)), (BB, A("df", *c))])
+        tl = F("tl")
+        ts(tl, lane, 1280.0, O.add)
+        choose(tmp, mer, df_, tl)
+        cp(S("su", "dL"), tmp)
+        cp(A("sz", cl, 1024, 4), p0)
+        cp(X(A("sz"), S("su", "dL")), A("zd"))
+        scan(A("bt", 0, 1024), A("d0"), A("sz", 0, 1024), O.mult, O.add)
+        cp(A("bl16"), A("bt", cl, 1024, 4))
+        choose(tmp, spl, sub(B1, 176, 192), tl)
+        cp(S("su", "eL"), tmp)
+        ts(visit, vk, 95.5, O.is_lt)
+        tt(visit, visit, idle, O.mult)
+        ts(tl, lane, 96.0, O.add)
+        choose(tmp, visit, vk, tl)
+        cp(S("su", "vL"), tmp)
+        cp(X(A("vs"), S("su", "vL")), A("xsb"))
+        q = T.cores[(rank + 1 + t % 7) % 8]
+        h = T.cores[(rank - 1 - t % 7) % 8]
+        send(q, "in%d" % t, A("vs", 0, 96), "ra%d" % t, "la%d" % t)
+        ts(tl, lane, 2048.0, O.add)
+        choose(tmp, visit, sf, tl)
+        cp(S("su", "vA"), tmp)
+        cp(A("res", 96, 352), A("xsb"))
+        if t:
+            cp(POS, sub(B2_, 0, 128))
+        for k in range(4):
+            c = (512 * k, 512 * k + 512)
+            ts(A("g16", *c), A("psA", *c), 0.0, O.is_lt)
+        cp(A("xb", *lanes), A("xsb"))
+        scan(A("rl"), A("m0"), A("g16"), O.mult, O.add)
+        gathO("g16", 0, 2048, s0s, sub(B2_, 0, 128))
+        lanes_of(A("rl"), ED2)
+        nl = F("nl")
+        sel(nl, 0)
+        tt(nl, nl, spl, O.mult)
+        cv, lv, cql, rp = F("cv", 128), F("lv", 128), F("cql", 128), F("rp", 128)
+        rkO, rlO = F("rkO", 128), F("rlO", 128)
+        cp(rkO, sub(B2_, 384, 512))
+        cp(x2, nl)
+        for w in range(16):
+            mm(sub(p2, w, 256, 16), ors(w), x2)
+        cp(xl_, p2)
+        mms(p0, [(I16, A("bl16")), (M7N, xl_)])
+        mms(p1, [(I16, A("bl16")), (M5, xn_), (M1N, xd_), (M81, ckl), (M7N, xl_)])
+        mms(p2, [(I23, A("bl16")), (M56, xn_), (M567, xl_), (IX, A("eg16")), (M81N, ckl)])
+        gathO("rl", 0, 2048, bws, sub(B1, 256, 384))
+        cp(lv, sub(B2_, 0, 128))
+        ts(cv, CQF, -0.75, O.mult, 1024.0 - cl / 4.0, O.add)
+        tt(cv, cv, lv, O.mult)
+        tt(cql, cv, CQF, O.add)
+        cp(S("su", "cqL", 128), cql)
+        gathO("bl16", 0, 256, setof("np"), sub(B2_, 192, 208))
+        cp(A("bt", cl, 1024, 4), p0)
+        cp(A("bt", 1024, 1280), p2)
+        cp(A("lft"), p2)
+        cp(A("dvt"), p1)
+        cp(X(A("bt"), S("su", "eL")), A("lft"))
+        if t < 3:
+            cp(A("lt16"), A("bt", cl + 1, 1024, 4))
+        else:
+            cp(A("bt16"), A("bt", 0, 1024))
+        cp(X(A("bt"), S("su", "dL")), A("dvt"))
+        for k in range(4):
+            act(A("gt", 512 * k, 512 * k + 512), X(A("bt", 0, 1280), chunks(S("su", "cqL", 128), k, 4)), AF.Copy)
+        cp(A("g16"), X(A("bt", 0, 1280), S("su", "cqL", 128)))
+        mms(p0, [(M237, xr_), (M237N, xl_), (I16, ckl)])
+        mms(p1, [(M237, xl_), (I16, A("eg16"))])
+        gathO("g16", 0, 2048, setof("np"), sub(B3, 256, 384))
+        cp(A("sz", cl, 1024, 4), p0)
+        cp(A("sze"), p1)
+        cp(X(A("sz"), S("su", "eL")), A("sze"))
+        agents()
+        ts(rlO, sub(B1, 256, 384), 0.0625, O.mult)
+        tt(rp, rkO, rlO, O.subtract)
+        tt(rlO, rlO, rp, O.subtract)
+        ts(rlO, rlO, -1.0, O.add)
+        tt(rlO, rlO, lv, O.mult)
+        tt(rp, rp, rlO, O.add)
+        stc = F("stc")
+        cp(stc, sub(B2_, 192, 208))
+        tt(stc, stc, rnk, O.add)
+        ts(tl, lane, 2048.0, O.add)
+        choose(tmp, visit, stc, tl)
+        cp(S("su", "vP"), tmp)
+        tt(rp, rp, sub(B3, 256, 384), O.add)
+        cp(S("su", "npL", 128), rp)
+        if t < 3:
+            cp(S("sh", "rp16", 128), rp)
+            for w in range(16):
+                for k in range(4):
+                    mm(A("psA", 512 * k + w, 512 * k + 512, 16), ors(w), chunks(S("sh", "rp16", 128), k, 4))
+            act(A("ks", 2080, 4128), A("psA"), AF.Copy)
+        tt(X(A(R[1]), S("su", "npL", 128)), A("gt", 0, 2048), A(R[0]), O.add)
+        R = R[::-1]
+        gens[:] = [visits(t, q, h)]
+        vstep()
+        if t < 3:
+            empties()
+        order_tables(R[0], t == 3)
+        if t < 3:
+            mt = S("sb", "mt")
+            cp(mt, mer)
+            mm(sub(B1, 240, 256), o128, mt)
+            emit("v", lambda: g.vector.tensor_reduce(ap(F("zz", 1)), ap(sub(B1, 240, 256)), AX.X, O.add), [F("zz", 1)], [sub(B1, 240, 256)])
+            zi = S("si", "zi", 1)
+            cp(zi, F("zz", 1))
+            ts(zi, zi, 15, O.bitwise_and)
+            tt(limz, sub(lims, 0, 1), zi, O.add)
+    for k in range(4):
+        mm(A("psA", 512 * k, 512 * k + 512), RPP, A("r16", 16 + 512 * k, 528 + 512 * k))
+        act(A("ks", 512 * k, 512 * k + 512), A("psA", 512 * k, 512 * k + 512), AF.Copy)
+    ms(A("ks", 2048, 2080), 2048.0)
+    fin.append(dmas("y", [(A("gt", 0, 2048), A("ks"), T["gt"][k::16, 0:2048], T["ks"][k::16, k:k + 2048]) for k in range(16)]))
+    gathO("bt16", 0, 1024, setof("st"), sub(B2_, 0, 64))
+    ts(S("su", "l64", 64), sub(B2_, 0, 64), 2047.0, O.min)
+    vstep()
+    for k in range(2):
+        mm(A("psA", 512 * k, 512 * k + 512), NRP, A("bt16", 512 * k, 512 * k + 512))
+    ye, yb = A("el", 0, 1024), A("bt", 0, 1024)
+    ts(yb, A("psA", 0, 1024), kcol, O.is_gt)
+    vstep()
+    vstep()
+    cp(ye, X(A("gt", 0, 2048), S("su", "l64", 64)))
+    ts(ye, ye, -2048.0, O.add)
+    tt(ye, ye, yb, O.mult)
+    ts(ye, ye, 2048.0, O.add)
+    fin.append(dmas("y", [(None, ye, T.ym[:, 0:1024], T["el"][:, 0:1024])]))
+    vstep()
+    fin.append(dmas("y", [(None, A("xa", 0, 2048), T.yx[:, 0:2048], T["xa"][:, 0:2048])]))
+    for who, v in fin + [(e, cnt[e]) for e in ("v", "s", "t", "g")]:
+        g.wait_ge(T.sem[SEM[who]], v)

@@ -26,6 +26,7 @@ SEMAPHORES = ["sv", "ss", "st", "sg"] + ["d%d" % i for i in range(12)]
 for _t in range(4):
     SEMAPHORES += ["ra%d" % _t, "rb%d" % _t, "la%d" % _t, "lb%d" % _t]
 BIG = 33554432.0
+HOP, SLACK, DMA, LINK = 60, 100, 2500, 4000
 
 
 def rank_program(g, core, T, topo):
@@ -56,7 +57,9 @@ def rank_program(g, core, T, topo):
     def sub(x, a, b, s=1):
         return (x[0], x[1] + a, x[1] + b, s)
 
-    def touch(e, outs, ins, seq_e):
+    ops = []
+
+    def touch(outs, ins):
         acc = []
         for x, w in [(o, True) for o in outs] + [(i, False) for i in ins]:
             if not isinstance(x, tuple):
@@ -68,36 +71,110 @@ def rank_program(g, core, T, topo):
                         acc.append((n, 512 * k, 512 * k + 512, True, True))
                 else:
                     acc.append((n, a, b, ww, False))
-        need = {}
+        me = len(ops)
+        deps = {}
         for n, a, b, w, ps in acc:
-            for r in recs.get(n, []):
-                if r[0] < b and a < r[1] and (w or r[4]) and not (r[2] == seq_e[0] and r[2][0] == "D") and not (ps and r[2] == e and e == "t"):
-                    need[r[2]] = max(need.get(r[2], 0), r[3])
-        for x in sorted(need):
-            if know[e].get(x, 0) < need[x]:
-                Q[e].wait_ge(T.sem[SEM[x]], need[x])
-                for k, v in hist[(x, need[x])].items():
-                    know[e][k] = max(know[e].get(k, 0), v)
-                know[e][x] = need[x]
-        who, seq = seq_e
-        hist[(who, seq)] = dict(know[e])
+            for r in recs.get((n, True), []) + (recs.get((n, False), []) if w else []):
+                if r[0] < b and a < r[1] and r[2] != me:
+                    deps[r[2]] = deps.get(r[2], True) and ps
         for n, a, b, w, ps in acc:
-            L = recs.setdefault(n, [])
             if w:
-                L[:] = [r for r in L if not (a <= r[0] and r[1] <= b)]
-                L.append([a, b, who, seq, True])
-            else:
-                for r in L:
-                    if r[0] == a and r[1] == b and r[2] == who and not r[4]:
-                        r[3] = seq
-                        break
-                else:
-                    L.append([a, b, who, seq, False])
+                for k in ((n, True), (n, False)):
+                    recs[k] = [r for r in recs.get(k, []) if not (a <= r[0] and r[1] <= b)]
+            recs.setdefault((n, w), []).append((a, b, me))
+        return deps
 
-    def emit(e, fn, outs, ins):
-        cnt[e] += 1
-        touch(e, outs, ins, (e, cnt[e]))
-        fn().then_inc(T.sem[SEM[e]], 1)
+    def width(x):
+        return 16 * width(x[2]) if x[0] == "X" else len(range(x[1], x[2], x[3]))
+
+    def narrow(xs):
+        return all(SCRATCH[x[0]][2] in (B2, H2, U2) for x in xs)
+
+    def cycles(e, kind, outs, ins):
+        big = [x for x in ins if isinstance(x, tuple) and width(x) > 1] or outs
+        n = width(big[-1] if e == "t" else big[0])
+        if outs[0][0] == "X":
+            return 60 + 3 * n
+        if big[0][0] == "X":
+            return 60 + 1.5 * n
+        if e == "g":
+            return 180 + 2 * n
+        if e == "t":
+            return max(64, n) * (1 if narrow(big) else 4)
+        if e == "s":
+            return max(64, n)
+        per = 2 if kind == "tt" and all(x[0][:2] != "ps" for x in big) else 1
+        return max(64, n * per * (0.5 if narrow(big + outs) else 1))
+
+    def emit(e, fn, outs, ins, kind="", sem=None, inc=1, busy=None, lat=0, after=()):
+        deps = touch(outs, ins)
+        for d in after:
+            deps[d] = False
+        ops.append({"e": e, "fn": fn, "deps": deps, "sem": sem, "inc": inc, "busy": cycles(e, kind, outs, ins) if busy is None else busy, "lat": lat})
+        return len(ops) - 1
+
+    def issue():
+        n = len(ops)
+        succ = [[] for _ in ops]
+        for i, o in enumerate(ops):
+            for d in o["deps"]:
+                succ[d].append(i)
+
+        def hop(d, i):
+            return 0 if ops[i]["deps"][d] and ops[d]["e"] == ops[i]["e"] == "t" else HOP
+        tail = [0.0] * n
+        for i in range(n - 1, -1, -1):
+            tail[i] = ops[i]["busy"] + ops[i]["lat"] + max([tail[j] + hop(i, j) for j in succ[i]] + [0])
+        left = [len(o["deps"]) for o in ops]
+        at = [0.0] * n
+        ready = {e: [] for e in "vstgya"}
+        free = {e: 0.0 for e in "vstgya"}
+        for i in range(n):
+            if not left[i]:
+                ready[ops[i]["e"]].append(i)
+        order = []
+        while len(order) < n:
+            t, e = min((max(free[x], min(at[i] for i in ready[x])), x) for x in ready if ready[x])
+            i = max((i for i in ready[e] if at[i] <= t + SLACK), key=lambda i: (tail[i], -i))
+            ready[e].remove(i)
+            order.append(i)
+            t = max(t, at[i])
+            free[e] = t + ops[i]["busy"]
+            for j in succ[i]:
+                at[j] = max(at[j], free[e] + ops[i]["lat"] + hop(i, j))
+                left[j] -= 1
+                if not left[j]:
+                    ready[ops[j]["e"]].append(j)
+        mark = {}
+        for i in order:
+            o = ops[i]
+            e = o["e"]
+            if e == "a":
+                mark[i] = (o["sem"], o["inc"])
+                hist[mark[i]] = {}
+                fin.append(mark[i])
+                continue
+            need = {}
+            for d, ps in o["deps"].items():
+                if not (ps and ops[d]["e"] == e == "t"):
+                    need[mark[d][0]] = max(need.get(mark[d][0], 0), mark[d][1])
+            for x in sorted(need):
+                if know[e].get(x, 0) < need[x]:
+                    Q[e].wait_ge(T.sem[x], need[x])
+                    for k, v in hist[(x, need[x])].items():
+                        know[e][k] = max(know[e].get(k, 0), v)
+                    know[e][x] = need[x]
+            if o["sem"]:
+                mark[i] = (o["sem"], o["inc"])
+                fin.append(mark[i])
+                o["fn"]()
+            else:
+                cnt[e] += 1
+                mark[i] = (SEM[e], cnt[e])
+                o["fn"]().then_inc(T.sem[SEM[e]], 1)
+            hist[mark[i]] = dict(know[e])
+        for who, v in fin + [(SEM[e], cnt[e]) for e in ("v", "s", "t", "g")]:
+            g.wait_ge(T.sem[who], v)
 
     def cp(out, i, e="v"):
         if e == "s":
@@ -106,7 +183,7 @@ def rank_program(g, core, T, topo):
             emit("v", lambda: g.vector.tensor_copy(ap(out), ap(i)), [out], [i])
 
     def tt(out, a, b, op):
-        emit("v", lambda: g.vector.tensor_tensor(ap(out), ap(a), ap(b), op), [out], [a, b])
+        emit("v", lambda: g.vector.tensor_tensor(ap(out), ap(a), ap(b), op), [out], [a, b], "tt")
 
     def ts(out, a, s1, op0, s2=None, op1=None):
         if op1 is None:
@@ -142,15 +219,16 @@ def rank_program(g, core, T, topo):
     nd = [0]
 
     def dmas(e, pairs):
-        who = "D%d" % nd[0]
-        SEM[who] = "d%d" % nd[0]
+        who = "d%d" % nd[0]
         nd[0] += 1
-        for k, (o, i, oa, ia) in enumerate(pairs):
-            touch(e, [o] if o else [], [i] if i else [], (who, 16 * len(pairs)))
-            Q[e].dma_start(oa, ia).then_inc(T.sem[SEM[who]], 16)
-        return who, 16 * len(pairs)
+
+        def go():
+            for o, i, oa, ia in pairs:
+                Q[e].dma_start(oa, ia).then_inc(T.sem[who], 16)
+        emit(e, go, [p[0] for p in pairs if p[0]], [p[1] for p in pairs if p[1]], sem=who, inc=16 * len(pairs), busy=60 * len(pairs), lat=DMA)
 
     fin = []
+    sent = {}
     slots = {}
     used = {"sm": 0, "si": 0, "su": 0, "sh": 0, "sb": 0}
 
@@ -165,7 +243,7 @@ def rank_program(g, core, T, topo):
 
     for n, src in (("mlt", T.ml), ("xa", T.x0), ("act", T.ac), ("lim", T.lims), ("wtc", T.wt)):
         w = src.shape[1]
-        fin.append(dmas("y" if n != "act" else "s", [(A(n, 0, w), None, T[n][:, 0:w], src[:, 0:w])]))
+        dmas("y" if n != "act" else "s", [(A(n, 0, w), None, T[n][:, 0:w], src[:, 0:w])])
 
     ms(A("ones"), 1.0)
     ms(A("rl"), 1.0)
@@ -462,17 +540,12 @@ def rank_program(g, core, T, topo):
         m = 0
         for e in es:
             m |= 1 << e
-        SEM[ls] = ls
-        touch("g", [], [src], (ls, len(es)))
-        g.remote_dma(out_ap=T[out][:], in_ap=ap(src), remote_sem=T.sem[rs], local_sem=T.sem[ls], pid=pid, routing_id=rid, dma_engine_mask=m)
-        fin.append((ls, len(es)))
+        sent[rs] = emit("g", lambda: g.remote_dma(out_ap=T[out][:], in_ap=ap(src), remote_sem=T.sem[rs], local_sem=T.sem[ls], pid=pid, routing_id=rid,
+                                                  dma_engine_mask=m), [], [src], sem=ls, inc=len(es), busy=300, lat=LINK)
 
     def arrived(buf, rs, src):
         n = len(topo.engines(src, core)[:4])
-        SEM[rs] = rs
-        hist[(rs, n)] = {}
-        recs.setdefault(buf, []).append([0, 96, rs, n, True])
-        fin.append((rs, n))
+        emit("a", None, [A(buf)], [], sem=rs, inc=n, busy=0, after=[sent[rs]])
 
     def visits(t, q, h):
         IN = "in%d" % t
@@ -885,7 +958,7 @@ def rank_program(g, core, T, topo):
         mm(A("psA", 512 * k, 512 * k + 512), RPP, A("r16", 16 + 512 * k, 528 + 512 * k))
         act(A("ks", 512 * k, 512 * k + 512), A("psA", 512 * k, 512 * k + 512), AF.Copy)
     ms(A("ks", 2048, 2080), 2048.0)
-    fin.append(dmas("y", [(A("gt", 0, 2048), A("ks"), T["gt"][k::16, 0:2048], T["ks"][k::16, k:k + 2048]) for k in range(16)]))
+    dmas("y", [(A("gt", 0, 2048), A("ks"), T["gt"][k::16, 0:2048], T["ks"][k::16, k:k + 2048]) for k in range(16)])
     gathO("bt16", 0, 1024, setof("st"), sub(B2_, 0, 64))
     ts(S("su", "l64", 64), sub(B2_, 0, 64), 2047.0, O.min)
     vstep()
@@ -899,8 +972,7 @@ def rank_program(g, core, T, topo):
     ts(ye, ye, -2048.0, O.add)
     tt(ye, ye, yb, O.mult)
     ts(ye, ye, 2048.0, O.add)
-    fin.append(dmas("y", [(None, ye, T.ym[:, 0:1024], T["el"][:, 0:1024])]))
+    dmas("y", [(None, ye, T.ym[:, 0:1024], T["el"][:, 0:1024])])
     vstep()
-    fin.append(dmas("y", [(None, A("xa", 0, 2048), T.yx[:, 0:2048], T["xa"][:, 0:2048])]))
-    for who, v in fin + [(e, cnt[e]) for e in ("v", "s", "t", "g")]:
-        g.wait_ge(T.sem[SEM[who]], v)
+    dmas("y", [(None, A("xa", 0, 2048), T.yx[:, 0:2048], T["xa"][:, 0:2048])])
+    issue()

@@ -3,20 +3,18 @@ from concourse.mybir import AluOpType as O, ActivationFunctionType as AF, AxisLi
 F4, B2, H2, I4, U2 = "float32", "bfloat16", "float16", "int32", "uint16"
 SCRATCH = {}
 for _n, _w, _d in [
-        ("xa", 2304, B2), ("xc", 2304, B2), ("xs", 2304, B2), ("ra", 2048, F4), ("rb", 2048, F4), ("r16", 2064, H2),
-        ("at", 2048, F4), ("bt", 1536, F4), ("sz", 1536, F4), ("el", 1280, F4), ("ks", 4128, F4),
-        ("gt", 2048, F4), ("g16", 2048, H2), ("df", 2048, B2), ("xr", 2048, B2), ("zb", 2048, B2), ("sqs", 2048, B2),
-        ("eq", 1024, B2), ("bw", 2048, B2), ("sets", 14336, H2), ("wts", 2048, B2), ("orp", 2048, H2),
-        ("mlt", 1024, I4), ("act", 1024, I4), ("d0", 1024, B2), ("ck16", 1024, H2),
-        ("mr", 1536, B2), ("ones", 512, B2), ("us", 2048, B2), ("rl", 2048, B2), ("m0", 2048, B2), ("rk", 2048, H2),
-        ("bt16", 1024, H2), ("xl", 1024, B2), ("xb", 1024, B2), ("wm", 3968, H2), ("wb", 1664, B2),
-        ("xsb", 256, B2), ("xbb", 256, B2), ("uc", 256, B2), ("ud", 256, B2), ("uv", 256, B2), ("acq", 256, U2), ("ai", 512, I4),
-        ("ahl", 512, F4), ("mrb", 512, B2), ("tg", 512, F4), ("tt", 512, F4),
-        ("ag16", 256, H2), ("eg16", 256, H2), ("drep", 256, H2), ("x16", 1024, H2), ("bl16", 256, H2), ("lt16", 256, H2),
-        ("dvt", 256, F4), ("lft", 256, F4), ("sze", 256, F4), ("zd", 256, F4), ("ctr", 256, F4),
-        ("vs", 352, B2), ("res", 352, B2), ("vag", 96, H2), ("yv", 96, B2), ("ri", 96, I4), ("nx", 256, B2),
-        ("sm", 2800, F4), ("si", 416, I4), ("su", 1120, U2), ("sh", 288, H2), ("sb", 160, B2), ("lim", 2, I4), ("wtc", 1, I4)]:
+        ("ML", 3088, F4), ("RT", 3088, F4), ("KT", 1808, F4), ("UT", 3088, B2), ("BT", 1792, B2), ("big", 4128, F4),
+        ("act", 1024, I4), ("xa", 2320, B2), ("xc", 2320, B2), ("xs", 2304, B2), ("xm0", 2048, B2), ("xm1", 2048, B2), ("xmb", 2304, B2),
+        ("usa", 2064, B2), ("usb", 2048, B2), ("oh", 2048, B2), ("m0", 2048, B2), ("df", 2048, B2), ("sq", 2048, B2),
+        ("prod", 2048, B2), ("cx", 4096, B2), ("cd", 2048, B2), ("hz", 1536, B2), ("hx", 1536, B2), ("at", 2064, B2),
+        ("XL", 1024, B2), ("TAU", 1024, B2), ("CK", 1024, B2), ("el", 1280, B2), ("eq", 1024, B2),
+        ("px", 2048, H2), ("mr", 1536, B2), ("mrb", 512, B2), ("ones", 256, B2), ("orp", 2048, B2),
+        ("wm", 5760, B2), ("zs", 2016, B2), ("lb", 7776, B2), ("lh", 3328, H2), ("lf", 4160, F4), ("li", 1024, I4), ("acq", 256, U2),
+        ("vs", 352, B2), ("res", 352, B2), ("yv", 96, B2),
+        ("sm", 2560, F4), ("si", 288, I4), ("su", 1120, U2), ("sh", 144, H2), ("sb", 256, B2), ("lim", 2, I4), ("wtc", 1, I4)]:
     SCRATCH[_n] = ("sbuf", [128, _w], _d)
+ALIAS = {"a1": ("df", 0, 2048), "pen": ("sq", 0, 2048), "XB": ("XL", 0, 1024), "g16": ("lh", 0, 2048), "pw": ("big", 2064, 2048),
+         "hd": ("cd", 0, 1536), "atp": ("prod", 0, 2048), "io0": ("RT", 0, 1024), "io1": ("RT", 2064, 1024)}
 for _t in range(4):
     SCRATCH["in%d" % _t] = ("sbuf", [128, 96], B2)
     SCRATCH["ry%d" % _t] = ("sbuf", [128, 96], B2)
@@ -26,6 +24,7 @@ SEMAPHORES = ["sv", "ss", "st", "sg"] + ["d%d" % i for i in range(12)]
 for _t in range(4):
     SEMAPHORES += ["ra%d" % _t, "rb%d" % _t, "la%d" % _t, "lb%d" % _t]
 BIG = 33554432.0
+BEHIND = 800
 HOP, SLACK, DMA, LINK = 60, 100, 2500, 4000
 
 
@@ -39,8 +38,14 @@ def rank_program(g, core, T, topo):
     know = {e: {} for e in Q}
     hist = {}
     recs = {}
+    ops = []
+    fin = []
+    sent = {}
 
     def A(n, a=0, b=None, s=1):
+        if n in ALIAS:
+            m, o, w = ALIAS[n]
+            return (m, o + a, o + (w if b is None else b), s)
         return (n, a, SCRATCH[n][1][1] if b is None else b, s)
 
     def X(w, o):
@@ -56,8 +61,6 @@ def rank_program(g, core, T, topo):
 
     def sub(x, a, b, s=1):
         return (x[0], x[1] + a, x[1] + b, s)
-
-    ops = []
 
     def touch(outs, ins):
         acc = []
@@ -106,11 +109,12 @@ def rank_program(g, core, T, topo):
         per = 2 if kind == "tt" and all(x[0][:2] != "ps" for x in big) else 1
         return max(64, n * per * (0.5 if narrow(big + outs) else 1))
 
-    def emit(e, fn, outs, ins, kind="", sem=None, inc=1, busy=None, lat=0, after=()):
+    def emit(e, fn, outs, ins, kind="", sem=None, inc=1, busy=None, lat=0, after=(), alt=None):
         deps = touch(outs, ins)
         for d in after:
             deps[d] = False
-        ops.append({"e": e, "fn": fn, "deps": deps, "sem": sem, "inc": inc, "busy": cycles(e, kind, outs, ins) if busy is None else busy, "lat": lat})
+        ops.append({"e": e, "fn": fn, "deps": deps, "sem": sem, "inc": inc, "busy": cycles(e, kind, outs, ins) if busy is None else busy, "lat": lat,
+                    "alt": (alt, cycles("s", kind, outs, ins)) if alt else None})
         return len(ops) - 1
 
     def issue():
@@ -134,9 +138,14 @@ def rank_program(g, core, T, topo):
                 ready[ops[i]["e"]].append(i)
         order = []
         while len(order) < n:
-            t, e = min((max(free[x], min(at[i] for i in ready[x])), x) for x in ready if ready[x])
-            i = max((i for i in ready[e] if at[i] <= t + SLACK), key=lambda i: (tail[i], -i))
-            ready[e].remove(i)
+            can = dict(ready)
+            can["s"] = ready["s"] + [i for i in ready["v"] if ops[i]["alt"]]
+            can["v"] = [i for i in ready["v"] if not ops[i]["alt"] or free["s"] > max(free["v"], at[i]) + BEHIND]
+            t, e = min((max(free[x], min(at[i] for i in can[x])), x) for x in can if can[x])
+            i = max((i for i in can[e] if at[i] <= t + SLACK), key=lambda i: (tail[i], -i))
+            ready[ops[i]["e"]].remove(i)
+            if e != ops[i]["e"]:
+                ops[i].update({"e": e, "fn": ops[i]["alt"][0], "busy": ops[i]["alt"][1]})
             order.append(i)
             t = max(t, at[i])
             free[e] = t + ops[i]["busy"]
@@ -176,23 +185,26 @@ def rank_program(g, core, T, topo):
         for who, v in fin + [(SEM[e], cnt[e]) for e in ("v", "s", "t", "g")]:
             g.wait_ge(T.sem[who], v)
 
+    def either(out, i, f, scale=1.0, bias=0.0):
+        if out[0] != "X" and all(SCRATCH[x[0]][2] in (F4, B2, H2) for x in (out, i[1] if i[0] == "X" else i)):
+            return lambda: g.scalar.activation(ap(out), ap(i), f, bias=ap(bias), scale=ap(scale))
+
     def cp(out, i, e="v"):
-        if e == "s":
-            act(out, i, AF.Copy)
-        else:
-            emit("v", lambda: g.vector.tensor_copy(ap(out), ap(i)), [out], [i])
+        emit("v", lambda: g.vector.tensor_copy(ap(out), ap(i)), [out], [i], alt=either(out, i, AF.Copy))
 
     def tt(out, a, b, op):
         emit("v", lambda: g.vector.tensor_tensor(ap(out), ap(a), ap(b), op), [out], [a, b], "tt")
 
     def ts(out, a, s1, op0, s2=None, op1=None):
         if op1 is None:
-            emit("v", lambda: g.vector.tensor_scalar(ap(out), ap(a), ap(s1), None, op0), [out], [a, s1])
+            alt = either(out, a, AF.Identity, 1.0, s1) if op0 == O.add else either(out, a, AF.Copy, s1) if op0 == O.mult else None
+            emit("v", lambda: g.vector.tensor_scalar(ap(out), ap(a), ap(s1), None, op0), [out], [a, s1], alt=alt)
         else:
-            emit("v", lambda: g.vector.tensor_scalar(ap(out), ap(a), ap(s1), ap(s2), op0, op1), [out], [a, s1, s2])
+            alt = either(out, a, AF.Identity, s1, s2) if (op0, op1) == (O.mult, O.add) else None
+            emit("v", lambda: g.vector.tensor_scalar(ap(out), ap(a), ap(s1), ap(s2), op0, op1), [out], [a, s1, s2], alt=alt)
 
-    def scan(out, d0, d1, op0, op1):
-        emit("v", lambda: g.vector.tensor_tensor_scan(ap(out), ap(d0), ap(d1), 0.0, op0, op1), [out], [d0, d1])
+    def scan(out, d0, d1, op0, op1, init=0.0):
+        emit("v", lambda: g.vector.tensor_tensor_scan(ap(out), ap(d0), ap(d1), ap(init), op0, op1), [out], [d0, d1, init])
 
     def vtr(out, i):
         emit("v", lambda: g.vector.transpose(ap(out), ap(i)), [out], [i])
@@ -200,8 +212,8 @@ def rank_program(g, core, T, topo):
     def ms(out, c):
         emit("v", lambda: g.vector.memset(ap(out), c), [out], [])
 
-    def act(out, i, f, scale=1.0):
-        emit("s", lambda: g.scalar.activation(ap(out), ap(i), f, scale=ap(scale)), [out], [i, scale])
+    def act(out, i, f, scale=1.0, bias=0.0):
+        emit("s", lambda: g.scalar.activation(ap(out), ap(i), f, bias=ap(bias), scale=ap(scale)), [out], [i, scale, bias])
 
     def mm(out, l, r, start=True, stop=True):
         emit("t", lambda: g.tensor.matmul(ap(out), ap(l), ap(r), start, stop), [out], [l, r])
@@ -218,321 +230,258 @@ def rank_program(g, core, T, topo):
 
     nd = [0]
 
-    def dmas(e, pairs):
+    def dma(e, o, i, oa, ia):
         who = "d%d" % nd[0]
         nd[0] += 1
+        emit(e, lambda: Q[e].dma_start(oa, ia).then_inc(T.sem[who], 16), [o] if o else [], [i] if i else [], sem=who, inc=16, busy=60, lat=DMA)
 
-        def go():
-            for o, i, oa, ia in pairs:
-                Q[e].dma_start(oa, ia).then_inc(T.sem[who], 16)
-        emit(e, go, [p[0] for p in pairs if p[0]], [p[1] for p in pairs if p[1]], sem=who, inc=16 * len(pairs), busy=60 * len(pairs), lat=DMA)
-
-    fin = []
-    sent = {}
     slots = {}
-    used = {"sm": 0, "si": 0, "su": 0, "sh": 0, "sb": 0}
+    used = {}
 
     def S(buf, name, w=16):
         if (buf, name) not in slots:
-            slots[(buf, name)] = A(buf, used[buf], used[buf] + w)
-            used[buf] += (w + 15) // 16 * 16
+            u = used.get(buf, 0)
+            slots[(buf, name)] = A(buf, u, u + w)
+            used[buf] = u + (w + 15) // 16 * 16
         return slots[(buf, name)]
 
     def F(name, w=16):
         return S("sm", name, w)
 
-    for n, src in (("mlt", T.ml), ("xa", T.x0), ("act", T.ac), ("lim", T.lims), ("wtc", T.wt)):
+    def U(name, w=16):
+        return S("su", name, w)
+
+    def LB(name, w=256):
+        return S("lb", name, w)
+
+    def LH(name, w=256):
+        return S("lh", name, w)
+
+    def LF(name, w=256):
+        return S("lf", name, w)
+
+    def bank(k, a=0, b=512):
+        return A("psA" if k < 4 else "psB", 512 * (k % 4) + a, 512 * (k % 4) + b)
+
+    def ch(n, k, w=512, o=0):
+        return A(n, o + w * k, o + w * k + w)
+
+    def chunks(off, k, n):
+        w = (off[2] - off[1]) // n
+        return sub(off, k * w, k * w + w)
+
+    for n, src, q in (("li", T.ml, "y"), ("xa", T.x0, "s"), ("act", T.ac, "y"), ("lim", T.lims, "s"), ("wtc", T.wt, "y")):
         w = src.shape[1]
-        dmas("y" if n != "act" else "s", [(A(n, 0, w), None, T[n][:, 0:w], src[:, 0:w])])
+        dma(q, A(n, 0, w), None, T[n][:, 0:w], src[:, 0:w])
 
-    ms(A("ones"), 1.0)
-    ms(A("rl"), 1.0)
-    iota(F("i16"), [[1, 16]], 0, 0)
-    iota(F("pi", 1), [[0, 1]], 0, 1)
-    cp1 = A("el", 0, 1024)
-    iota(cp1, [[1, 1024]], 1, 0)
-    iota(F("l16"), [[16, 16]], 0, 0)
-    iota(F("c64", 64), [[16, 64]], 0, 0)
-    m8 = A("tg", 384, 512)
-    iota(m8, [[1, 128]], 0, 0)
-    wb = {}
-
-    def W1(name, buf="wb"):
-        k = (buf, name)
-        if k not in wb:
-            i = len([1 for z in wb if z[0] == buf])
-            wb[k] = A(buf, 128 * i, 128 * i + 128)
-        return wb[k]
-
+    ones = A("ones")
+    ms(ones, 1.0)
     o128 = A("ones", 0, 128)
-    BB, ID, SP, SN, TW = W1("BB"), W1("ID"), W1("SP"), W1("SN"), W1("TW")
+    iota(F("i144", 144), [[1, 144]], 0, 0)
+    i16 = sub(F("i144", 144), 0, 16)
+    iota(F("pi", 1), [[0, 1]], 0, 1)
+    iota(F("c64", 64), [[16, 64]], 0, 0)
+
+    def W1(name):
+        return S("wm", name, 128)
+    BB, ID, SP, SN, TW, REV = W1("BB"), W1("ID"), W1("SP"), W1("SN"), W1("TW"), W1("REV")
     asel(BB, o128, [[-16, 8], [0, 16]], O.is_ge, 0, 1)
     asel(BB, BB, [[16, 8], [0, 16]], O.is_ge, 15, -1)
     asel(ID, o128, [[-1, 128]], O.is_equal, 0, 1)
-    asel(A("bw"), A("rl"), [[1, 16], [0, 8], [-1, 16]], O.is_equal, 0, 0)
-    asel(A("bw"), A("bw"), [[0, 16], [-16, 8], [0, 16]], O.is_ge, 0, 1)
-    asel(A("bw"), A("bw"), [[0, 16], [16, 8], [0, 16]], O.is_ge, 15, -1)
+    iota(A("io0"), [[1, 1024]], 1, 0)
+    iota(A("io1"), [[1, 1024]], 1025, 0)
+    chi, clo, ccl = A("cx", 0, 1024), A("cx", 1024, 2048), A("cd", 0, 1024)
+    iota(chi, [[1, 64], [0, 16]], 0, 0)
+    iota(clo, [[0, 64], [1, 16]], 0, 0)
+    iota(ccl, [[0, 256], [1, 4]], 0, 0)
     asel(SP, o128, [[-1, 128]], O.is_equal, 16, 1)
     asel(SN, o128, [[-1, 128]], O.is_equal, -16, 1)
     asel(TW, BB, [[1, 128]], O.is_gt, 0, -1)
-    iota(A("rb"), [[1, 2048]], 0, 0)
-    pi = S("si", "pi", 1)
-    kcol, mO, mE = F("kcol", 1), F("mO", 1), F("mE", 1)
+    asel(REV, o128, [[-16, 8], [1, 16]], O.is_equal, -15, 1)
+    SH = [W1("SH%d" % b) for b in range(4)]
+    for b in range(4):
+        asel(SH[b], BB, [[-1, 128]], O.is_equal, 1 << b, 1)
+        tt(SH[b], SH[b], ID, O.subtract)
+    pi, p2 = S("si", "pi", 1), S("si", "p2", 1)
+    kcol, mO, mE, g15 = F("kcol", 1), F("mO", 1), F("mE", 1), F("g15", 1)
     cp(pi, F("pi", 1))
-    ts(S("si", "p2", 1), pi, 15, O.bitwise_and)
-    cp(kcol, S("si", "p2", 1))
-    ts(S("si", "p2", 1), pi, 4, O.arith_shift_right, 1, O.bitwise_and)
-    cp(mO, S("si", "p2", 1))
+    ts(p2, pi, 15, O.bitwise_and)
+    cp(kcol, p2)
+    ts(S("si", "p3", 1), pi, 4, O.arith_shift_right, 1, O.bitwise_and)
+    cp(mO, S("si", "p3", 1))
     ts(mE, mO, -1.0, O.mult, 1.0, O.add)
-    ts(F("mE4", 1), mE, 4096.0, O.mult)
-    ts(F("mO4", 1), mO, 4096.0, O.mult)
-    ts(F("k128", 1), kcol, 128.0, O.mult)
-    ts(F("k11", 1), kcol, -11.0, O.add)
+    ts(g15, F("pi", 1), kcol, O.subtract, 15.0, O.add)
     rm = F("rm")
-    ts(rm, F("i16"), kcol, O.is_equal)
+    ts(rm, i16, kcol, O.is_equal)
 
     def RM(r):
         return sub(rm, r, r + 1)
 
     def coef(name, terms):
         c = F("c_" + name, 1)
-        r0, w0 = terms[0]
-        ts(c, RM(r0), float(w0), O.mult)
+        ts(c, RM(terms[0][0]), float(terms[0][1]), O.mult)
         for r, w in terms[1:]:
-            ts(F("c_t", 1), RM(r), float(w), O.mult)
-            tt(c, c, F("c_t", 1), O.add)
+            ts(c, RM(r), float(w), O.mult, c, O.add)
         return c
 
-    lane, c4 = F("lane"), F("c4", 64)
-    ts(lane, F("l16"), kcol, O.add)
-    ts(c4, F("c64", 64), kcol, O.add)
-    ts(S("sb", "tri"), F("i16"), kcol, O.is_gt)
-    ci, ck0, ck1 = A("ai"), A("ks", 0, 512), A("ks", 512, 1024)
-    for h in (0, 1):
-        cpart = A("el", 512 * h, 512 * h + 512)
-        ts(ck0, cpart, -1.0, O.add)
-        cp(ci, ck0)
-        ts(ci, ci, 3, O.bitwise_and)
-        ts(ck1, ci, F("k11", 1), O.is_equal)
-        ts(ck0, ck0, RM(8), O.mult)
-        tt(A("ck16", 512 * h, 512 * h + 512), ck0, ck1, O.add)
-    ts(A("d0"), A("rl", 0, 1024), RM(2), O.mult)
+    def kc(name, a, b):
+        c = F("k_" + name, 1)
+        ts(c, kcol, float(a), O.mult, float(b), O.add)
+        return c
 
-    def mk(name, src, col, w=1.0, buf="wm"):
-        m = W1(name, buf)
+    def zset(name, col):
+        z = S("zs", name, 144)
+        ts(z, F("i144", 144), g15, O.is_equal, col, O.mult)
+        return lambda w: sub(z, 15 - w, 143 - w)
+
+    def mk(name, src, col, w=1.0):
+        m = W1(name)
         ts(m, src, col, O.mult, float(w), O.mult)
         return m
 
-    one = F("one1", 1)
-    ms(one, 1.0)
-    I16 = mk("I16", ID, one)
-    mi = S("si", "mi", 128)
-    par, ta, tb = A("tg", 256, 384), A("tg", 0, 128), A("tg", 128, 256)
-    cp(mi, m8)
-    ts(mi, mi, 15, O.bitwise_and)
-    ts(ta, mi, 2.0, O.is_equal)
-    for r in (3.0, 7.0):
-        ts(tb, mi, r, O.is_equal)
-        tt(ta, ta, tb, O.add)
-    BB237 = W1("BB237", "wb")
-    tt(BB237, BB, ta, O.mult)
-    ts(A("us", 0, 1024), A("mlt"), 2048.0, O.is_lt)
-    for k in range(2):
-        mms(A("psB", 512 * k, 512 * k + 512), [(BB237, A("us", 512 * k, 512 * k + 512)), (I16, A("ck16", 512 * k, 512 * k + 512))])
-    cp(A("sz", 0, 1024), A("psB", 0, 1024))
-    scan(A("bt", 0, 1024), A("d0"), A("sz", 0, 1024), O.mult, O.add)
-    cp(A("bt16"), A("bt", 0, 1024))
-    cp(A("lt16"), A("bt", 0, 1024, 4))
-    ms(A("ks", 0, 2048), 0.0)
-    names = ["E", "n", "r8", "cid", "P", "np", "st"]
-    terms = [[(2, 1), (3, -1), (6, 1), (7, 1)], [(7, 1)], [(8, 1)], [(1, 1)], [(0, 16), (10, 1)], [(2, 1), (3, -1), (5, 1)], [(2, 1), (3, -1), (6, 1)]]
-    ccol = {}
-
-    def setof(name):
-        i = names.index(name)
-        return lambda w: A("sets", 2048 * i + 128 * w, 2048 * i + 128 * w + 128)
-    for i, nm in enumerate(names):
-        ccol[nm] = coef(nm, terms[i])
-    for nm in ("np", "n", "cid", "P", "E", "r8", "st"):
-        i = names.index(nm)
-        act(A("sets", 2048 * i, 2048 * i + 2048), A("bw"), AF.Copy, ccol[nm])
+    cE = RM(0)
+    zall, zneg, z256 = zset("all", 1.0), zset("neg", -1.0), zset("256", 256.0)
+    z0, z0n, zn, zms = zset("0", RM(0)), zset("0n", coef("0n", [(0, -1)])), zset("n", RM(2)), zset("ms", RM(3))
+    zst = zset("st", coef("st", [(0, 1), (1, -1)]))
+    zown, zc, zp = zset("own", coef("own", [(0, 16), (1, 1)])), zset("c", coef("c", [(4, 16), (5, 1)])), zset("p", coef("p", [(6, 16), (7, 1)]))
+    znn = zset("nn", coef("nn", [(2, -1)]))
     wf = F("wf", 1)
     cp(wf, A("wtc"))
-    act(A("wts"), A("bw"), AF.Copy, wf)
-
-    def bws(w):
-        return A("bw", 128 * w, 128 * w + 128)
-
-    s0s = setof("cid")
-
-    def wtw(w):
-        return A("wts", 128 * w, 128 * w + 128)
+    zw = zset("w", wf)
+    Z16 = zset("16", 16.0)
 
     def ors(w):
         return A("orp", 128 * w, 128 * w + 128)
+    W012 = W1("W012")
+    tt(W012, zall(0), zall(1), O.add)
+    W01 = W1("W01")
+    cp(W01, W012)
+    tt(W012, W012, zall(2), O.add)
+    PE_, PO_, P01, P10 = mk("PE", ID, mE), mk("PO", ID, mO), mk("P01", SP, mE), mk("P10", SN, mO)
+    BB16, BBN, B64, B64N, BK = mk("BB16", BB, 16.0), mk("BBN", BB, -1.0), mk("B64", BB, 64.0), mk("B64N", BB, -64.0), mk("BK", BB, -32768.0)
+    I17, I23, IPN = mk("I17", ID, 131072.0), mk("I23", ID, 8388608.0), mk("IPN", ID, -4096.0)
+    NREP, CREP = mk("NREP", BB, RM(2)), mk("CREP", BB, F("c_c", 1))
+    BIT = [mk("BIT%d" % b, BB, RM(4 + b)) for b in range(4)]
+    CLS = [mk("CLS%d" % m, BB, RM(8 + m), 64.0) for m in range(4)]
+    D01 = mk("D01", ID, coef("01", [(0, 1), (1, 1)]))
+    DH, DL, DH2, DL2 = mk("DH", ID, RM(4)), mk("DL", ID, RM(5)), mk("DH2", ID, coef("06", [(0, 1), (6, 1)])), mk("DL2", ID, coef("17", [(1, 1), (7, 1)]))
+    Q1, Q2, TW2, ZERO = W1("Q1"), W1("Q2"), mk("TW2", TW, -2.0), mk("ZERO", ID, 0.0)
+    ts(Q1, ID, -0.5, O.mult)
+    tt(Q1, Q1, TW, O.subtract)
+    ts(Q2, ID, 16.0, O.mult)
+    tt(Q2, Q2, TW, O.add)
+    WC, WD = W1("WC"), W1("WD")
+    tt(WC, zms(0), zn(2), O.add)
+    tt(WC, WC, znn(3), O.add)
+    tt(WD, zms(1), zn(2), O.add)
     for w in range(16):
         ts(ors(w), BB, RM(w), O.mult)
-
-    PE_, PO_, P01, P10 = mk("PE", ID, mE), mk("PO", ID, mO), mk("P01", SP, mE), mk("P10", SN, mO)
-    BBK, BBS, BBN = mk("BBK", BB, one, 2048.0, "wb"), mk("BBS", BB, one, -8.0, "wb"), mk("BBN", BB, one, -1.0, "wb")
-    RKS, RKB = mk("RKS", BB, RM(0), -0.5), mk("RKB", BB, RM(0), -128.0)
-    BB16 = mk("BB16", BB, one)
-    RPS = mk("RPS", BB, coef("ks", [(0, 2.0 ** -8), (10, 2.0 ** -12), (9, 2048)]))
-    CDP, CDN = mk("CDP", BB, RM(1)), mk("CDN", BB, RM(1), -1.0)
-    STR, NRP = mk("STR", BB, ccol["st"]), mk("NRP", BB, ccol["n"])
-    CLS = [mk("CLS%d" % m, BB, RM(11 + m), 64.0, "wb") for m in range(4)]
-    ts(mi, mi, 1, O.bitwise_and)
-    cp(par, mi)
-    RPB = W1("RPB", "wm")
-    ts(ta, BB, coef("kb1", [(10, 1.0), (0, -1.0)]), O.mult)
-    tt(ta, ta, par, O.mult)
-    ts(tb, BB, coef("kb2", [(0, 1.0), (9, 2048.0)]), O.mult)
-    tt(RPB, ta, tb, O.add)
-
-    def rowmap(name, src, rows, w=1.0):
-        m = W1(name, "wm")
-        ts(ta, bws(rows[0]), RM(src), O.mult, float(w), O.mult)
-        for r in rows[1:]:
-            ts(tb, bws(r), RM(src), O.mult, float(w), O.mult)
-            tt(ta, ta, tb, O.add)
-        cp(m, ta)
-        return m
-    M237, M237N, M7N = rowmap("M237", 0, [2, 3, 7]), rowmap("M237N", 0, [2, 3, 7], -1), rowmap("M7N", 0, [7], -1)
-    M5, M1N, M81, M81N, M56 = rowmap("M5", 0, [5]), rowmap("M1N", 0, [1], -1), rowmap("M81", 8, [1]), rowmap("M81N", 8, [1], -1), rowmap("M56", 0, [5, 6])
-    M567 = W1("M567", "wm")
-    tt(M567, M7N, M56, O.add)
-    ts(M567, M567, -1.0, O.mult)
-    I23 = mk("I23", ID, coef("i23", [(2, 1), (3, 1)]))
-    IX = W1("IX", "wm")
-    tt(IX, I16, M81, O.add)
-    RPP = mk("RPP", BB, ccol["P"])
-    H0, PX10, H10, C1 = rowmap("H0", 0, [0]), W1("PX10", "wm"), rowmap("H10", 0, [10], -16), rowmap("C1", 0, [1])
-    cp(PX10, bws(10))
+    lane, c4 = F("lane"), F("c4", 64)
+    ts(c4, F("c64", 64), kcol, O.add)
+    lane = sub(c4, 0, 16)
+    k15, kkt, kab, k128 = kc("15", -1, 15), kc("kt", -2048, 15 * 2048 + 2048), kc("ab", -1, -0.5), kc("128", 128, 0)
     ms(A("mr"), 1.0)
     ms(A("mr", 0, 1536, 16), 0.0)
     ms(A("mrb"), 0.0)
     ms(A("mrb", 0, 512, 16), BIG)
-    for n in ("zb", "eq", "xl", "xb"):
-        ms(A(n), 0.0)
+    ms(A("hz"), 0.0)
+    ms(A("XL"), 0.0)
+    ms(A("TAU"), 64.0)
     ms(A("vs"), 0.0)
-    ms(A("zd"), 0.0)
-    ms(F("neg"), -1.0)
-    cp(A("r16", 0, 16), F("neg"))
+    ms(A("el", 0, 256), 0.0)
+    ms(A("xs", 2048, 2304), 0.0)
+    ms(A("xa", 2048, 2064), 64.0)
+    ms(A("usa", 2048, 2064), 0.0)
+    ms(A("UT", 2048, 2064), 0.0)
+    ms(A("ML", 2048, 2064), 0.0)
+    ms(A("RT", 2048, 2064), 0.0)
+    ms(A("KT", 1024, 1040), 0.0)
+    ts(A("RT", 2049, 2050), RM(2), 99.0, O.mult)
+    cp(A("at", 2048, 2049), coef("far", [(4, 127), (5, 15), (6, 128), (7, 1)]))
+    zero = LB("zero")
+    ms(zero, 0.0)
+    dg = LB("dg")
+    ts(dg, sub(clo, 0, 256), kcol, O.is_lt, -64.0, O.mult)
+    NB, nbi = A("sb", 224, 256), S("si", "nbi", 32)
+    ts(nbi, sub(F("i144", 144), 0, 32), coef("pw", [(4, 1), (5, 0.5), (6, 0.25), (7, 0.125)]), O.mult, -0.4375, O.add)
+    ts(nbi, nbi, 1, O.bitwise_and)
+    cp(NB, nbi)
     lims = F("lims", 2)
     cp(lims, A("lim"))
-    limz = F("limz", 1)
-    cp(limz, sub(lims, 0, 1))
+    thr0, thr = F("thr0", 1), F("thr", 1)
+    ts(thr0, sub(lims, 0, 1), 256.0, O.add, F("c_01", 1), O.mult)
+    tt(thr0, thr0, coef("t23", [(2, 16), (3, -1)]), O.add)
+    lim2 = F("lim2", 1)
+    ts(lim2, sub(lims, 1, 2), 256.0, O.add)
+    hi4 = coef("hi4", [(r, 1) for r in (4, 5, 6, 7, 8, 9, 10, 11)])
+    cde = coef("de", [(0, 128)])
 
-    def gathO(src, a, n, st, out):
+    def gath(out, st, src, a, n, step=1):
         for w in range(16):
-            mm(out, st(w), A(src, a + w, a + n, 16), w == 0, w == 15)
+            mm(out, st(w), A(src, a + step * w, a + step * n, 16 * step), w == 0, w == 15)
+
+    def rows(out, lst):
+        n = width(lst)
+        for w in range(16):
+            mm(sub(out, w, 16 * n, 16), ors(w), lst)
 
     def s2o(r1, out, n):
         mms(sub(out, 0, n, 2), [(PE_, sub(r1, 0, n, 2)), (P01, sub(r1, 1, n, 2))])
         mms(sub(out, 1, n, 2), [(P10, sub(r1, 0, n, 2)), (PO_, sub(r1, 1, n, 2))])
 
-    def lanes_of(win, dup):
-        cp(A("tg"), X(win, dup))
-        vtr(A("tt"), A("tg"))
-
-    def sel(out, r, me=mE, mo=mO):
-        ts(F("selA"), A("tt", r, 512, 32), me, O.mult)
-        ts(F("selB"), A("tt", 16 + r, 512, 32), mo, O.mult)
-        tt(out, F("selA"), F("selB"), O.add)
-
     def prefix(ind, n, out, tag, ps):
         mm(sub(ps, 0, n), TW, ind)
         mm(sub(ps, n, 2 * n), BB, ind)
-        cp(F(tag + "tot", n), sub(ps, n, 2 * n))
-        inc = F(tag + "inc", n)
-        scan(inc, A("ones", 0, n), F(tag + "tot", n), O.mult, O.add)
-        tt(out, inc, F(tag + "tot", n), O.subtract)
-        tt(out, out, sub(ps, 0, n), O.add)
-        return sub(inc, n - 1, n)
+        inc = F(tag + "inc", n + 1)
+        if tag not in used:
+            used[tag] = 0
+            ms(sub(inc, 0, 1), 0.0)
+        scan(sub(inc, 1, n + 1), A("ones", 0, n), sub(ps, n, 2 * n), O.mult, O.add)
+        tt(out, sub(ps, 0, n), sub(inc, 0, n), O.add)
+        return sub(inc, n, n + 1)
 
-    def lt(name):
-        return F(name)
-
-    def choose(out, cond, a, b, tmp="chT", w=16):
-        d = F(tmp + str(w), w)
+    def choose(out, cond, a, b, tag, w=16):
+        d = F("ch" + tag, w)
         tt(d, a, b, O.subtract)
         tt(d, d, cond, O.mult)
         tt(out, d, b, O.add)
 
-    B0, B1, B2_, B3 = [A("psB", 512 * k, 512 * k + 512) for k in range(4)]
-    PO, CQ, CQF = S("su", "po", 128), S("su", "cq", 128), F("cqf", 128)
+    def best(src, n, tag, mask, op0, op1):
+        a, b = LF("t" + tag, n), LF(("k" if mask == "mrb" else "g") + tag, n)
+        vtr(a, src)
+        scan(b, A(mask, 0, n), a, op0, op1)
+        return a, b
 
-    def chunks(off, k, n):
-        w = (off[2] - off[1]) // n
-        return sub(off, k * w, k * w + w)
-
-    def order_tables(R, last):
+    def segscan(out, passes, banks):
         for k in range(4):
-            act(A("r16", 16 + 512 * k, 528 + 512 * k), A(R, 512 * k, 512 * k + 512), AF.Copy)
-        gathO("r16", 16, 2048, setof("P"), sub(B1, 0, 128))
-        cp(PO, sub(B1, 0, 128))
-        gather_xs()
-        if last:
-            return
+            ps = bank(banks[k % 2])
+            mms(ps, [(m, ch(n, k)) for m, n in passes])
+            scan(sub(out, 512 * k, 512 * k + 512), ch("m0", k), ps, O.mult, O.max, sub(out, 512 * k - 1, 512 * k) if k else 0.0)
+
+    CP, CPF, POS, IX = U("cp", 128), F("cpf", 128), U("pos", 128), U("ix", 128)
+    sc, sc2 = A("big", 0, 2064), A("big", 2064, 4128)
+
+    def agents(lst, hi, last):
         for k in range(4):
-            c = (B0, B2_)[k % 2]
-            mms(c, [(CDP, A("r16", 16 + 512 * k, 528 + 512 * k)), (CDN, A("r16", 15 + 512 * k, 527 + 512 * k))])
-            ts(A("m0", 512 * k, 512 * k + 512), c, 0.0, O.is_equal)
-        gathO("r16", 16, 2048, setof("cid"), sub(B2_, 0, 128))
-        cp(CQF, sub(B2_, 0, 128))
-        cp(CQ, CQF)
-        scan(A("rk"), A("m0"), A("m0"), O.mult, O.add)
-
-    def gather_xs():
-        cp(A("xs", 1024, 2048), X(A("xa", 0, 2048), chunks(PO, 1, 2)))
-        for k in range(2):
-            act(A("xs", 512 * k, 512 * k + 512), X(A("xa", 0, 2048), chunks(PO, k, 4)), AF.Copy)
-
-    POS = S("su", "pos", 128)
-
-    def agents():
+            cp(ch("atp", k), X(A("BT", 0, hi), chunks(lst, k, 4)))
         for k in range(4):
-            act(A("at", 512 * k, 512 * k + 512), X(A("gt", 0, 2048), chunks(POS, k, 4)), AF.Copy)
-
-    def build_xc(m):
-        act(A("rl"), A("at"), AF.Copy)
-        for k in range(4):
-            c = (B0, B3)[k % 2]
-            mms(c, [(ID, A("xa", 512 * k, 512 * k + 512)), (CLS[m], A("rl", 512 * k, 512 * k + 512))])
-            act(A("xc", 512 * k, 512 * k + 512), c, AF.Copy)
-
-    def new_pos():
-        for k in range(4):
-            act(A("gt", 512 * k, 512 * k + 512), X(A("ks", 2080, 4128), chunks(POS, k, 4)), AF.Copy)
-            act(A("g16", 512 * k, 512 * k + 512), A("gt", 512 * k, 512 * k + 512), AF.Copy)
-
-    def s_keys():
-        for k in range(4):
-            mm(A("psA", 512 * k, 512 * k + 512), RKS, A("rk", 512 * k, 512 * k + 512), True, False)
-            mm(A("psA", 512 * k, 512 * k + 512), RPS, A("r16", 16 + 512 * k, 528 + 512 * k), False, False)
-        for k in range(4):
-            mm(A("psA", 512 * k, 512 * k + 512), BBS, A("xs", 512 * k, 512 * k + 512), False, True)
-
-    def u_scan():
-        scan(A("us"), A("m0"), A("xs", 0, 2048), O.mult, O.max)
-
-    def k_scan():
-        scan(A("ks", 0, 2048), A("m0"), A("psA"), O.mult, O.max)
+            cp(ch("at", k), X(A("atp"), chunks(POS, k, 4)))
+        if hi > 1024 and not last:
+            gath(bank(4, 384, 512), zc, "atp", 0, 2048)
+            cp(CPF, bank(4, 384, 512))
+            cp(CP, bank(4, 384, 512))
 
     def empties():
-        act(A("bt16"), A("sz", 0, 1024), AF.Copy)
-        gathO("bt16", 0, 1024, setof("n"), sub(B2_, 0, 64))
-        e64, r64 = F("e64", 64), F("r64", 64)
-        ts(e64, sub(B2_, 0, 64), 0.5, O.is_lt)
-        cp(S("sb", "e64", 64), e64)
-        e = prefix(S("sb", "e64", 64), 64, r64, "pe", sub(B2_, 64, 192))
-        cp(F("ecnt", 1), e)
-        ts(F("t64", 64), c4, 256.0, O.add)
-        ts(F("u64", 64), r64, 255.5, O.is_lt)
-        tt(e64, e64, F("u64", 64), O.mult)
-        choose(r64, e64, r64, F("t64", 64), "ch64", 64)
-        cp(S("su", "l64", 64), r64)
-        cp(X(A("el"), S("su", "l64", 64)), A("ck16"))
+        gath(bank(6, 0, 64), zn, "BT", 0, 1024)
+        e64, r64, eb = F("e64", 64), F("r64", 64), S("sb", "e64", 64)
+        ts(eb, bank(6, 0, 64), 0.5, O.is_lt)
+        e = prefix(eb, 64, r64, "pe", bank(6, 64, 192))
+        ts(e64, r64, 255.5, O.is_lt)
+        tt(e64, e64, eb, O.mult)
+        choose(r64, e64, r64, F("c256", 64), "s", 64)
+        cp(U("l64", 64), r64)
+        cp(X(A("el"), U("l64", 64)), A("CK"))
+        return e
 
     def send(dst, out, src, rs, ls):
         rid, pid, _ = topo.addr(dst)
@@ -544,435 +493,424 @@ def rank_program(g, core, T, topo):
                                                   dma_engine_mask=m), [], [src], sem=ls, inc=len(es), busy=300, lat=LINK)
 
     def arrived(buf, rs, src):
-        n = len(topo.engines(src, core)[:4])
-        emit("a", None, [A(buf)], [], sem=rs, inc=n, busy=0, after=[sent[rs]])
+        emit("a", None, [A(buf)], [], sem=rs, inc=len(topo.engines(src, core)[:4]), busy=0, after=[sent[rs]])
 
-    def visits(t, q, h):
+    def payload(out, lst, n, tag):
+        ai = S("li", tag, 2 * n)
+        cp(sub(ai, 0, n), lst)
+        ts(sub(ai, n, 2 * n), sub(ai, 0, n), 15, O.bitwise_and)
+        ts(sub(ai, 0, n), sub(ai, 0, n), 4, O.arith_shift_right)
+        ts(out, ai, k128, O.add, 1.0 / 2048, O.mult)
+
+    def nearest(ps, pay, n, tag):
+        key = LF("k" + tag, 2 * n)
+        for h in (0, 1):
+            tt(sub(key, n * h, n * h + n), ps, sub(pay, n * h, n * h + n), O.add)
+        a, b = best(key, 2 * n, tag, "mrb", O.max, O.min)
+        m = n // 16
+        r = S("si", "r" + tag, 2 * m)
+        ts(r, sub(b, 15, 2 * n, 16), 2048.0, O.mult)
+        ts(sub(r, 0, m), sub(r, 0, m), 127, O.bitwise_and)
+        ts(sub(r, m, 2 * m), sub(r, m, 2 * m), 15, O.bitwise_and)
+        ah = F("ah" + tag, m)
+        ts(ah, sub(r, 0, m), 16.0, O.mult, -2048.0, O.add)
+        tt(ah, ah, sub(r, m, 2 * m), O.add)
+        return sub(b, 15, n, 16), ah
+
+    def host(t, h):
         IN = "in%d" % t
         arrived(IN, "ra%d" % t, h)
-        for w in range(16):
-            mm(sub(B3, 0, 6), wtw(w), A(IN, w, 96, 16), w == 0, w == 15)
+        gath(bank(7, 0, 6), zw, IN, 0, 96)
         vi = S("si", "vi", 6)
-        cp(vi, sub(B3, 0, 6))
+        cp(vi, bank(7, 0, 6))
         ts(vi, vi, 2047, O.bitwise_and)
-        cp(S("su", "vi", 6), vi)
-        cp(A("vag"), X(A("at"), S("su", "vi", 6)))
-        mm(sub(B3, 16, 112), STR, A("vag"))
-        mm(sub(B3, 112, 208), NRP, A("vag"))
-        cp(A("zb", 0, 1536, 16), A(IN))
-        scan(A("xr", 0, 1536), A("mr", 0, 1536), A("zb", 0, 1536), O.mult, O.add)
-        yield
-        hl = F("hl", 96)
-        ts(hl, sub(B3, 112, 208), -1.0, O.add, kcol, O.min)
-        tt(hl, hl, sub(B3, 16, 112), O.add)
-        cp(S("su", "hl", 96), hl)
-        hx = A("sqs", 0, 1536)
-        tt(hx, X(A("xs", 0, 2048), S("su", "hl", 96)), A("xr", 0, 1536), O.subtract)
-        act(hx, hx, AF.Square)
-        for w in range(16):
-            mm(sub(B3, 208, 214), setof("st")(w), A("vag", w, 96, 16), w == 0, w == 15)
-        for i in range(16):
-            mm(sub(B0, 256, 352), bws(i), A("sqs", i, 1536, 16), i == 0, i == 15)
-        yield
-        ts(A("tg", 0, 96), sub(B0, 256, 352), 16.0, O.mult, kcol, O.add)
-        vtr(A("tt", 0, 96), A("tg", 0, 96))
-        scan(A("tg", 0, 96), A("mrb", 0, 96), A("tt", 0, 96), O.max, O.min)
-        k6 = S("si", "k6", 6)
-        cp(k6, A("tg", 15, 96, 16))
-        ts(k6, k6, 15, O.bitwise_and)
-        cp(S("sh", "k6", 6), k6)
-        s2o(S("sh", "k6", 6), sub(B3, 224, 230), 6)
-        yield
-        y6 = F("y6", 6)
-        cp(y6, sub(B3, 224, 230))
-        tt(y6, y6, sub(B3, 208, 214), O.add)
-        cp(S("su", "y6", 6), y6)
-        cp(A("yv"), X(A("xs", 0, 2048), S("su", "y6", 6)))
+        cp(U("vi", 6), vi)
+        vag = LB("vag", 96)
+        cp(vag, X(A("at", 0, 2049), U("vi", 6)))
+        gath(bank(7, 16, 22), zp, "lb", vag[1], 96)
+        lo = 768 - 256 * t
+        ts(U("hp", 6), bank(7, 16, 22), float(-lo), O.add)
+        hl = U("hl", 96)
+        ts(hl, X(A("ML", lo, 2320 + 256 * t), U("hp", 6)), -1.0, O.mult, 2048.0, O.add)
+        cp(A("hz", 0, 1536, 16), A(IN))
+        scan(A("hx"), A("mr"), A("hz"), O.mult, O.add)
+        for k in range(2):
+            tt(ch("hd", k, 768), X(A("xa", 0, 2049), chunks(hl, k, 2)), ch("hx", k, 768), O.subtract)
+            act(ch("hd", k, 768), ch("hd", k, 768), AF.Square)
+        pay = LF("hpay", 192)
+        payload(pay, hl, 96, "h")
+        gath(bank(7, 32, 128), zall, "hd", 0, 1536)
+        _, ah = nearest(bank(7, 32, 128), pay, 96, "h")
+        ts(S("sh", "y6", 6), ah, 2048.0, O.add)
+        s2o(S("sh", "y6", 6), bank(7, 128, 134), 6)
+        cp(U("y6", 6), bank(7, 128, 134))
+        cp(A("yv"), X(A("xa", 0, 2049), U("y6", 6)))
         send(h, "ry%d" % t, A("yv"), "rb%d" % t, "lb%d" % t)
-        yield
+
+    def answer(t, q):
         arrived("ry%d" % t, "rb%d" % t, q)
-        tt(A("ri"), A("ry%d" % t), A("vs", 0, 96), O.add)
-        ts(A("ri"), A("ri"), 1, O.arith_shift_right)
-        cp(A("res", 0, 96), A("ri"))
-        cp(A("nx"), X(A("res"), S("su", "vL")))
-        cp(X(A("xa"), S("su", "vA")), A("nx"))
-        if t < 3:
-            cp(X(A("xs"), S("su", "vP")), A("nx"))
-            cp(X(A("xc"), S("su", "vA")), A("nx"))
-        yield
+        ri, nx = S("li", "ri", 96), LB("nx")
+        tt(ri, A("ry%d" % t), A("vs", 0, 96), O.add)
+        ts(ri, ri, 1, O.arith_shift_right)
+        cp(A("res", 0, 96), ri)
+        cp(nx, X(A("res"), U("vL")))
+        return nx
 
-    gathO("bt16", 0, 1024, setof("np"), sub(B2_, 0, 64))
-    gathO("bt16", 0, 1024, setof("n"), sub(B2_, 64, 128))
-    t64, u64 = F("t64", 64), F("u64", 64)
+    ind, rt0, rt1 = A("usb", 0, 1024), A("ML", 0, 1024), A("ML", 2064, 3088)
+    ts(ind, A("li"), 2048.0, O.is_lt)
+    ts(A("ML", 1024, 2048), A("li"), -1.0, O.mult, 2048.0, O.add)
+    d0 = A("usb", 1024, 2048)
+    act(d0, chi, AF.Identity, 0.0, RM(0))
+    for k in range(2):
+        mm(bank(k), W012, sub(ind, 512 * k, 512 * k + 512))
+    scan(rt0, d0, A("psA", 0, 1024), O.mult, O.add)
+    cp(A("g16", 0, 1024), rt0)
+    gath(bank(4, 0, 64), zst, "g16", 0, 1024)
+    gath(bank(5, 0, 64), zn, "g16", 0, 1024)
+    gath(bank(5, 64, 128), z0, "g16", 0, 1024)
+    al, t64, s64 = F("al", 64), F("t64", 64), F("s64", 64)
+    ks = A("big", 0, 3072)
+    ms(A("big", 0, 2048), 0.0)
+    ts(F("c256", 64), c4, 256.0, O.add)
     ts(t64, c4, 2048.0, O.add)
-    ts(u64, sub(B2_, 64, 128), 0.5, O.is_gt)
-    s64 = F("s64", 64)
-    cp(s64, sub(B2_, 0, 64))
-    choose(s64, u64, s64, t64, "ch64", 64)
-    cp(S("su", "l64", 64), s64)
-    cp(X(A("ks", 0, 3072), S("su", "l64", 64)), cp1)
-    ts(A("m0"), A("ks", 0, 2048), 0.0, O.is_equal)
-    scan(A("g16"), A("m0"), A("ks", 0, 2048), O.mult, O.add)
-    ms(A("el"), 0.0)
-    r91 = coef("r91", [(9, 1), (1, -1)])
-    gathO("g16", 0, 2048, s0s, sub(B2_, 0, 128))
-    ts(CQF, sub(B2_, 0, 128), -1.0, O.add)
-    cp(CQ, CQF)
-    scan(A("rk"), A("m0"), A("m0"), O.mult, O.add)
-    ts(A("rl"), A("rk"), kcol, O.is_equal)
+    ts(al, bank(5, 0, 64), 0.5, O.is_gt)
+    choose(s64, al, bank(4, 0, 64), t64, "s", 64)
+    cp(U("s64", 64), s64)
+    cp(X(ks, U("s64", 64)), A("io0"))
+    cp(U("n64", 64), bank(5, 0, 64))
+    ts(s64, bank(5, 64, 128), -2049.0, O.add)
+    tt(s64, s64, al, O.mult)
+    ts(U("e64", 64), s64, 2048.0, O.add)
+    ts(A("m0"), A("big", 0, 2048), 0.0, O.is_equal)
+    scan(A("g16"), A("m0"), A("big", 0, 2048), O.mult, O.add)
+    gath(bank(4, 384, 512), z0, "g16", 0, 2048)
+    ts(CPF, bank(4, 384, 512), -1.0, O.add)
+    ts(CP, bank(4, 384, 512), -1.0, O.add)
+    scan(A("a1"), A("m0"), A("m0"), O.mult, O.add)
+    ts(A("oh"), A("a1"), kcol, O.is_equal)
+    PO = U("po", 128)
     for k in range(4):
+        tt(ch("px", k), X(A("ML", 1024, 2048), chunks(CP, k, 4)), ch("oh", k), O.mult)
+        gath(bank(2 + k % 2, 0, 32), zneg, "px", 512 * k, 512)
+        ts(chunks(PO, k, 4), bank(2 + k % 2, 0, 32), 2048.0, O.add)
+        cp(ch("xs", k), X(A("xa", 0, 2048), chunks(PO, k, 4)), "s")
+    tt(rt1, X(NB, U("n64", 64)), rt0, O.add)
+    ms(A("big", 2048, 2064), 0.0)
+    segscan(sc, [(BK, "xs"), (I23, "oh"), (BBN, "px")], (0, 1))
+    ts(A("KT", 0, 1024), X(sc, U("e64", 64)), kkt, O.add)
+    segscan(A("usa"), [(zneg(3), "xs"), (z256(3), "oh")], (0, 1))
+    tt(A("RT", 1024, 2048), X(A("usa"), U("e64", 64)), rt1, O.add)
+    scan(A("usa", 0, 2048), A("m0"), A("xs", 0, 2048), O.mult, O.max)
+    cp(A("UT", 1024, 2048), X(A("usa"), U("e64", 64)), "s")
+    for k in range(2):
+        cp(X(A("pw"), chunks(PO, k, 2)), A("io%d" % k))
+    act(A("g16"), A("pw"), AF.Copy)
+    gath(bank(2, 0, 128), z0, "g16", 0, 2048)
+    ts(POS, bank(2, 0, 128), -1.0, O.add)
+    ts(A("cd", 1024, 2048), ccl, kc("8", 1, -8), O.is_equal)
+    for k in range(2):
         c = (512 * k, 512 * k + 512)
-        px = A("r16", 16 + 512 * k, 528 + 512 * k)
-        tt(px, X(A("mlt"), chunks(CQ, k, 4)), A("rl", *c), O.mult)
-        mm(A("psA", *c), BB16, px)
-        ts(A("ai"), A("psA", *c), 0.0625, O.mult, -0.46875, O.add)
-        cp(A("bt16", 0, 512), A("ai"))
-        mms(A("psB", *c), [(H0, A("bt16", 0, 512)), (PX10, px), (H10, A("bt16", 0, 512)), (C1, A("g16", *c))])
-        ts(A("ra", *c), A("psB", *c), r91, O.add)
-    for k in range(4):
-        act(A("r16", 16 + 512 * k, 528 + 512 * k), A("ra", 512 * k, 512 * k + 512), AF.Copy)
-    gathO("r16", 16, 2048, setof("P"), sub(B1, 0, 128))
-    empties()
-    cp(PO, sub(B1, 0, 128))
-    gather_xs()
-    cp(X(A("at"), PO), A("rb"))
-    for k in range(4):
-        act(A("gt", 512 * k, 512 * k + 512), X(A("bt", 0, 1024), chunks(CQ, k, 4)), AF.Copy)
-    act(A("g16"), A("at"), AF.Copy)
-    gathO("g16", 0, 2048, s0s, sub(B2_, 256, 384))
-    R = ["ra", "rb"]
-    gens = []
-
-    def vstep():
-        if gens:
-            next(gens[0])
+        own = [(DH, sub(chi, *c)), (DL, sub(clo, *c)), (ID, A("cd", 1024 + c[0], 1024 + c[1]))]
+        mms(bank(6), own)
+        cp(A("CK", *c), bank(6), "s")
+        mms(bank(7), own + [(DH2, sub(chi, *c)), (DL2, sub(clo, *c)), (zall(2), sub(ind, *c))])
+        act(A("BT", *c), bank(7), AF.Identity, 1.0, coef("64", [(0, 64), (6, 64)]))
+    lb0 = LB("lb0")
+    mms(bank(6, 0, 256), [(DH2, sub(chi, 0, 256)), (DL2, sub(clo, 0, 256))])
+    cp(lb0, bank(6, 0, 256), "s")
+    agents(CP, 1024, False)
+    xm = A("xs", 0, 2048)
+    zi = None
 
     for t in range(4):
-        cl = t
+        cl, last = t, t == 3
         lanes = (cl, 1024, 4)
-        gathO("lt16", 0, 256, setof("E"), sub(B1, 0, 16))
-        gathO("lt16", 0, 256, setof("n"), sub(B1, 16, 32))
-        EU, ED2 = S("su", "eu"), S("su", "ed2", 32)
-        nc = F("nc")
-        for o in (EU, sub(ED2, 0, 32, 2), sub(ED2, 1, 32, 2)):
-            ts(o, sub(B1, 0, 16), -1.0, O.add)
-        cp(nc, sub(B1, 16, 32))
-        s_keys()
-        u_scan()
-        vstep()
-        cp(A("uc"), X(A("us"), EU))
-        k_scan()
-        for w in range(16):
-            mm(sub(B1, 32, 48), bws(w), A("uc", w, 256, 16), w == 0, w == 15)
-        lanes_of(A("ks", 0, 2048), ED2)
-        sel(F("key"), 0, F("mE4", 1), F("mO4", 1))
-        ki, k2 = S("si", "ki"), S("si", "k2")
-        sf, hf, sig, rnk = F("sf"), F("hf"), F("sig"), F("rnk")
-        cp(ki, F("key"))
-        ts(k2, ki, 2047, O.bitwise_and)
-        cp(sf, k2)
-        cp(S("su", "sU"), k2)
-        ts(k2, ki, 1023, O.bitwise_and)
-        cp(S("su", "hU"), k2)
-        cp(A("acq"), X(A("act"), S("su", "hU")))
-        cp(A("xsb"), X(A("xa", 0, 2048), S("su", "sU")))
-        cp(A("xl", *lanes), A("xsb"))
-        for k in range(4):
-            c = (512 * k, 512 * k + 512)
-            mm(A("psA", *c), RKB, A("rk", *c), True, False)
-            mm(A("psA", *c), RPB, A("r16", 16 + 512 * k, 528 + 512 * k), False, False)
-            tt(A("df", *c), X(A("xl"), chunks(CQ, k, 4)), A("xs", *c), O.subtract)
-            act(A("sqs", *c), A("df", *c), AF.Square)
-        vstep()
-        for k in range(4):
-            mm(A("psA", 512 * k, 512 * k + 512), BBK, A("sqs", 512 * k, 512 * k + 512), False, True)
-        ts(k2, ki, 11, O.arith_shift_right)
-        ts(F("y"), k2, -1.0, O.mult, 4096.0, O.add)
-        cp(ki, F("y"))
-        ts(k2, ki, 4, O.arith_shift_right)
-        cp(sig, k2)
-        ts(k2, ki, 15, O.bitwise_and)
-        cp(rnk, k2)
-        vstep()
-        if t == 0:
-            cp(POS, sub(B2_, 256, 384))
-            agents()
-        build_xc(cl)
-        gr, live, want0 = F("gr"), F("live"), F("want0")
-        tt(gr, sub(B1, 32, 48), sig, O.subtract)
-        ts(live, nc, 0.5, O.is_gt)
-        ts(want0, gr, sub(lims, 1, 2), O.is_gt)
-        tt(want0, want0, live, O.mult)
-        ai0, ai1 = A("ai", 0, 256), A("ai", 256, 512)
-        cp(ai0, A("acq"))
-        ts(ai1, ai0, 15, O.bitwise_and)
-        ts(ai0, ai0, 4, O.arith_shift_right)
-        ts(A("ahl"), A("ai"), F("k128", 1), O.add, 1.0 / 2048, O.mult)
-        scan(A("gt", 0, 2048), A("m0"), A("psA"), O.mult, O.max)
-        lanes_of(A("gt", 0, 2048), ED2)
-        vstep()
-        if t:
-            s_keys()
-        for k in range(4):
-            z0 = 1024 * (k % 2)
-            c = (z0, z0 + 1024)
-            cp(A("zb", z0, z0 + 1024, 16), A("xsb", 64 * k, 64 * k + 64))
-            scan(A("xr", *c), A("mr", 0, 1024), A("zb", *c), O.mult, O.add)
-            tt(A("df", *c), X(A("xc", 0, 2048), A("acq", 64 * k, 64 * k + 64)), A("xr", *c), O.subtract)
-            act(A("df", *c), A("df", *c), AF.Square)
-            for i in range(16):
-                mm(A("psB", 64 * k, 64 * k + 64), bws(i), A("df", z0 + i, z0 + 1024, 16), i == 0, i == 15)
-        if t:
-            new_pos()
-        sel(F("kb0"), 0)
-        sel(F("kb1"), 1)
-        cp(ki, F("kb0"))
-        ts(ki, ki, 127, O.bitwise_and)
-        cp(k2, F("kb1"))
-        ts(k2, k2, 15, O.bitwise_and)
-        bf = F("bf")
-        ts(bf, ki, 16.0, O.mult)
-        tt(bf, bf, k2, O.add)
-        for h in (0, 1):
-            tt(A("tg", 256 * h, 256 * h + 256), sub(B0, 0, 256), A("ahl", 256 * h, 256 * h + 256), O.add)
-        vtr(A("tt"), A("tg"))
-        scan(A("tg"), A("mrb"), A("tt"), O.max, O.min)
-        r32 = S("si", "r32", 32)
-        ts(r32, A("tg", 15, 512, 16), 2048.0, O.mult)
-        ts(S("si", "rh"), sub(r32, 0, 16), 127, O.bitwise_and)
-        ts(S("si", "rl"), sub(r32, 16, 32), 15, O.bitwise_and)
-        ts(F("ah"), S("si", "rh"), 16.0, O.mult, -2048.0, O.add)
-        tt(F("ah"), F("ah"), S("si", "rl"), O.add)
-        ts(F("fit"), A("tg", 15, 256, 16), 4096.0, O.is_lt)
-        tt(F("ah"), F("ah"), F("fit"), O.mult)
-        ts(S("sh", "a16"), F("ah"), 2048.0, O.add)
-        s2o(S("sh", "a16"), sub(B1, 48, 64), 16)
-        has = F("has")
-        ts(has, sub(B1, 48, 64), 2047.5, O.is_lt)
-        tt(has, has, live, O.mult)
-        ts(S("su", "aU"), sub(B1, 48, 64), 2047.0, O.min)
-        cp(A("ag16"), X(A("at"), S("su", "aU")))
-        gathO("ag16", 0, 256, setof("E"), sub(B1, 64, 80))
-        gathO("ag16", 0, 256, setof("r8"), sub(B3, 480, 496))
-        gathO("ag16", 0, 256, setof("n"), sub(B3, 496, 512))
-        if t:
-            u_scan()
-            k_scan()
-        DU, DD2 = S("su", "du"), S("su", "dd2", 32)
-        for o in (DU, sub(DD2, 0, 32, 2), sub(DD2, 1, 32, 2)):
-            ts(o, sub(B1, 64, 80), -1.0, O.add)
-        dn, df_, d47 = F("dn"), F("d"), F("d47")
-        cp(A("ud"), X(A("us"), DU))
-        cp(dn, sub(B3, 496, 512))
-        cp(df_, sub(B3, 480, 496))
-        ts(d47, df_, -2047.0, O.add)
-        tt(d47, d47, has, O.mult)
-        ts(d47, d47, 2047.0, O.add)
-        cp(S("sh", "d16"), d47)
-        for w in range(16):
-            mm(sub(B3, w, 256, 16), ors(w), S("sh", "d16"))
-        tt(A("uv"), A("uc"), A("ud"), O.max)
-        cp(A("drep"), sub(B3, 0, 256))
-        for w in range(16):
-            mm(sub(B1, 112, 128), bws(w), A("uv", w, 256, 16), w == 0, w == 15)
-        for u in range(16):
-            q0 = 256 * (u % 4)
-            if u % 4 == u:
-                if u:
-                    ms(A("eq", q0, q0 + 16 * u), 0.0)
-            else:
-                ms(A("eq", q0 + 16 * (u - 4), q0 + 16 * u), 0.0)
-            ts(A("eq", q0 + 16 * u, q0 + 256), A("drep", 16 * u, 256), sub(d47, u, u + 1), O.is_equal)
-            tt(A("eq", q0 + 16 * u, q0 + 16 * u + 16), A("eq", q0 + 16 * u, q0 + 16 * u + 16), S("sb", "tri"), O.mult)
-            mm(sub(B3, 256, 512), BB, A("eq", q0, q0 + 256), u == 0, u == 15)
-        lanes_of(A("ks", 0, 2048), DD2)
-        sel(F("key"), 0, F("mE4", 1), F("mO4", 1))
-        cp(ki, F("key"))
-        ts(k2, ki, 11, O.arith_shift_right)
-        ts(F("y"), k2, -1.0, O.mult, 4096.0, O.add)
-        cp(ki, F("y"))
-        ts(k2, ki, 4, O.arith_shift_right)
-        cp(F("sigd"), k2)
-        mer, tmp = F("mer"), F("tmp")
-        tt(tmp, F("sigd"), sig, O.min)
-        tt(tmp, sub(B1, 112, 128), tmp, O.subtract)
-        ts(mer, tmp, limz, O.is_le)
-        tt(tmp, nc, dn, O.add)
-        ts(tmp, tmp, 16.5, O.is_lt)
-        tt(mer, mer, tmp, O.mult)
-        tt(mer, mer, has, O.mult)
-        vtr(A("ctr"), sub(B3, 256, 512))
-        cp(S("sh", "ct"), A("ctr", 0, 256, 16))
-        s2o(S("sh", "ct"), sub(B1, 128, 144), 16)
-        ts(tmp, sub(B1, 128, 144), 0.5, O.is_lt)
-        tt(mer, mer, tmp, O.mult)
-        want, spl, wk = F("want"), F("spl"), F("wk")
-        ts(tmp, mer, -1.0, O.mult, 1.0, O.add)
-        tt(want, want0, tmp, O.mult)
-        cp(S("sb", "wb"), want)
-        prefix(S("sb", "wb"), 16, wk, "pw", sub(B1, 144, 176))
-        ts(tmp, wk, F("ecnt", 1), O.is_lt)
-        tt(spl, want, tmp, O.mult)
-        cp(S("su", "kU"), wk)
-        cp(A("eg16"), X(A("el"), S("su", "kU")))
-        choose(bf, spl, bf, sf)
-        cp(S("su", "bU"), bf)
-        cp(A("xbb"), X(A("xa", 0, 2048), S("su", "bU")))
-        cp(A("xb", *lanes), A("xbb"))
-        idle, visit, vk = F("idle"), F("visit"), F("vk")
-        tt(tmp, mer, spl, O.add)
-        tt(idle, live, tmp, O.subtract)
-        cp(S("sb", "ib"), idle)
-        prefix(S("sb", "ib"), 16, vk, "pv", sub(B1, 208, 240))
-        x1, x2 = S("sh", "x1", 48), S("sh", "x2")
-        tt(tmp, mer, dn, O.mult)
-        tt(sub(x1, 0, 16), nc, tmp, O.add)
-        cp(sub(x1, 16, 32), nc)
-        cp(sub(x1, 32, 48), df_)
-        for w in range(16):
-            mm(A("psA", w, 512, 16), ors(w), sub(x1, 0, 32))
-            mm(A("psA", 512 + w, 768, 16), ors(w), sub(x1, 32, 48))
-        act(A("x16", 0, 768), A("psA", 0, 768), AF.Copy)
-        xr_, xn_, xd_, xl_ = [A("x16", 256 * k, 256 * k + 256) for k in range(4)]
-        ckl = A("ck16", cl, 1024, 4)
-        p0, p1, p2 = sub(B0, 0, 256), sub(B0, 256, 512), sub(B3, 0, 256)
-        mms(p0, [(M237, xr_), (I16, ckl)])
-        gathO("eg16", 0, 256, setof("r8"), sub(B1, 176, 192))
-        if t:
-            gathO("g16", 0, 2048, s0s, sub(B2_, 0, 128))
-        gathO("rk", 0, 2048, s0s, sub(B2_, 384, 512))
-        for k in range(4):
-            c = (512 * k, 512 * k + 512)
-            tt(A("df", *c), X(A("xb"), chunks(CQ, k, 4)), A("xs", *c), O.subtract)
-            act(A("df", *c), A("df", *c), AF.Square)
-            mms(A("psA", *c), [(BBN, A("sqs", *c)), (BB, A("df", *c))])
-        tl = F("tl")
-        ts(tl, lane, 1280.0, O.add)
-        choose(tmp, mer, df_, tl)
-        cp(S("su", "dL"), tmp)
-        cp(A("sz", cl, 1024, 4), p0)
-        cp(X(A("sz"), S("su", "dL")), A("zd"))
-        scan(A("bt", 0, 1024), A("d0"), A("sz", 0, 1024), O.mult, O.add)
-        cp(A("bl16"), A("bt", cl, 1024, 4))
-        choose(tmp, spl, sub(B1, 176, 192), tl)
-        cp(S("su", "eL"), tmp)
-        ts(visit, vk, 95.5, O.is_lt)
-        tt(visit, visit, idle, O.mult)
-        ts(tl, lane, 96.0, O.add)
-        choose(tmp, visit, vk, tl)
-        cp(S("su", "vL"), tmp)
-        cp(X(A("vs"), S("su", "vL")), A("xsb"))
+        NA, NL = 2064 + 256 * t, 768 - 256 * t
         q = T.cores[(rank + 1 + t % 7) % 8]
         h = T.cores[(rank - 1 - t % 7) % 8]
-        send(q, "in%d" % t, A("vs", 0, 96), "ra%d" % t, "la%d" % t)
-        ts(tl, lane, 2048.0, O.add)
-        choose(tmp, visit, sf, tl)
-        cp(S("su", "vA"), tmp)
-        cp(A("res", 96, 352), A("xsb"))
+        gath(bank(4, 0, 16), zown, "BT", cl, 256, 4)
+        LP = U("lp")
+        ts(LP, bank(4, 0, 16), -1024.0, O.add)
+        kt, mlc, rtc, uc, uv = LF("kt"), LH("mlc"), LH("rtc"), LB("uc"), LB("uv")
+        cp(kt, X(A("KT", 0, NA - 1024), LP))
+        cp(rtc, X(A("RT", 1024, NA), LP), "s")
+        cp(mlc, X(A("ML", 1024, NA), LP), "s")
+        cp(uc, X(A("UT", 1024, NA), LP), "s")
+        gath(bank(4, 32, 48), zst, "lh", rtc[1], 256)
+        gath(bank(4, 16, 32), z0, "lh", rtc[1], 256)
+        ta, tb = best(kt, 256, "s", "mr", O.mult, O.max)
+        ki, k4 = S("si", "ki"), S("si", "k4", 64)
+        cp(ki, sub(tb, 15, 256, 16))
+        ts(sub(k4, 0, 16), ki, 1023, O.bitwise_and)
+        ts(sub(k4, 16, 32), ki, 11, O.arith_shift_right, 15, O.bitwise_and)
+        ts(sub(k4, 32, 48), ki, 2047, O.bitwise_and)
+        ts(sub(k4, 48, 64), ki, 15, O.arith_shift_right)
+        cp(S("sh", "k4", 64), k4)
+        s2o(S("sh", "k4", 64), bank(4, 48, 112), 64)
+        cp(U("hU"), bank(4, 48, 64))
+        s3 = F("s3", 48)
+        cp(s3, bank(4, 64, 112))
+        sg, sf, mS = sub(s3, 0, 16), sub(s3, 16, 32), sub(s3, 32, 48)
+        st15, live, lval, tmp = F("st15"), F("live"), F("lval"), F("tmp")
+        ts(st15, bank(4, 32, 48), 15.0, O.add)
+        EU = U("eu")
+        ts(EU, bank(4, 16, 32), -1.0, O.add)
+        ts(live, mS, 15.5, O.is_gt)
+        ts(lval, sub(k4, 48, 64), 15.5, O.is_gt)
+        sp = F("sp")
+        tt(sp, st15, sg, O.subtract)
+        if t == 0:
+            ts(F("l2048"), lane, 2048.0, O.add)
+            ts(F("l2064"), lane, 2064.0, O.add)
+            ts(F("l96"), lane, 96.0, O.add)
+            ts(F("l1280"), lane, 1280.0, O.add)
+            ts(F("l1536"), lane, 1536.0, O.add)
+        choose(sp, live, sp, F("l2048"), "sp")
+        cp(U("sp"), sp)
+        xsb, xbb = LB("xsb"), LB("xbb")
+        cp(xsb, X(A("xs"), U("sp")))
+        cp(A("acq"), X(A("act"), U("hU")))
+        cp(A("XL", *lanes), xsb)
+        for k in range(4):
+            tt(ch("df", k), X(A("XL"), chunks(CP, k, 4)), ch("xs", k), O.subtract)
+            act(ch("sq", k), ch("df", k), AF.Square)
+        segscan(sc, [(I17, "oh"), (BB16, "sq")], (0, 1))
+        dsl, dbl, kb = LF("dsl"), LF("dbl"), LF("kb")
+        ts(dsl, X(sc, EU), k15, O.add)
+        tt(kb, dsl, kt, O.min)
+        _, bb = best(kb, 256, "b", "mr", O.mult, O.max)
+        kj = S("si", "kj")
+        cp(kj, sub(bb, 15, 256, 16))
+        ts(kj, kj, 15, O.bitwise_and)
+        cp(S("sh", "kj"), kj)
+        s2o(S("sh", "kj"), bank(4, 112, 128), 16)
+        tt(F("bp"), st15, bank(4, 112, 128), O.subtract)
+        cp(U("bp"), F("bp"))
+        cp(xbb, X(A("xs"), U("bp")))
+        cp(A("XB", *lanes), xbb)
+        for k in range(4):
+            tt(ch("df", k), X(A("XB"), chunks(CP, k, 4)), ch("xs", k), O.subtract)
+            act(ch("sq", k), ch("df", k), AF.Square)
+        segscan(sc2, [(I17, "oh"), (BB16, "sq")], (0, 1))
+        ts(dbl, X(sub(sc2, 0, 2048), EU), k15, O.add)
+        here, away = LB("here"), LB("away")
+        ts(here, kt, 524287.5, O.is_gt)
+        tt(away, dbl, dsl, O.is_lt)
+        tt(away, away, here, O.mult)
+        mms(bank(0, 0, 256), [(Q1, here), (TW, away)])
+        mms(bank(0, 256, 512), [(Q2, here), (TW2, away)])
+        tq = LB("tq")
+        tt(tq, bank(0, 256, 512), away, O.mult)
         if t:
-            cp(POS, sub(B2_, 0, 128))
+            ms(A("TAU", cl - 1, 1024, 4), 64.0)
+        tt(A("TAU", *lanes), bank(0, 0, 256), tq, O.add)
+        mm(bank(1, 0, 256), BB, away)
+        mms(bank(1, 256, 512), [(NREP, rtc), (BBN, away)])
+        nlr, mka, mks = LB("nlr"), LH("mka"), LH("mks")
+        cp(nlr, bank(1, 0, 256), "s")
+        ts(mks, bank(1, 256, 512), kcol, O.is_gt)
+        ts(mka, nlr, kcol, O.is_gt)
+        xn = A("xm%d" % (t % 2))
         for k in range(4):
-            c = (512 * k, 512 * k + 512)
-            ts(A("g16", *c), A("psA", *c), 0.0, O.is_lt)
-        cp(A("xb", *lanes), A("xsb"))
-        scan(A("rl"), A("m0"), A("g16"), O.mult, O.add)
-        gathO("g16", 0, 2048, s0s, sub(B2_, 0, 128))
-        lanes_of(A("rl"), ED2)
-        nl = F("nl")
-        sel(nl, 0)
-        tt(nl, nl, spl, O.mult)
-        cv, lv, cql, rp = F("cv", 128), F("lv", 128), F("cql", 128), F("rp", 128)
-        rkO, rlO = F("rkO", 128), F("rlO", 128)
-        cp(rkO, sub(B2_, 384, 512))
-        cp(x2, nl)
-        for w in range(16):
-            mm(sub(p2, w, 256, 16), ors(w), x2)
-        cp(xl_, p2)
-        mms(p0, [(I16, A("bl16")), (M7N, xl_)])
-        mms(p1, [(I16, A("bl16")), (M5, xn_), (M1N, xd_), (M81, ckl), (M7N, xl_)])
-        mms(p2, [(I23, A("bl16")), (M56, xn_), (M567, xl_), (IX, A("eg16")), (M81N, ckl)])
-        gathO("rl", 0, 2048, bws, sub(B1, 256, 384))
-        cp(lv, sub(B2_, 0, 128))
-        ts(cv, CQF, -0.75, O.mult, 1024.0 - cl / 4.0, O.add)
-        tt(cv, cv, lv, O.mult)
-        tt(cql, cv, CQF, O.add)
-        cp(S("su", "cqL", 128), cql)
-        gathO("bl16", 0, 256, setof("np"), sub(B2_, 192, 208))
-        cp(A("bt", cl, 1024, 4), p0)
-        cp(A("bt", 1024, 1280), p2)
-        cp(A("lft"), p2)
-        cp(A("dvt"), p1)
-        cp(X(A("bt"), S("su", "eL")), A("lft"))
-        if t < 3:
-            cp(A("lt16"), A("bt", cl + 1, 1024, 4))
-        else:
-            cp(A("bt16"), A("bt", 0, 1024))
-        cp(X(A("bt"), S("su", "dL")), A("dvt"))
+            tt(ch("prod", k), X(A("TAU"), chunks(CP, k, 4)), ch("oh", k), O.mult)
+            mm(bank(k % 2), B64, ch("prod", k))
+            act(ch("a1", k), bank(k % 2), AF.Abs, 1.0 / 64)
+            if not last:
+                tt(sub(xn, 512 * k, 512 * k + 512), bank(k % 2), sub(xm, 512 * k, 512 * k + 512), O.min)
+            act(ch("pen", k), ch("a1", k), AF.Abs, 1.0, kab)
+        gath(bank(4, 256, 384), zall, "prod", 0, 2048)
+        aw, cv = F("aw", 128), F("cv", 128)
+        ts(aw, bank(4, 256, 384), 0.0, O.is_gt)
+        ts(cv, bank(4, 256, 384), 32.0, O.is_lt)
+        tt(aw, aw, cv, O.mult)
+        ts(cv, CPF, -0.75, O.mult, 1024.0 - cl / 4.0, O.add)
+        tt(cv, cv, aw, O.mult)
+        tt(cv, cv, CPF, O.add)
+        cp(IX, cv)
+        segscan(sc, [(BB, "px"), (IPN, "pen")], (0, 1))
+        comb, stay, dif = LH("comb"), LH("stay"), LH("dif")
+        cp(comb, X(sc, EU), "s")
+        mm(bank(0, 0, 256), REV, comb)
+        tt(A("ML", NA, NA + 256), bank(0, 0, 256), mka, O.mult)
+        tt(stay, comb, mks, O.mult)
+        tt(dif, mlc, stay, O.subtract)
+        if not last:
+            for k in range(4):
+                mm(bank(k % 2), B64N, ch("prod", k))
+                tt(ch("xmb", k), bank(k % 2), sub(xm, 512 * k, 512 * k + 512), O.min)
+            cp(X(A("xmb"), U("sp")), zero)
+            scan(A("usa", 0, 2048), A("m0"), xn, O.mult, O.max)
+            scan(A("usb"), A("m0"), A("xmb", 0, 2048), O.mult, O.max)
+            ua, ub = A("UT", NA, NA + 256), LB("ub")
+            cp(ua, X(A("usa"), EU), "s")
+            cp(ub, X(A("usb"), EU), "s")
+            xm = xn
+            kta = A("KT", NA - 1024, NA - 768)
+            tt(kta, kt, away, O.mult)
+            _, ba = best(kta, 256, "b", "mr", O.mult, O.max)
+            t2, g2, k2 = kb, dbl, S("si", "k2", 32)
+            ms(sub(t2, 0, 1), 0.0)
+            ms(sub(tb, 15, 256, 16), 0.0)
+            tt(sub(t2, 1, 256), sub(ta, 1, 256), sub(tb, 0, 255), O.min)
+            scan(g2, A("mr", 0, 256), t2, O.mult, O.max)
+            cp(sub(k2, 0, 16), sub(g2, 15, 256, 16))
+            cp(sub(k2, 16, 32), sub(ba, 15, 256, 16))
+            ts(k2, k2, 15, O.arith_shift_right)
+            cp(S("sh", "k2", 32), k2)
+            s2o(S("sh", "k2", 32), bank(4, 128, 160), 32)
+            cp(S("sb", "k2", 32), bank(4, 128, 160))
+            rows(bank(0), S("sb", "k2", 32))
+            m2a = LB("m2a", 512)
+            cp(m2a, bank(0), "s")
+            gath(bank(4, 160, 176), zall, "lb", away[1], 256)
+            cp(U("nl"), bank(4, 160, 176))
+            nb = LB("nb")
+            cp(nb, X(NB, U("nl")), "s")
+            mms(bank(1, 0, 256), [(ID, nb), (D01, rtc), (z0(2), nlr), (z0(3), sub(m2a, 256, 512))])
+            cp(A("RT", NA, NA + 256), bank(1, 0, 256), "s")
         for k in range(4):
-            act(A("gt", 512 * k, 512 * k + 512), X(A("bt", 0, 1280), chunks(S("su", "cqL", 128), k, 4)), AF.Copy)
-        cp(A("g16"), X(A("bt", 0, 1280), S("su", "cqL", 128)))
-        mms(p0, [(M237, xr_), (M237N, xl_), (I16, ckl)])
-        mms(p1, [(M237, xl_), (I16, A("eg16"))])
-        gathO("g16", 0, 2048, setof("np"), sub(B3, 256, 384))
-        cp(A("sz", cl, 1024, 4), p0)
-        cp(A("sze"), p1)
-        cp(X(A("sz"), S("su", "eL")), A("sze"))
-        agents()
-        ts(rlO, sub(B1, 256, 384), 0.0625, O.mult)
-        tt(rp, rkO, rlO, O.subtract)
-        tt(rlO, rlO, rp, O.subtract)
-        ts(rlO, rlO, -1.0, O.add)
-        tt(rlO, rlO, lv, O.mult)
-        tt(rp, rp, rlO, O.add)
-        stc = F("stc")
-        cp(stc, sub(B2_, 192, 208))
-        tt(stc, stc, rnk, O.add)
-        ts(tl, lane, 2048.0, O.add)
-        choose(tmp, visit, stc, tl)
-        cp(S("su", "vP"), tmp)
-        tt(rp, rp, sub(B3, 256, 384), O.add)
-        cp(S("su", "npL", 128), rp)
-        if t < 3:
-            cp(S("sh", "rp16", 128), rp)
-            for w in range(16):
-                for k in range(4):
-                    mm(A("psA", 512 * k + w, 512 * k + 512, 16), ors(w), chunks(S("sh", "rp16", 128), k, 4))
-            act(A("ks", 2080, 4128), A("psA"), AF.Copy)
-        tt(X(A(R[1]), S("su", "npL", 128)), A("gt", 0, 2048), A(R[0]), O.add)
-        R = R[::-1]
-        gens[:] = [visits(t, q, h)]
-        vstep()
-        if t < 3:
-            empties()
-        order_tables(R[0], t == 3)
-        if t < 3:
-            mt = S("sb", "mt")
-            cp(mt, mer)
-            mm(sub(B1, 240, 256), o128, mt)
-            emit("v", lambda: g.vector.tensor_reduce(ap(F("zz", 1)), ap(sub(B1, 240, 256)), AX.X, O.add), [F("zz", 1)], [sub(B1, 240, 256)])
-            zi = S("si", "zi", 1)
-            cp(zi, F("zz", 1))
-            ts(zi, zi, 15, O.bitwise_and)
-            tt(limz, sub(lims, 0, 1), zi, O.add)
-    for k in range(4):
-        mm(A("psA", 512 * k, 512 * k + 512), RPP, A("r16", 16 + 512 * k, 528 + 512 * k))
-        act(A("ks", 512 * k, 512 * k + 512), A("psA", 512 * k, 512 * k + 512), AF.Copy)
-    ms(A("ks", 2048, 2080), 2048.0)
-    dmas("y", [(A("gt", 0, 2048), A("ks"), T["gt"][k::16, 0:2048], T["ks"][k::16, k:k + 2048]) for k in range(16)])
-    gathO("bt16", 0, 1024, setof("st"), sub(B2_, 0, 64))
-    ts(S("su", "l64", 64), sub(B2_, 0, 64), 2047.0, O.min)
-    vstep()
-    for k in range(2):
-        mm(A("psA", 512 * k, 512 * k + 512), NRP, A("bt16", 512 * k, 512 * k + 512))
-    ye, yb = A("el", 0, 1024), A("bt", 0, 1024)
-    ts(yb, A("psA", 0, 1024), kcol, O.is_gt)
-    vstep()
-    vstep()
-    cp(ye, X(A("gt", 0, 2048), S("su", "l64", 64)))
-    ts(ye, ye, -2048.0, O.add)
-    tt(ye, ye, yb, O.mult)
-    ts(ye, ye, 2048.0, O.add)
-    dmas("y", [(None, ye, T.ym[:, 0:1024], T["el"][:, 0:1024])])
-    vstep()
-    dmas("y", [(None, A("xa", 0, 2048), T.yx[:, 0:2048], T["xa"][:, 0:2048])])
+            mms(bank(2 + k % 2), [(ID, ch("xa", k)), (CLS[cl], ch("at", k))])
+            act(ch("xc", k), bank(2 + k % 2), AF.Copy)
+        if t:
+            nx = answer(t - 1, T.cores[(rank + t) % 8])
+            cp(X(A("xc"), U("vA")), nx)
+            cp(X(A("xa"), U("vA")), nx)
+            tt(A("UT", NL + 256, NL + 512), LB("u4"), nx, O.max)
+            mms(bank(5, 0, 256), [(zneg(3), nx), (Z16(3), ones)])
+            tt(A("RT", NL + 256, NL + 512), bank(5, 0, 256), LH("r1"), O.max)
+        pay = LF("pay", 512)
+        payload(pay, A("acq"), 256, "c")
+        for i in range(16):
+            asel(A("cx", i, 4096, 16), xsb, [[0, 256]], O.is_ge, 0, 0)
+        for k in range(4):
+            z = k % 2
+            tt(ch("cd", z, 1024), X(A("xc", 0, 2048), A("acq", 64 * k, 64 * k + 64)), ch("cx", k, 1024), O.subtract)
+            act(ch("cd", z, 1024), ch("cd", z, 1024), AF.Square)
+            gath(bank(3, 64 * k, 64 * k + 64), zall, "cd", 1024 * z, 1024)
+        key, ah = nearest(bank(3, 0, 256), pay, 256, "c")
+        ts(F("fit"), key, 4096.0, O.is_lt)
+        tt(F("fit"), F("fit"), lval, O.mult)
+        tt(ah, ah, F("fit"), O.mult)
+        ts(S("sh", "a16"), ah, 2048.0, O.add)
+        s2o(S("sh", "a16"), bank(2, 0, 16), 16)
+        cp(U("aU"), bank(2, 0, 16))
+        ag = LB("ag")
+        cp(ag, X(A("at", 0, 2049), U("aU")))
+        gath(bank(2, 16, 32), zp, "lb", ag[1], 256)
+        DP, plo = U("dp"), NL + 256
+        ts(DP, bank(2, 16, 32), float(-plo), O.add)
+        mm(bank(5, 0, 256), CREP, ag)
+        drep = LH("drep")
+        cp(drep, bank(5, 0, 256), "s")
+        gath(bank(3, 256, 272), zc, "lb", ag[1], 256)
+        df_ = F("d")
+        cp(df_, bank(3, 256, 272))
+        ud, rtd, y = LB("ud"), LH("rtd"), LH("y")
+        cp(ud, X(A("UT", plo, NA), DP))
+        cp(rtd, X(A("RT", plo, NA), DP), "s")
+        cp(y, X(A("ML", plo, NA), DP), "s")
+        tt(uv, ud, uc, O.max)
+        mm(bank(5, 0, 256), ID, dg, True, False)
+        for u in range(16):
+            e0 = 256 * (u % 4)
+            ts(A("eq", e0 + 16 * u, e0 + 256), sub(drep, 16 * u, 256), sub(df_, u, u + 1), O.is_equal)
+            mm(bank(5, 16 * u, 16 * u + 16), TW, A("eq", e0 + 16 * u, e0 + 16 * u + 16), False, u == 15)
+            if u < 15:
+                mm(bank(5, 16 * u + 16, 256), BB, A("eq", e0 + 16 * u + 16, e0 + 256), False, False)
+        if t:
+            ts(thr, F("c_01", 1), zi, O.mult, thr0, O.add)
+        mms(bank(2, 256, 512), [(W01, uv), (WC, rtc), (WD, rtd)])
+        ok1, ok2 = LB("ok1"), LB("ok2")
+        ts(ok1, bank(2, 256, 512), thr if t else thr0, O.is_le)
+        ts(ok2, bank(5, 0, 256), 0.5, O.is_lt)
+        tt(ok1, ok1, ok2, O.mult)
+        gath(bank(2, 32, 48), zall, "lb", ok1[1], 256)
+        ecnt = empties()
+        y1 = LH("y1")
+        for b in range(4):
+            mm(bank(6, 0, 256), BIT[b], rtc)
+            tt(y1, bank(6, 0, 256), y, O.mult)
+            mms(bank(6, 256, 512), [(ID, y), (SH[b], y1)])
+            cp(y, bank(6, 256, 512), "s")
+        gath(bank(3, 272, 288), zall, "lb", uc[1], 256)
+        want0, mer, want, spl, wk = F("want0"), F("mer"), F("want"), F("spl"), F("wk")
+        tt(want0, bank(3, 272, 288), mS, O.add)
+        ts(want0, want0, lim2, O.is_gt)
+        tt(want0, want0, live, O.mult)
+        dec = S("sb", "dec", 32)
+        ts(mer, bank(2, 32, 48), 15.5, O.is_gt)
+        ts(tmp, bank(2, 32, 48), 15.5, O.is_lt)
+        wb = S("sb", "wb")
+        tt(wb, want0, tmp, O.mult)
+        prefix(wb, 16, wk, "pw", bank(2, 48, 80))
+        ts(spl, wk, ecnt, O.is_lt)
+        tt(spl, spl, wb, O.mult)
+        cp(U("kU"), wk)
+        idle, visit, vk = S("sb", "idle"), F("visit"), F("vk")
+        tt(tmp, tmp, live, O.mult)
+        tt(idle, tmp, spl, O.subtract)
+        prefix(idle, 16, vk, "pv", bank(2, 80, 112))
+        ts(visit, vk, 95.5, O.is_lt)
+        tt(visit, visit, idle, O.mult)
+        choose(F("vl"), visit, vk, F("l96"), "vl")
+        cp(U("vL"), F("vl"))
+        cp(X(A("vs"), U("vL")), xsb)
+        send(q, "in%d" % t, A("vs", 0, 96), "ra%d" % t, "la%d" % t)
+        choose(F("va"), visit, sf, F("l2064"), "va")
+        cp(U("vA"), F("va"))
+        cp(A("res", 96, 352), xsb)
+        cp(sub(dec, 0, 16), mer)
+        ts(sub(dec, 16, 32), spl, -1.0, O.mult, 1.0, O.add)
+        rows(bank(3), dec)
+        mr_, ns_ = bank(3, 0, 256), bank(3, 256, 512)
+        eg = LB("eg")
+        cp(eg, X(A("el", 0, 256), U("kU")), "s")
+        gath(bank(2, 112, 128), zc, "lb", eg[1], 256)
+        DE = U("de", 32)
+        choose(F("dl"), mer, df_, F("l1280"), "dl")
+        cp(sub(DE, 0, 16), F("dl"))
+        choose(F("elst"), spl, bank(2, 112, 128), F("l1536"), "el")
+        cp(sub(DE, 16, 32), F("elst"))
+        le, de, lb2, sd = LB("le"), LB("de", 512), LB("lb2"), LB("sd")
+        ts(le, lb0, coef("nl%d" % t, [(0, NL // 16), (6, NL // 16)]), O.add)
+        tt(le, le, A("CK", *lanes), O.add)
+        ts(sub(de, 0, 256), le, hi4, O.mult, cde, O.add)
+        ts(lb2, lb0, coef("na%d" % t, [(0, NA // 16), (6, NA // 16), (2, 1)]), O.add)
+        mm(bank(5, 256, 512), zn(2), rtc)
+        tt(A("BT", *lanes), bank(5, 256, 512), le, O.add)
+        ee = sub(de, 256, 512)
+        tt(ee, lb2, eg, O.add)
+        tt(sd, le, ee, O.subtract)
+        tt(sd, ns_, sd, O.mult)
+        tt(A("BT", 1024, 1280), sd, ee, O.add)
+        cp(X(A("BT"), DE), de)
+        agents(IX, 1280, last)
+        tt(dif, ns_, dif, O.mult)
+        tt(y1, mr_, y, O.mult)
+        tt(dif, dif, stay, O.add)
+        tt(A("ML", NL, NL + 256), dif, y1, O.add)
+        if not last:
+            u1, u2, u4, p1, n1 = LB("u1"), LB("u2"), LB("u4"), LH("p1"), LB("n1")
+            tt(u1, ns_, ua, O.mult)
+            tt(u2, mr_, uv, O.mult)
+            tt(p1, mr_, rtd, O.mult)
+            tt(n1, ns_, nlr, O.mult)
+            tt(u1, u1, u2, O.max)
+            tt(u4, u1, ub, O.max)
+            mms(bank(5, 256, 512), [(zn(2), rtc), (zn(2), p1), (z0n(2), nlr), (z0(2), n1), (z0(3), sub(m2a, 0, 256))])
+            tt(LH("r1"), bank(5, 256, 512), p1, O.max)
+            mm(bank(2, 128, 144), o128, sub(dec, 0, 16))
+            emit("v", lambda: g.vector.tensor_reduce(ap(F("zz", 1)), ap(bank(2, 128, 144)), AX.X, O.add), [F("zz", 1)], [bank(2, 128, 144)])
+            zj, zi = S("si", "zj", 1), F("zi", 1)
+            cp(zj, F("zz", 1))
+            ts(zj, zj, 15, O.bitwise_and)
+            cp(zi, zj)
+        host(t, h)
+    gath(bank(6, 0, 64), zown, "BT", 0, 1024)
+    cp(U("l64", 64), bank(6, 0, 64))
+    ts(A("RT", 0, 1024), X(A("ML"), U("l64", 64)), -1.0, O.mult, 2048.0, O.add)
+    dma("y", None, A("RT", 0, 1024), T.ym[:, 0:1024], T["RT"][:, 0:1024])
+    nx = answer(3, T.cores[(rank + 4) % 8])
+    cp(X(A("xa"), U("vA")), nx)
+    dma("y", None, A("xa", 0, 2048), T.yx[:, 0:2048], T["xa"][:, 0:2048])
     issue()

@@ -5,25 +5,26 @@ SCRATCH = {}
 for _n, _w, _d in [
         ("ML", 3088, F4), ("RT", 3088, F4), ("KT", 1808, F4), ("UT", 3088, B2), ("BT", 1792, B2), ("big", 4128, F4),
         ("act", 1024, I4), ("xa", 2320, B2), ("xc", 2320, B2), ("xs", 2304, B2), ("xm0", 2048, B2), ("xm1", 2048, B2), ("xmb", 2304, B2),
-        ("usa", 2064, B2), ("usb", 2048, B2), ("oh", 2048, B2), ("m0", 2048, B2), ("df", 2048, B2), ("sq", 2048, B2),
-        ("prod", 2048, B2), ("cx", 4096, B2), ("cd", 2048, B2), ("hz", 1536, B2), ("hx", 1536, B2), ("at", 2064, B2),
-        ("XL", 1024, B2), ("TAU", 1024, B2), ("CK", 1024, B2), ("el", 1280, B2), ("eq", 1024, B2),
-        ("px", 2048, H2), ("mr", 1536, B2), ("mrb", 512, B2), ("ones", 256, B2), ("orp", 2048, B2),
-        ("wm", 5760, B2), ("zs", 2016, B2), ("lb", 7776, B2), ("lh", 3328, H2), ("lf", 4160, F4), ("li", 1024, I4), ("acq", 256, U2),
-        ("vs", 352, B2), ("res", 352, B2), ("yv", 96, B2),
-        ("sm", 2560, F4), ("si", 288, I4), ("su", 1120, U2), ("sh", 144, H2), ("sb", 256, B2), ("lim", 2, I4), ("wtc", 1, I4)]:
+        ("usa", 2064, B2), ("atp", 2048, B2), ("oh", 2048, B2), ("sel", 2048, B2), ("m0", 2048, B2), ("df", 2048, B2), ("sq", 2048, B2),
+        ("prod", 2048, B2), ("cx", 4096, B2), ("pt", 2048, B2), ("hx", 1536, B2), ("at", 2064, B2),
+        ("XL", 1024, B2), ("TAU", 1024, B2), ("CK", 1024, B2), ("el", 256, B2), ("eq", 1024, B2),
+        ("px", 2048, H2), ("mr", 256, B2), ("mrb", 512, B2), ("ones", 256, B2), ("orp", 2048, B2),
+        ("wm", 7680, B2), ("zs", 2448, B2), ("lb", 9152, B2), ("lh", 3808, H2), ("lf", 3456, F4), ("li", 1024, I4), ("acq", 256, U2),
+        ("vs", 512, B2), ("yv", 96, B2),
+        ("sm", 2560, F4), ("si", 288, I4), ("su", 1200, U2), ("sh", 144, H2), ("sb", 320, B2), ("lim", 2, I4), ("wtc", 1, I4)]:
     SCRATCH[_n] = ("sbuf", [128, _w], _d)
-ALIAS = {"a1": ("df", 0, 2048), "pen": ("sq", 0, 2048), "XB": ("XL", 0, 1024), "g16": ("lh", 0, 2048), "pw": ("big", 2064, 2048),
-         "hd": ("cd", 0, 1536), "atp": ("prod", 0, 2048), "io0": ("RT", 0, 1024), "io1": ("RT", 2064, 1024)}
+ALIAS = {"a1": ("df", 0, 2048), "pen": ("sq", 0, 2048), "XB": ("XL", 0, 1024), "g16": ("lh", 0, 2048),
+         "hd": ("hx", 0, 1536), "usb": ("df", 0, 2048)}
 for _t in range(4):
     SCRATCH["in%d" % _t] = ("sbuf", [128, 96], B2)
     SCRATCH["ry%d" % _t] = ("sbuf", [128, 96], B2)
 SCRATCH["psA"] = ("psum", [128, 2048], F4)
 SCRATCH["psB"] = ("psum", [128, 2048], F4)
-SEMAPHORES = ["sv", "ss", "st", "sg"] + ["d%d" % i for i in range(12)]
+SEMAPHORES = ["sv", "ss", "st", "sg"] + ["d%d" % i for i in range(16)]
 for _t in range(4):
     SEMAPHORES += ["ra%d" % _t, "rb%d" % _t, "la%d" % _t, "lb%d" % _t]
 BIG = 33554432.0
+PLAN, PASSES = {}, 6
 BEHIND = 800
 HOP, SLACK, DMA, LINK = 60, 100, 2500, 4000
 
@@ -71,20 +72,20 @@ def rank_program(g, core, T, topo):
                 n, a, b, s = y
                 if n[:2] == "ps":
                     for k in range(a // 512, (b - 1) // 512 + 1):
-                        acc.append((n, 512 * k, 512 * k + 512, True, True))
+                        acc.append((n, 512 * k, 512 * k + 512, True, True, 1))
                 else:
-                    acc.append((n, a, b, ww, False))
+                    acc.append((n, a, b, ww, False, s))
         me = len(ops)
         deps = {}
-        for n, a, b, w, ps in acc:
+        for n, a, b, w, ps, s in acc:
             for r in recs.get((n, True), []) + (recs.get((n, False), []) if w else []):
-                if r[0] < b and a < r[1] and r[2] != me:
+                if r[0] < b and a < r[1] and r[2] != me and not (s == r[3] and (a - r[0]) % s):
                     deps[r[2]] = deps.get(r[2], True) and ps
-        for n, a, b, w, ps in acc:
+        for n, a, b, w, ps, s in acc:
             if w:
                 for k in ((n, True), (n, False)):
-                    recs[k] = [r for r in recs.get(k, []) if not (a <= r[0] and r[1] <= b)]
-            recs.setdefault((n, w), []).append((a, b, me))
+                    recs[k] = [r for r in recs.get(k, []) if not (a <= r[0] and r[1] <= b and (s == 1 or (s == r[3] and (a - r[0]) % s == 0)))]
+            recs.setdefault((n, w), []).append((a, b, me, s))
         return deps
 
     def width(x):
@@ -126,34 +127,46 @@ def rank_program(g, core, T, topo):
 
         def hop(d, i):
             return 0 if ops[i]["deps"][d] and ops[d]["e"] == ops[i]["e"] == "t" else HOP
-        tail = [0.0] * n
-        for i in range(n - 1, -1, -1):
-            tail[i] = ops[i]["busy"] + ops[i]["lat"] + max([tail[j] + hop(i, j) for j in succ[i]] + [0])
-        left = [len(o["deps"]) for o in ops]
-        at = [0.0] * n
-        ready = {e: [] for e in "vstgya"}
-        free = {e: 0.0 for e in "vstgya"}
-        for i in range(n):
-            if not left[i]:
-                ready[ops[i]["e"]].append(i)
-        order = []
-        while len(order) < n:
-            can = dict(ready)
-            can["s"] = ready["s"] + [i for i in ready["v"] if ops[i]["alt"]]
-            can["v"] = [i for i in ready["v"] if not ops[i]["alt"] or free["s"] > max(free["v"], at[i]) + BEHIND]
-            t, e = min((max(free[x], min(at[i] for i in can[x])), x) for x in can if can[x])
-            i = max((i for i in can[e] if at[i] <= t + SLACK), key=lambda i: (tail[i], -i))
-            ready[ops[i]["e"]].remove(i)
+        pred = [list(o["deps"]) for o in ops]
+
+        def plan(prio, eng):
+            nxt, left = (pred, [len(x) for x in succ]) if eng else (succ, [len(x) for x in pred])
+            home = eng or [o["e"] for o in ops]
+            at, end, got, order = [0.0] * n, [0.0] * n, list(home), []
+            ready = {e: [] for e in "vstgya"}
+            free = {e: 0.0 for e in "vstgya"}
+            for i in range(n):
+                if not left[i]:
+                    ready[home[i]].append(i)
+            while len(order) < n:
+                can = dict(ready)
+                if not eng:
+                    can["s"] = ready["s"] + [i for i in ready["v"] if ops[i]["alt"]]
+                    can["v"] = [i for i in ready["v"] if not ops[i]["alt"] or free["s"] > max(free["v"], at[i]) + BEHIND]
+                t, e = min((max(free[x], min(at[i] for i in can[x])), x) for x in can if can[x])
+                i = max((i for i in can[e] if at[i] <= t + SLACK), key=lambda i: (prio[i], -i))
+                ready[home[i]].remove(i)
+                got[i] = e
+                order.append(i)
+                free[e] = end[i] = max(t, at[i]) + (ops[i]["busy"] if e == ops[i]["e"] else ops[i]["alt"][1])
+                for j in nxt[i]:
+                    at[j] = max(at[j], end[i] + (ops[j]["lat"] + hop(j, i) if eng else ops[i]["lat"] + hop(i, j)))
+                    left[j] -= 1
+                    if not left[j]:
+                        ready[home[j]].append(j)
+            return max(end[i] + ops[i]["lat"] for i in range(n)), order, got, end
+        if n not in PLAN:
+            tail = [0.0] * n
+            for i in range(n - 1, -1, -1):
+                tail[i] = ops[i]["busy"] + ops[i]["lat"] + max([tail[j] + hop(i, j) for j in succ[i]] + [0])
+            plans = [plan(tail, None)]
+            for _ in range(PASSES):
+                plans.append(plan(plan(plans[-1][3], plans[-1][2])[3], None))
+            PLAN[n] = min(plans, key=lambda p: p[0])
+        order = PLAN[n][1]
+        for i, e in enumerate(PLAN[n][2]):
             if e != ops[i]["e"]:
-                ops[i].update({"e": e, "fn": ops[i]["alt"][0], "busy": ops[i]["alt"][1]})
-            order.append(i)
-            t = max(t, at[i])
-            free[e] = t + ops[i]["busy"]
-            for j in succ[i]:
-                at[j] = max(at[j], free[e] + ops[i]["lat"] + hop(i, j))
-                left[j] -= 1
-                if not left[j]:
-                    ready[ops[j]["e"]].append(j)
+                ops[i].update({"e": e, "fn": ops[i]["alt"][0]})
         mark = {}
         for i in order:
             o = ops[i]
@@ -212,6 +225,9 @@ def rank_program(g, core, T, topo):
     def ms(out, c):
         emit("v", lambda: g.vector.memset(ap(out), c), [out], [])
 
+    def fill(out, c):
+        iota(out, [[0, width(out)]], c, 0)
+
     def act(out, i, f, scale=1.0, bias=0.0):
         emit("s", lambda: g.scalar.activation(ap(out), ap(i), f, bias=ap(bias), scale=ap(scale)), [out], [i, scale, bias])
 
@@ -230,10 +246,12 @@ def rank_program(g, core, T, topo):
 
     nd = [0]
 
-    def dma(e, o, i, oa, ia):
+    def dma(e, o, i, oa, ia, add=False):
         who = "d%d" % nd[0]
         nd[0] += 1
-        emit(e, lambda: Q[e].dma_start(oa, ia).then_inc(T.sem[who], 16), [o] if o else [], [i] if i else [], sem=who, inc=16, busy=60, lat=DMA)
+        how = {"accum_op": O.add} if add else {}
+        emit(e, lambda: Q[e].dma_start(oa, ia, **how).then_inc(T.sem[who], 16), [o] if o else [], [i] if i else [], sem=who, inc=16,
+             busy=1000 if e == "g" else 60, lat=DMA + (2000 if add else 0))
 
     slots = {}
     used = {}
@@ -270,9 +288,9 @@ def rank_program(g, core, T, topo):
         w = (off[2] - off[1]) // n
         return sub(off, k * w, k * w + w)
 
-    for n, src, q in (("li", T.ml, "y"), ("xa", T.x0, "s"), ("act", T.ac, "y"), ("lim", T.lims, "s"), ("wtc", T.wt, "y")):
+    for n, src in (("li", T.ml), ("xa", T.x0), ("act", T.ac), ("lim", T.lims), ("wtc", T.wt)):
         w = src.shape[1]
-        dma(q, A(n, 0, w), None, T[n][:, 0:w], src[:, 0:w])
+        dma("y", A(n, 0, w), None if n == "li" else A("li", 0, 1), T[n][:, 0:w], src[:, 0:w])
 
     ones = A("ones")
     ms(ones, 1.0)
@@ -288,9 +306,7 @@ def rank_program(g, core, T, topo):
     asel(BB, o128, [[-16, 8], [0, 16]], O.is_ge, 0, 1)
     asel(BB, BB, [[16, 8], [0, 16]], O.is_ge, 15, -1)
     asel(ID, o128, [[-1, 128]], O.is_equal, 0, 1)
-    iota(A("io0"), [[1, 1024]], 1, 0)
-    iota(A("io1"), [[1, 1024]], 1025, 0)
-    chi, clo, ccl = A("cx", 0, 1024), A("cx", 1024, 2048), A("cd", 0, 1024)
+    chi, clo, ccl = A("xm0", 0, 1024), A("xm0", 1024, 2048), A("prod", 0, 1024)
     iota(chi, [[1, 64], [0, 16]], 0, 0)
     iota(clo, [[0, 64], [1, 16]], 0, 0)
     iota(ccl, [[0, 256], [1, 4]], 0, 0)
@@ -359,13 +375,14 @@ def rank_program(g, core, T, topo):
     tt(W012, W012, zall(2), O.add)
     PE_, PO_, P01, P10 = mk("PE", ID, mE), mk("PO", ID, mO), mk("P01", SP, mE), mk("P10", SN, mO)
     BB16, BBN, B64, B64N, BK = mk("BB16", BB, 16.0), mk("BBN", BB, -1.0), mk("B64", BB, 64.0), mk("B64N", BB, -64.0), mk("BK", BB, -32768.0)
-    I17, I23, IPN = mk("I17", ID, 131072.0), mk("I23", ID, 8388608.0), mk("IPN", ID, -4096.0)
+    N16, K16 = mk("N16", BB, RM(1), 65536.0), mk("K16", ID, kc("k16", -65536, 65536))
+    I23, IPN = mk("I23", ID, 8388608.0), mk("IPN", ID, -16384.0)
     NREP, CREP = mk("NREP", BB, RM(2)), mk("CREP", BB, F("c_c", 1))
     BIT = [mk("BIT%d" % b, BB, RM(4 + b)) for b in range(4)]
     CLS = [mk("CLS%d" % m, BB, RM(8 + m), 64.0) for m in range(4)]
     D01 = mk("D01", ID, coef("01", [(0, 1), (1, 1)]))
     DH, DL, DH2, DL2 = mk("DH", ID, RM(4)), mk("DL", ID, RM(5)), mk("DH2", ID, coef("06", [(0, 1), (6, 1)])), mk("DL2", ID, coef("17", [(1, 1), (7, 1)]))
-    Q1, Q2, TW2, ZERO = W1("Q1"), W1("Q2"), mk("TW2", TW, -2.0), mk("ZERO", ID, 0.0)
+    Q1, Q2, TW2, IDN = W1("Q1"), W1("Q2"), mk("TW2", TW, -2.0), mk("IDN", ID, -1.0)
     ts(Q1, ID, -0.5, O.mult)
     tt(Q1, Q1, TW, O.subtract)
     ts(Q2, ID, 16.0, O.mult)
@@ -379,30 +396,39 @@ def rank_program(g, core, T, topo):
     lane, c4 = F("lane"), F("c4", 64)
     ts(c4, F("c64", 64), kcol, O.add)
     lane = sub(c4, 0, 16)
-    k15, kkt, kab, k128 = kc("15", -1, 15), kc("kt", -2048, 15 * 2048 + 2048), kc("ab", -1, -0.5), kc("128", 128, 0)
-    ms(A("mr"), 1.0)
-    ms(A("mr", 0, 1536, 16), 0.0)
-    ms(A("mrb"), 0.0)
+    kneg, kab, k128 = kc("neg", -1, 0), kc("ab", -1, -0.5), kc("128", 128, 0)
+    DK = mk("DK", ID, kc("kt", -2048, 16 * 2048))
+    fill(A("mr"), 1)
+    fill(A("mr", 0, 256, 16), 0)
+    fill(A("mrb"), 0)
     ms(A("mrb", 0, 512, 16), BIG)
-    ms(A("hz"), 0.0)
-    ms(A("XL"), 0.0)
-    ms(A("TAU"), 64.0)
-    ms(A("vs"), 0.0)
-    ms(A("el", 0, 256), 0.0)
-    ms(A("xs", 2048, 2304), 0.0)
-    ms(A("xa", 2048, 2064), 64.0)
-    ms(A("usa", 2048, 2064), 0.0)
-    ms(A("UT", 2048, 2064), 0.0)
-    ms(A("ML", 2048, 2064), 0.0)
-    ms(A("RT", 2048, 2064), 0.0)
-    ms(A("KT", 1024, 1040), 0.0)
+    fill(A("XL"), 0)
+    ts(A("TAU"), A("XL"), 0.25, O.add)
+    zbig = zset("big", 16384.0)
+    I11, I17N, DK16, REVN = mk("I11", ID, 1.0 / 2048), mk("I17N", ID, -17.0), mk("DK16", ID, kc("16", 0.0625, -0.75)), mk("REVN", REV, -1.0)
+    fill(A("vs"), 0)
+    fill(A("xs", 2048, 2304), 0)
+    fill(A("xa", 2048, 2064), 64)
+    fill(A("usa", 2048, 2064), 0)
+    fill(A("UT", 2048, 2064), 0)
+    fill(A("ML", 2048, 2064), 0)
+    fill(A("RT", 2048, 2064), 0)
+    fill(A("KT", 1024, 1040), 0)
     ts(A("RT", 2049, 2050), RM(2), 99.0, O.mult)
     cp(A("at", 2048, 2049), coef("far", [(4, 127), (5, 15), (6, 128), (7, 1)]))
-    zero = LB("zero")
-    ms(zero, 0.0)
+    zero, i256 = LB("zero"), LB("i256")
+    fill(zero, 0)
+    iota(i256, [[1, 256]], 0, 0)
+    zk = zset("k", kcol)
+    l05, l2048, l2064, l256, l32 = F("l05"), F("l2048"), F("l2064"), F("l256"), F("l32", 32)
+    for c, v in ((l05, 0.5), (l2048, 2048.0), (l2064, 2064.0), (l256, 256.0), (sub(l32, 0, 16), 1280.0), (sub(l32, 16, 32), 1536.0)):
+        ts(c, lane, v, O.add)
+    TS = {1: (PE_, P01, P10, PO_)}
+    for w in (16, -1):
+        TS[w] = [mk("%s%d" % (n, w + 1), m, float(w)) for n, m in zip("abcd", TS[1])]
     dg = LB("dg")
     ts(dg, sub(clo, 0, 256), kcol, O.is_lt, -64.0, O.mult)
-    NB, nbi = A("sb", 224, 256), S("si", "nbi", 32)
+    NB, nbi = S("sb", "NB", 32), S("si", "nbi", 32)
     ts(nbi, sub(F("i144", 144), 0, 32), coef("pw", [(4, 1), (5, 0.5), (6, 0.25), (7, 0.125)]), O.mult, -0.4375, O.add)
     ts(nbi, nbi, 1, O.bitwise_and)
     cp(NB, nbi)
@@ -410,7 +436,7 @@ def rank_program(g, core, T, topo):
     cp(lims, A("lim"))
     thr0, thr = F("thr0", 1), F("thr", 1)
     ts(thr0, sub(lims, 0, 1), 256.0, O.add, F("c_01", 1), O.mult)
-    tt(thr0, thr0, coef("t23", [(2, 16), (3, -1)]), O.add)
+    ts(thr0, thr0, coef("t23", [(2, 16), (3, -1)]), O.add, 0.5, O.add)
     lim2 = F("lim2", 1)
     ts(lim2, sub(lims, 1, 2), 256.0, O.add)
     hi4 = coef("hi4", [(r, 1) for r in (4, 5, 6, 7, 8, 9, 10, 11)])
@@ -428,6 +454,11 @@ def rank_program(g, core, T, topo):
     def s2o(r1, out, n):
         mms(sub(out, 0, n, 2), [(PE_, sub(r1, 0, n, 2)), (P01, sub(r1, 1, n, 2))])
         mms(sub(out, 1, n, 2), [(P10, sub(r1, 0, n, 2)), (PO_, sub(r1, 1, n, 2))])
+
+    def lin(out, tr, terms):
+        n = width(tr)
+        for h in (0, 1):
+            mms(sub(out, h, n // 16, 2), [(TS[w][2 * h + z], sub(tr, 16 * z + r, n, 32)) for r, w in terms for z in (0, 1)][::1 - 2 * h])
 
     def prefix(ind, n, out, tag, ps):
         mm(sub(ps, 0, n), TW, ind)
@@ -458,29 +489,45 @@ def rank_program(g, core, T, topo):
             mms(ps, [(m, ch(n, k)) for m, n in passes])
             scan(sub(out, 512 * k, 512 * k + 512), ch("m0", k), ps, O.mult, O.max, sub(out, 512 * k - 1, 512 * k) if k else 0.0)
 
+    def byslot(out):
+        for k in range(4):
+            mm(bank(k % 2), BB16, ch("sq", k))
+            scan(sub(out, 512 * k, 512 * k + 512), ch("sel", k), bank(k % 2), O.add, O.min, sub(out, 512 * k - 1, 512 * k) if k else 0.0)
+
     CP, CPF, POS, IX = U("cp", 128), F("cpf", 128), U("pos", 128), U("ix", 128)
     sc, sc2 = A("big", 0, 2064), A("big", 2064, 4128)
 
     def agents(lst, hi, last):
         for k in range(4):
             cp(ch("atp", k), X(A("BT", 0, hi), chunks(lst, k, 4)))
-        for k in range(4):
+        for k in range(0 if last else 4):
             cp(ch("at", k), X(A("atp"), chunks(POS, k, 4)))
         if hi > 1024 and not last:
-            gath(bank(4, 384, 512), zc, "atp", 0, 2048)
-            cp(CPF, bank(4, 384, 512))
-            cp(CP, bank(4, 384, 512))
+            for k in range(2):
+                gath(bank(k, 0, 64), zc, "atp", 1024 * k, 1024)
+                cp(chunks(CP, k, 2), bank(k, 0, 64))
+                ts(chunks(CPF, k, 2), bank(k, 0, 64), 4096.0, O.add)
 
     def empties():
         gath(bank(6, 0, 64), zn, "BT", 0, 1024)
         e64, r64, eb = F("e64", 64), F("r64", 64), S("sb", "e64", 64)
         ts(eb, bank(6, 0, 64), 0.5, O.is_lt)
         e = prefix(eb, 64, r64, "pe", bank(6, 64, 192))
-        ts(e64, r64, 255.5, O.is_lt)
-        tt(e64, e64, eb, O.mult)
-        choose(r64, e64, r64, F("c256", 64), "s", 64)
-        cp(U("l64", 64), r64)
-        cp(X(A("el"), U("l64", 64)), A("CK"))
+        inc, acc, rb = sub(F("peinc"), 1, 65), F("acc"), S("sb", "rb", 64)
+        for u in range(16):
+            emit("s", lambda u=u: g.scalar.activation(ap(e64), ap(inc), AF.Sign, bias=ap(sub(l05, u, u + 1)), scale=-1.0, accum_out=ap(sub(acc, u, u + 1))),
+                 [e64, sub(acc, u, u + 1)], [inc, l05], busy=90)
+        ts(acc, acc, 8.0, O.mult, 512.0, O.add)
+        ts(acc, acc, 1008.0, O.min)
+        ts(U("ub"), acc, 0.0625, O.mult)
+        ts(rb, eb, 1000.0, O.mult, -1000.0, O.add)
+        tt(rb, r64, rb, O.subtract)
+        ek = LB("ek")
+        tt(ek, X(rb, U("ub")), i256, O.is_equal)
+        gath(bank(6, 192, 208), zk, "lb", ek[1], 256)
+        tt(acc, bank(6, 192, 208), acc, O.add)
+        cp(U("ec"), acc)
+        cp(A("el"), X(A("CK"), U("ec")))
         return e
 
     def send(dst, out, src, rs, ls):
@@ -495,18 +542,27 @@ def rank_program(g, core, T, topo):
     def arrived(buf, rs, src):
         emit("a", None, [A(buf)], [], sem=rs, inc=len(topo.engines(src, core)[:4]), busy=0, after=[sent[rs]])
 
-    def payload(out, lst, n, tag):
-        ai = S("li", tag, 2 * n)
-        cp(sub(ai, 0, n), lst)
-        ts(sub(ai, n, 2 * n), sub(ai, 0, n), 15, O.bitwise_and)
-        ts(sub(ai, 0, n), sub(ai, 0, n), 4, O.arith_shift_right)
-        ts(out, ai, k128, O.add, 1.0 / 2048, O.mult)
+    def payload(lst, n, tag, ps):
+        idf, hi, dl = LH("id" + tag, n), LH("hi" + tag, n), LB("dl" + tag, n)
+        cp(idf, lst)
+        ts(hi, idf, 0.0625, O.mult, 1535.53125, O.add)
+        mms(ps, [(ID, idf), (I17N, hi)])
+        ts(dl, ps, 1.0 / 2048, O.mult, 12.75, O.add)
+        return hi, dl
 
-    def nearest(ps, pay, n, tag):
-        key = LF("k" + tag, 2 * n)
-        for h in (0, 1):
-            tt(sub(key, n * h, n * h + n), ps, sub(pay, n * h, n * h + n), O.add)
-        a, b = best(key, 2 * n, tag, "mrb", O.max, O.min)
+    def sums(ps, src, a, hi):
+        n = width(ps)
+        mm(ps, I11, hi, True, False)
+        mm(ps, DK16, A("ones", 0, n), False, False)
+        for w in range(16):
+            mm(ps, zall(w), A(src, a + w, a + 16 * n, 16), False, w == 15)
+
+    def nearest(ps, dl, n, tag):
+        a, b = LF("t" + tag, 2 * n), LF("k" + tag, 2 * n)
+        vtr(sub(a, 0, n), ps)
+        tt(sub(b, 0, n), ps, dl, O.add)
+        vtr(sub(a, n, 2 * n), sub(b, 0, n))
+        scan(b, A("mrb", 0, 2 * n), a, O.max, O.min)
         m = n // 16
         r = S("si", "r" + tag, 2 * m)
         ts(r, sub(b, 15, 2 * n, 16), 2048.0, O.mult)
@@ -526,21 +582,40 @@ def rank_program(g, core, T, topo):
         ts(vi, vi, 2047, O.bitwise_and)
         cp(U("vi", 6), vi)
         vag = LB("vag", 96)
-        cp(vag, X(A("at", 0, 2049), U("vi", 6)))
-        gath(bank(7, 16, 22), zp, "lb", vag[1], 96)
+        cp(vag, X(A("pt"), U("vi", 6)))
+        vtr(LB("vagt", 96), vag)
+        lin(bank(7, 8, 14), LB("vagt", 96), [(0, 16), (1, 1)])
+        cp(U("vp", 6), bank(7, 8, 14))
+        cp(vag, X(A("atp"), U("vp", 6)))
+        if t == 3:
+            vt, vc, vw = LB("vt", 96), F("vc", 6), F("vw", 6)
+            cp(vt, X(A("prod"), U("vp", 6)))
+            vtr(LB("vagt", 96), vag)
+            lin(bank(7, 8, 14), LB("vagt", 96), [(4, 16), (5, 1)])
+            ts(vc, bank(7, 8, 14), 4096.0, O.add)
+            gath(bank(7, 0, 6), zbig, "lb", vt[1], 96)
+            ts(vw, vc, 0.25, O.mult, 4096.0 - t / 4.0, O.add)
+            tt(vw, bank(7, 0, 6), vw, O.min)
+            tt(vw, vw, vc, O.max)
+            ts(U("vx", 6), vw, -4096.0, O.add)
+            cp(vag, X(A("BT", 0, 1280), U("vx", 6)))
+        vtr(LB("vagt", 96), vag)
+        lin(bank(7, 16, 22), LB("vagt", 96), [(6, 16), (7, 1)])
         lo = 768 - 256 * t
         ts(U("hp", 6), bank(7, 16, 22), float(-lo), O.add)
         hl = U("hl", 96)
         ts(hl, X(A("ML", lo, 2320 + 256 * t), U("hp", 6)), -1.0, O.mult, 2048.0, O.add)
-        cp(A("hz", 0, 1536, 16), A(IN))
-        scan(A("hx"), A("mr"), A("hz"), O.mult, O.add)
+        for i in range(16):
+            if i % 2:
+                asel(A("hx", i, 1536, 16), A(IN), [[0, 96]], O.is_ge, 0, 0)
+            else:
+                cp(A("hx", i, 1536, 16), A(IN))
         for k in range(2):
             tt(ch("hd", k, 768), X(A("xa", 0, 2049), chunks(hl, k, 2)), ch("hx", k, 768), O.subtract)
             act(ch("hd", k, 768), ch("hd", k, 768), AF.Square)
-        pay = LF("hpay", 192)
-        payload(pay, hl, 96, "h")
-        gath(bank(7, 32, 128), zall, "hd", 0, 1536)
-        _, ah = nearest(bank(7, 32, 128), pay, 96, "h")
+        hi, dl = payload(hl, 96, "h", bank(7, 160, 256))
+        sums(bank(7, 32, 128), "hd", 0, hi)
+        _, ah = nearest(bank(7, 32, 128), dl, 96, "h")
         ts(S("sh", "y6", 6), ah, 2048.0, O.add)
         s2o(S("sh", "y6", 6), bank(7, 128, 134), 6)
         cp(U("y6", 6), bank(7, 128, 134))
@@ -552,14 +627,14 @@ def rank_program(g, core, T, topo):
         ri, nx = S("li", "ri", 96), LB("nx")
         tt(ri, A("ry%d" % t), A("vs", 0, 96), O.add)
         ts(ri, ri, 1, O.arith_shift_right)
-        cp(A("res", 0, 96), ri)
-        cp(nx, X(A("res"), U("vL")))
+        cp(A("vs", 0, 96), ri)
+        cp(nx, X(A("vs"), U("vL")))
         return nx
 
-    ind, rt0, rt1 = A("usb", 0, 1024), A("ML", 0, 1024), A("ML", 2064, 3088)
+    ind, rt0, rt1 = A("at", 0, 1024), A("ML", 0, 1024), A("ML", 2064, 3088)
     ts(ind, A("li"), 2048.0, O.is_lt)
     ts(A("ML", 1024, 2048), A("li"), -1.0, O.mult, 2048.0, O.add)
-    d0 = A("usb", 1024, 2048)
+    d0 = A("at", 1024, 2048)
     act(d0, chi, AF.Identity, 0.0, RM(0))
     for k in range(2):
         mm(bank(k), W012, sub(ind, 512 * k, 512 * k + 512))
@@ -569,25 +644,38 @@ def rank_program(g, core, T, topo):
     gath(bank(5, 0, 64), zn, "g16", 0, 1024)
     gath(bank(5, 64, 128), z0, "g16", 0, 1024)
     al, t64, s64 = F("al", 64), F("t64", 64), F("s64", 64)
-    ks = A("big", 0, 3072)
-    ms(A("big", 0, 2048), 0.0)
-    ts(F("c256", 64), c4, 256.0, O.add)
+    ks = A("cx", 0, 3072)
+    fill(A("cx", 0, 2048), 0)
+    ts(A("prod", 1024, 2048), ccl, kc("8", 1, -8), O.is_equal)
+    for k in range(2):
+        c = (512 * k, 512 * k + 512)
+        own = [(DH, sub(chi, *c)), (DL, sub(clo, *c)), (ID, A("prod", 1024 + c[0], 1024 + c[1]))]
+        mms(bank(6), own)
+        ts(A("xm1", *c), bank(6), 1.0, O.add)
+        cp(A("CK", *c), bank(6), "s")
+        mms(bank(7), own + [(DH2, sub(chi, *c)), (DL2, sub(clo, *c)), (zall(2), sub(ind, *c))])
+        act(A("BT", *c), bank(7), AF.Identity, 1.0, coef("64", [(0, 64), (6, 64)]))
     ts(t64, c4, 2048.0, O.add)
     ts(al, bank(5, 0, 64), 0.5, O.is_gt)
     choose(s64, al, bank(4, 0, 64), t64, "s", 64)
     cp(U("s64", 64), s64)
-    cp(X(ks, U("s64", 64)), A("io0"))
+    cp(X(ks, U("s64", 64)), A("xm1", 0, 1024))
     cp(U("n64", 64), bank(5, 0, 64))
     ts(s64, bank(5, 64, 128), -2049.0, O.add)
     tt(s64, s64, al, O.mult)
     ts(U("e64", 64), s64, 2048.0, O.add)
-    ts(A("m0"), A("big", 0, 2048), 0.0, O.is_equal)
-    scan(A("g16"), A("m0"), A("big", 0, 2048), O.mult, O.add)
-    gath(bank(4, 384, 512), z0, "g16", 0, 2048)
-    ts(CPF, bank(4, 384, 512), -1.0, O.add)
-    ts(CP, bank(4, 384, 512), -1.0, O.add)
+    ts(A("m0"), A("cx", 0, 2048), 0.0, O.is_equal)
+    scan(A("sq"), A("m0"), A("cx", 0, 2048), O.mult, O.add)
+    gath(bank(4, 384, 512), zc, "sq", 0, 2048)
+    ts(CP, bank(4, 384, 512), -17.0, O.add)
+    ts(CPF, bank(4, 384, 512), 4096.0 - 17.0, O.add)
     scan(A("a1"), A("m0"), A("m0"), O.mult, O.add)
     ts(A("oh"), A("a1"), kcol, O.is_equal)
+    ts(A("sel"), A("oh"), 2.0 ** 30, O.mult, -65536.0, O.add)
+    for k in range(4):
+        c = (512 * (k % 2), 512 * (k % 2) + 512)
+        mms(bank(7), [(DH2, sub(chi, *c)), (DL2, sub(clo, *c))])
+        act(ch("xmb", k), bank(7), AF.Identity, 1.0, coef("p%d" % k, [(0, 64 * (k // 2))]))
     PO = U("po", 128)
     for k in range(4):
         tt(ch("px", k), X(A("ML", 1024, 2048), chunks(CP, k, 4)), ch("oh", k), O.mult)
@@ -596,25 +684,16 @@ def rank_program(g, core, T, topo):
         cp(ch("xs", k), X(A("xa", 0, 2048), chunks(PO, k, 4)), "s")
     tt(rt1, X(NB, U("n64", 64)), rt0, O.add)
     ms(A("big", 2048, 2064), 0.0)
-    segscan(sc, [(BK, "xs"), (I23, "oh"), (BBN, "px")], (0, 1))
-    ts(A("KT", 0, 1024), X(sc, U("e64", 64)), kkt, O.add)
+    segscan(sc, [(I23, "oh"), (DK, "oh"), (BBN, "px"), (BK, "xs")], (0, 1))
+    cp(A("KT", 0, 1024), X(sc, U("e64", 64)))
     segscan(A("usa"), [(zneg(3), "xs"), (z256(3), "oh")], (0, 1))
     tt(A("RT", 1024, 2048), X(A("usa"), U("e64", 64)), rt1, O.add)
     scan(A("usa", 0, 2048), A("m0"), A("xs", 0, 2048), O.mult, O.max)
     cp(A("UT", 1024, 2048), X(A("usa"), U("e64", 64)), "s")
     for k in range(2):
-        cp(X(A("pw"), chunks(PO, k, 2)), A("io%d" % k))
-    act(A("g16"), A("pw"), AF.Copy)
-    gath(bank(2, 0, 128), z0, "g16", 0, 2048)
-    ts(POS, bank(2, 0, 128), -1.0, O.add)
-    ts(A("cd", 1024, 2048), ccl, kc("8", 1, -8), O.is_equal)
-    for k in range(2):
-        c = (512 * k, 512 * k + 512)
-        own = [(DH, sub(chi, *c)), (DL, sub(clo, *c)), (ID, A("cd", 1024 + c[0], 1024 + c[1]))]
-        mms(bank(6), own)
-        cp(A("CK", *c), bank(6), "s")
-        mms(bank(7), own + [(DH2, sub(chi, *c)), (DL2, sub(clo, *c)), (zall(2), sub(ind, *c))])
-        act(A("BT", *c), bank(7), AF.Identity, 1.0, coef("64", [(0, 64), (6, 64)]))
+        cp(X(A("pt"), chunks(PO, k, 2)), ch("xmb", k, 1024))
+    gath(bank(2, 0, 128), zown, "pt", 0, 2048)
+    cp(POS, bank(2, 0, 128))
     lb0 = LB("lb0")
     mms(bank(6, 0, 256), [(DH2, sub(chi, 0, 256)), (DL2, sub(clo, 0, 256))])
     cp(lb0, bank(6, 0, 256), "s")
@@ -628,7 +707,8 @@ def rank_program(g, core, T, topo):
         NA, NL = 2064 + 256 * t, 768 - 256 * t
         q = T.cores[(rank + 1 + t % 7) % 8]
         h = T.cores[(rank - 1 - t % 7) % 8]
-        gath(bank(4, 0, 16), zown, "BT", cl, 256, 4)
+        vtr(LB("ek"), A("BT", *lanes))
+        lin(bank(4, 0, 16), LB("ek"), [(0, 16), (1, 1)])
         LP = U("lp")
         ts(LP, bank(4, 0, 16), -1024.0, O.add)
         kt, mlc, rtc, uc, uv = LF("kt"), LH("mlc"), LH("rtc"), LB("uc"), LB("uv")
@@ -636,8 +716,9 @@ def rank_program(g, core, T, topo):
         cp(rtc, X(A("RT", 1024, NA), LP), "s")
         cp(mlc, X(A("ML", 1024, NA), LP), "s")
         cp(uc, X(A("UT", 1024, NA), LP), "s")
-        gath(bank(4, 32, 48), zst, "lh", rtc[1], 256)
-        gath(bank(4, 16, 32), z0, "lh", rtc[1], 256)
+        vtr(LH("comb"), rtc)
+        lin(bank(4, 32, 48), LH("comb"), [(0, 1), (1, -1)])
+        lin(bank(4, 16, 32), LH("comb"), [(0, 1)])
         ta, tb = best(kt, 256, "s", "mr", O.mult, O.max)
         ki, k4 = S("si", "ki"), S("si", "k4", 64)
         cp(ki, sub(tb, 15, 256, 16))
@@ -659,14 +740,14 @@ def rank_program(g, core, T, topo):
         ts(lval, sub(k4, 48, 64), 15.5, O.is_gt)
         sp = F("sp")
         tt(sp, st15, sg, O.subtract)
-        if t == 0:
-            ts(F("l2048"), lane, 2048.0, O.add)
-            ts(F("l2064"), lane, 2064.0, O.add)
-            ts(F("l96"), lane, 96.0, O.add)
-            ts(F("l1280"), lane, 1280.0, O.add)
-            ts(F("l1536"), lane, 1536.0, O.add)
-        choose(sp, live, sp, F("l2048"), "sp")
+        dead = F("dead")
+        ts(dead, mS, 15.5, O.is_lt, 4096.0, O.mult)
+        tt(sp, sp, dead, O.add)
+        tt(sp, sp, l2048, O.min)
         cp(U("sp"), sp)
+        tt(dead, dead, sf, O.add)
+        tt(dead, dead, l2064, O.min)
+        cp(U("vA%d" % (t % 2)), dead)
         xsb, xbb = LB("xsb"), LB("xbb")
         cp(xsb, X(A("xs"), U("sp")))
         cp(A("acq"), X(A("act"), U("hU")))
@@ -674,13 +755,15 @@ def rank_program(g, core, T, topo):
         for k in range(4):
             tt(ch("df", k), X(A("XL"), chunks(CP, k, 4)), ch("xs", k), O.subtract)
             act(ch("sq", k), ch("df", k), AF.Square)
-        segscan(sc, [(I17, "oh"), (BB16, "sq")], (0, 1))
+        byslot(sc)
         dsl, dbl, kb = LF("dsl"), LF("dbl"), LF("kb")
-        ts(dsl, X(sc, EU), k15, O.add)
-        tt(kb, dsl, kt, O.min)
+        ts(dsl, X(sc, EU), kneg, O.add)
+        mms(bank(0, 0, 256), [(N16, rtc), (K16, ones)])
+        tt(kb, bank(0, 0, 256), dsl, O.add)
+        tt(kb, kb, kt, O.min)
         _, bb = best(kb, 256, "b", "mr", O.mult, O.max)
         kj = S("si", "kj")
-        cp(kj, sub(bb, 15, 256, 16))
+        ts(kj, sub(bb, 15, 256, 16), 15.0, O.add)
         ts(kj, kj, 15, O.bitwise_and)
         cp(S("sh", "kj"), kj)
         s2o(S("sh", "kj"), bank(4, 112, 128), 16)
@@ -691,25 +774,23 @@ def rank_program(g, core, T, topo):
         for k in range(4):
             tt(ch("df", k), X(A("XB"), chunks(CP, k, 4)), ch("xs", k), O.subtract)
             act(ch("sq", k), ch("df", k), AF.Square)
-        segscan(sc2, [(I17, "oh"), (BB16, "sq")], (0, 1))
-        ts(dbl, X(sub(sc2, 0, 2048), EU), k15, O.add)
+        byslot(sc2)
         here, away = LB("here"), LB("away")
-        ts(here, kt, 524287.5, O.is_gt)
-        tt(away, dbl, dsl, O.is_lt)
+        act(here, kt, AF.Sign)
+        tt(away, X(sub(sc2, 0, 2048), EU), dsl, O.is_lt)
         tt(away, away, here, O.mult)
         mms(bank(0, 0, 256), [(Q1, here), (TW, away)])
         mms(bank(0, 256, 512), [(Q2, here), (TW2, away)])
         tq = LB("tq")
         tt(tq, bank(0, 256, 512), away, O.mult)
         if t:
-            ms(A("TAU", cl - 1, 1024, 4), 64.0)
+            ts(A("TAU", cl - 1, 1024, 4), zero, 0.25, O.add)
         tt(A("TAU", *lanes), bank(0, 0, 256), tq, O.add)
         mm(bank(1, 0, 256), BB, away)
         mms(bank(1, 256, 512), [(NREP, rtc), (BBN, away)])
-        nlr, mka, mks = LB("nlr"), LH("mka"), LH("mks")
+        nlr, mks = LB("nlr"), LH("mks")
         cp(nlr, bank(1, 0, 256), "s")
         ts(mks, bank(1, 256, 512), kcol, O.is_gt)
-        ts(mka, nlr, kcol, O.is_gt)
         xn = A("xm%d" % (t % 2))
         for k in range(4):
             tt(ch("prod", k), X(A("TAU"), chunks(CP, k, 4)), ch("oh", k), O.mult)
@@ -718,21 +799,19 @@ def rank_program(g, core, T, topo):
             if not last:
                 tt(sub(xn, 512 * k, 512 * k + 512), bank(k % 2), sub(xm, 512 * k, 512 * k + 512), O.min)
             act(ch("pen", k), ch("a1", k), AF.Abs, 1.0, kab)
-        gath(bank(4, 256, 384), zall, "prod", 0, 2048)
-        aw, cv = F("aw", 128), F("cv", 128)
-        ts(aw, bank(4, 256, 384), 0.0, O.is_gt)
-        ts(cv, bank(4, 256, 384), 32.0, O.is_lt)
-        tt(aw, aw, cv, O.mult)
-        ts(cv, CPF, -0.75, O.mult, 1024.0 - cl / 4.0, O.add)
-        tt(cv, cv, aw, O.mult)
-        tt(cv, cv, CPF, O.add)
-        cp(IX, cv)
+        if not last:
+            gath(bank(4, 256, 384), zbig, "prod", 0, 2048)
+            cv = F("cv", 128)
+            ts(cv, CPF, 0.25, O.mult, 4096.0 - cl / 4.0, O.add)
+            tt(cv, bank(4, 256, 384), cv, O.min)
+            tt(cv, cv, CPF, O.max)
+            ts(IX, cv, -4096.0, O.add)
         segscan(sc, [(BB, "px"), (IPN, "pen")], (0, 1))
         comb, stay, dif = LH("comb"), LH("stay"), LH("dif")
         cp(comb, X(sc, EU), "s")
-        mm(bank(0, 0, 256), REV, comb)
-        tt(A("ML", NA, NA + 256), bank(0, 0, 256), mka, O.mult)
         tt(stay, comb, mks, O.mult)
+        mms(bank(0, 0, 256), [(REV, comb), (REVN, stay)])
+        cp(A("ML", NA, NA + 256), bank(0, 0, 256))
         tt(dif, mlc, stay, O.subtract)
         if not last:
             for k in range(4):
@@ -769,25 +848,30 @@ def rank_program(g, core, T, topo):
             mms(bank(1, 0, 256), [(ID, nb), (D01, rtc), (z0(2), nlr), (z0(3), sub(m2a, 256, 512))])
             cp(A("RT", NA, NA + 256), bank(1, 0, 256), "s")
         for k in range(4):
-            mms(bank(2 + k % 2), [(ID, ch("xa", k)), (CLS[cl], ch("at", k))])
+            mm(bank(2 + k % 2), CLS[cl], ch("at", k))
             act(ch("xc", k), bank(2 + k % 2), AF.Copy)
+            if k % 2:
+                c = (512 * k - 512, 512 * k + 512)
+                dma("g", A("xc", *c), A("xa", *c), T["xc"][:, c[0]:c[1]], T["xa"][:, c[0]:c[1]], True)
         if t:
             nx = answer(t - 1, T.cores[(rank + t) % 8])
-            cp(X(A("xc"), U("vA")), nx)
-            cp(X(A("xa"), U("vA")), nx)
+            cp(X(A("xc"), U("vA%d" % (1 - t % 2))), nx)
+            cp(X(A("xa"), U("vA%d" % (1 - t % 2))), nx)
             tt(A("UT", NL + 256, NL + 512), LB("u4"), nx, O.max)
             mms(bank(5, 0, 256), [(zneg(3), nx), (Z16(3), ones)])
             tt(A("RT", NL + 256, NL + 512), bank(5, 0, 256), LH("r1"), O.max)
-        pay = LF("pay", 512)
-        payload(pay, A("acq"), 256, "c")
+        hi, dl = payload(A("acq"), 256, "c", bank(3, 0, 256))
         for i in range(16):
-            asel(A("cx", i, 4096, 16), xsb, [[0, 256]], O.is_ge, 0, 0)
-        for k in range(4):
-            z = k % 2
-            tt(ch("cd", z, 1024), X(A("xc", 0, 2048), A("acq", 64 * k, 64 * k + 64)), ch("cx", k, 1024), O.subtract)
-            act(ch("cd", z, 1024), ch("cd", z, 1024), AF.Square)
-            gath(bank(3, 64 * k, 64 * k + 64), zall, "cd", 1024 * z, 1024)
-        key, ah = nearest(bank(3, 0, 256), pay, 256, "c")
+            if t or i % 2:
+                asel(A("cx", i, 4096, 16), xsb, [[0, 256]], O.is_ge, 0, 0)
+            else:
+                cp(A("cx", i, 4096, 16), xsb)
+        for k in range(8):
+            tt(ch("cx", k), X(A("xc", 0, 2048), A("acq", 32 * k, 32 * k + 32)), ch("cx", k), O.subtract)
+            act(ch("cx", k), ch("cx", k), AF.Square)
+            if k % 2:
+                sums(bank(3, 32 * k - 32, 32 * k + 32), "cx", 512 * k - 512, sub(hi, 32 * k - 32, 32 * k + 32))
+        key, ah = nearest(bank(3, 0, 256), dl, 256, "c")
         ts(F("fit"), key, 4096.0, O.is_lt)
         tt(F("fit"), F("fit"), lval, O.mult)
         tt(ah, ah, F("fit"), O.mult)
@@ -796,14 +880,16 @@ def rank_program(g, core, T, topo):
         cp(U("aU"), bank(2, 0, 16))
         ag = LB("ag")
         cp(ag, X(A("at", 0, 2049), U("aU")))
-        gath(bank(2, 16, 32), zp, "lb", ag[1], 256)
+        vtr(LB("agt"), ag)
+        lin(bank(2, 16, 32), LB("agt"), [(6, 16), (7, 1)])
         DP, plo = U("dp"), NL + 256
         ts(DP, bank(2, 16, 32), float(-plo), O.add)
         mm(bank(5, 0, 256), CREP, ag)
         drep = LH("drep")
         cp(drep, bank(5, 0, 256), "s")
-        gath(bank(3, 256, 272), zc, "lb", ag[1], 256)
-        df_ = F("d")
+        lin(bank(3, 256, 272), LB("agt"), [(4, 16), (5, 1)])
+        de32, no32 = F("de32", 32), F("no32", 32)
+        df_ = sub(de32, 0, 16)
         cp(df_, bank(3, 256, 272))
         ud, rtd, y = LB("ud"), LH("rtd"), LH("y")
         cp(ud, X(A("UT", plo, NA), DP))
@@ -821,11 +907,15 @@ def rank_program(g, core, T, topo):
             ts(thr, F("c_01", 1), zi, O.mult, thr0, O.add)
         mms(bank(2, 256, 512), [(W01, uv), (WC, rtc), (WD, rtd)])
         ok1, ok2 = LB("ok1"), LB("ok2")
-        ts(ok1, bank(2, 256, 512), thr if t else thr0, O.is_le)
-        ts(ok2, bank(5, 0, 256), 0.5, O.is_lt)
-        tt(ok1, ok1, ok2, O.mult)
+        act(ok1, bank(2, 256, 512), AF.Sign, -1.0, thr if t else thr0)
+        act(ok2, bank(5, 0, 256), AF.Sign, -1.0, 0.5)
+        tt(ok1, ok1, ok2, O.min)
         gath(bank(2, 32, 48), zall, "lb", ok1[1], 256)
         ecnt = empties()
+        le, de = LB("le"), LB("de", 512)
+        mms(bank(6, 0, 256), [(ID, lb0), (ID, A("CK", *lanes)), (zn(2), rtc)])
+        ts(le, bank(6, 0, 256), coef("nl%d" % t, [(0, NL // 16), (6, NL // 16)]), O.add)
+        ts(sub(de, 0, 256), le, hi4, O.mult, cde, O.add)
         y1 = LH("y1")
         for b in range(4):
             mm(bank(6, 0, 256), BIT[b], rtc)
@@ -833,62 +923,57 @@ def rank_program(g, core, T, topo):
             mms(bank(6, 256, 512), [(ID, y), (SH[b], y1)])
             cp(y, bank(6, 256, 512), "s")
         gath(bank(3, 272, 288), zall, "lb", uc[1], 256)
-        want0, mer, want, spl, wk = F("want0"), F("mer"), F("want"), F("spl"), F("wk")
+        want0, spl, wk = F("want0"), F("spl"), F("wk")
         tt(want0, bank(3, 272, 288), mS, O.add)
         ts(want0, want0, lim2, O.is_gt)
         tt(want0, want0, live, O.mult)
         dec = S("sb", "dec", 32)
-        ts(mer, bank(2, 32, 48), 15.5, O.is_gt)
         ts(tmp, bank(2, 32, 48), 15.5, O.is_lt)
         wb = S("sb", "wb")
         tt(wb, want0, tmp, O.mult)
+        ts(sub(dec, 0, 16), tmp, -1.0, O.mult, 1.0, O.add)
+        ts(sub(no32, 0, 16), tmp, 2048.0, O.mult)
         prefix(wb, 16, wk, "pw", bank(2, 48, 80))
         ts(spl, wk, ecnt, O.is_lt)
         tt(spl, spl, wb, O.mult)
         cp(U("kU"), wk)
-        idle, visit, vk = S("sb", "idle"), F("visit"), F("vk")
+        idle, vk, busy = S("sb", "idle"), F("vk"), F("busy")
         tt(tmp, tmp, live, O.mult)
         tt(idle, tmp, spl, O.subtract)
         prefix(idle, 16, vk, "pv", bank(2, 80, 112))
-        ts(visit, vk, 95.5, O.is_lt)
-        tt(visit, visit, idle, O.mult)
-        choose(F("vl"), visit, vk, F("l96"), "vl")
-        cp(U("vL"), F("vl"))
+        ts(busy, idle, -1000.0, O.mult, 1000.0, O.add)
+        tt(vk, vk, busy, O.add)
+        tt(vk, vk, l256, O.min)
+        cp(U("vL"), vk)
         cp(X(A("vs"), U("vL")), xsb)
         send(q, "in%d" % t, A("vs", 0, 96), "ra%d" % t, "la%d" % t)
-        choose(F("va"), visit, sf, F("l2064"), "va")
-        cp(U("vA"), F("va"))
-        cp(A("res", 96, 352), xsb)
-        cp(sub(dec, 0, 16), mer)
         ts(sub(dec, 16, 32), spl, -1.0, O.mult, 1.0, O.add)
         rows(bank(3), dec)
         mr_, ns_ = bank(3, 0, 256), bank(3, 256, 512)
         eg = LB("eg")
-        cp(eg, X(A("el", 0, 256), U("kU")), "s")
-        gath(bank(2, 112, 128), zc, "lb", eg[1], 256)
+        cp(eg, X(A("el"), U("kU")), "s")
+        vtr(LB("agt"), eg)
+        lin(bank(2, 112, 128), LB("agt"), [(4, 16), (5, 1)])
         DE = U("de", 32)
-        choose(F("dl"), mer, df_, F("l1280"), "dl")
-        cp(sub(DE, 0, 16), F("dl"))
-        choose(F("elst"), spl, bank(2, 112, 128), F("l1536"), "el")
-        cp(sub(DE, 16, 32), F("elst"))
-        le, de, lb2, sd = LB("le"), LB("de", 512), LB("lb2"), LB("sd")
-        ts(le, lb0, coef("nl%d" % t, [(0, NL // 16), (6, NL // 16)]), O.add)
-        tt(le, le, A("CK", *lanes), O.add)
-        ts(sub(de, 0, 256), le, hi4, O.mult, cde, O.add)
-        ts(lb2, lb0, coef("na%d" % t, [(0, NA // 16), (6, NA // 16), (2, 1)]), O.add)
-        mm(bank(5, 256, 512), zn(2), rtc)
-        tt(A("BT", *lanes), bank(5, 256, 512), le, O.add)
-        ee = sub(de, 256, 512)
-        tt(ee, lb2, eg, O.add)
+        cp(sub(de32, 16, 32), bank(2, 112, 128))
+        ts(sub(no32, 16, 32), spl, -2048.0, O.mult, 2048.0, O.add)
+        tt(no32, no32, de32, O.add)
+        tt(no32, no32, l32, O.min)
+        cp(DE, no32)
+        ee, sd = sub(de, 256, 512), LB("sd")
+        mms(bank(5, 256, 512), [(ID, lb0), (ID, eg)])
+        ts(ee, bank(5, 256, 512), coef("na%d" % t, [(0, NA // 16), (6, NA // 16), (2, 1)]), O.add)
+        cp(A("BT", *lanes), le)
         tt(sd, le, ee, O.subtract)
         tt(sd, ns_, sd, O.mult)
         tt(A("BT", 1024, 1280), sd, ee, O.add)
         cp(X(A("BT"), DE), de)
-        agents(IX, 1280, last)
+        if not last:
+            agents(IX, 1280, last)
         tt(dif, ns_, dif, O.mult)
         tt(y1, mr_, y, O.mult)
-        tt(dif, dif, stay, O.add)
-        tt(A("ML", NL, NL + 256), dif, y1, O.add)
+        mms(bank(6, 0, 256), [(ID, stay), (ID, dif), (ID, y1)])
+        cp(A("ML", NL, NL + 256), bank(6, 0, 256))
         if not last:
             u1, u2, u4, p1, n1 = LB("u1"), LB("u2"), LB("u4"), LH("p1"), LB("n1")
             tt(u1, ns_, ua, O.mult)
@@ -911,6 +996,6 @@ def rank_program(g, core, T, topo):
     ts(A("RT", 0, 1024), X(A("ML"), U("l64", 64)), -1.0, O.mult, 2048.0, O.add)
     dma("y", None, A("RT", 0, 1024), T.ym[:, 0:1024], T["RT"][:, 0:1024])
     nx = answer(3, T.cores[(rank + 4) % 8])
-    cp(X(A("xa"), U("vA")), nx)
+    cp(X(A("xa"), U("vA1")), nx)
     dma("y", None, A("xa", 0, 2048), T.yx[:, 0:2048], T["xa"][:, 0:2048])
     issue()

@@ -7,14 +7,14 @@ for _n, _w, _d in [
         ("act", 1024, I4), ("xa", 2320, B2), ("xc", 2320, B2), ("xs", 2304, B2), ("xm0", 2048, B2), ("xm1", 2048, B2), ("xmb", 2304, B2),
         ("usa", 2064, B2), ("atp", 2048, B2), ("oh", 2048, B2), ("sel", 2048, B2), ("m0", 2048, B2), ("df", 2048, B2), ("sq", 2048, B2),
         ("prod", 2048, B2), ("cx", 4096, B2), ("pt", 2048, B2), ("hx", 1536, B2), ("at", 2064, B2),
-        ("XL", 1024, B2), ("TAU", 1024, B2), ("CK", 1024, B2), ("el", 256, B2), ("eq", 1024, B2),
+        ("XL", 1024, B2), ("TAU", 1024, B2), ("CK", 1024, B2), ("el", 256, B2),
         ("px", 2048, H2), ("mr", 256, B2), ("mrb", 512, B2), ("ones", 256, B2), ("orp", 2048, B2),
-        ("wm", 7680, B2), ("zs", 2448, B2), ("lb", 9152, B2), ("lh", 3808, H2), ("lf", 3456, F4), ("li", 1024, I4), ("acq", 256, U2),
+        ("wm", 7040, B2), ("zs", 2448, B2), ("lb", 9408, B2), ("lh", 3808, H2), ("lf", 3456, F4), ("li", 1024, I4), ("acq", 256, U2),
         ("vs", 512, B2), ("yv", 96, B2),
-        ("sm", 2560, F4), ("si", 288, I4), ("su", 1200, U2), ("sh", 144, H2), ("sb", 320, B2), ("lim", 2, I4), ("wtc", 1, I4)]:
+        ("sm", 2560, F4), ("si", 400, I4), ("su", 1200, U2), ("sh", 144, H2), ("sb", 416, B2), ("lim", 2, I4), ("wtc", 1, I4)]:
     SCRATCH[_n] = ("sbuf", [128, _w], _d)
 ALIAS = {"a1": ("df", 0, 2048), "pen": ("sq", 0, 2048), "XB": ("XL", 0, 1024), "g16": ("lh", 0, 2048),
-         "hd": ("hx", 0, 1536), "usb": ("df", 0, 2048)}
+         "hd": ("hx", 0, 1536), "usb": ("df", 0, 2048), "eq": ("cx", 0, 4096)}
 for _t in range(4):
     SCRATCH["in%d" % _t] = ("sbuf", [128, 96], B2)
     SCRATCH["ry%d" % _t] = ("sbuf", [128, 96], B2)
@@ -24,9 +24,10 @@ SEMAPHORES = ["sv", "ss", "st", "sg"] + ["d%d" % i for i in range(16)]
 for _t in range(4):
     SEMAPHORES += ["ra%d" % _t, "rb%d" % _t, "la%d" % _t, "lb%d" % _t]
 BIG = 33554432.0
+ENG = 8
 PLAN, PASSES = {}, 6
-BEHIND = 800
-HOP, SLACK, DMA, LINK = 60, 100, 2500, 4000
+BEHIND = 400
+HOP, SLACK, DMA, LINK = 100, 100, 2500, 4000
 
 
 def rank_program(g, core, T, topo):
@@ -216,6 +217,13 @@ def rank_program(g, core, T, topo):
             alt = either(out, a, AF.Identity, s1, s2) if (op0, op1) == (O.mult, O.add) else None
             emit("v", lambda: g.vector.tensor_scalar(ap(out), ap(a), ap(s1), ap(s2), op0, op1), [out], [a, s1, s2], alt=alt)
 
+    def gt(out, x, b, op, k):
+        if k % 2:
+            act(out, x, AF.Copy)
+            tt(out, out, b, op)
+        else:
+            tt(out, x, b, op)
+
     def scan(out, d0, d1, op0, op1, init=0.0):
         emit("v", lambda: g.vector.tensor_tensor_scan(ap(out), ap(d0), ap(d1), ap(init), op0, op1), [out], [d0, d1, init])
 
@@ -356,10 +364,9 @@ def rank_program(g, core, T, topo):
         return m
 
     cE = RM(0)
-    zall, zneg, z256 = zset("all", 1.0), zset("neg", -1.0), zset("256", 256.0)
+    zall, zneg = zset("all", 1.0), zset("neg", -1.0)
     z0, z0n, zn, zms = zset("0", RM(0)), zset("0n", coef("0n", [(0, -1)])), zset("n", RM(2)), zset("ms", RM(3))
-    zst = zset("st", coef("st", [(0, 1), (1, -1)]))
-    zown, zc, zp = zset("own", coef("own", [(0, 16), (1, 1)])), zset("c", coef("c", [(4, 16), (5, 1)])), zset("p", coef("p", [(6, 16), (7, 1)]))
+    zown, zc = zset("own", coef("own", [(0, 16), (1, 1)])), zset("c", coef("c", [(4, 16), (5, 1)]))
     znn = zset("nn", coef("nn", [(2, -1)]))
     wf = F("wf", 1)
     cp(wf, A("wtc"))
@@ -374,11 +381,10 @@ def rank_program(g, core, T, topo):
     cp(W01, W012)
     tt(W012, W012, zall(2), O.add)
     PE_, PO_, P01, P10 = mk("PE", ID, mE), mk("PO", ID, mO), mk("P01", SP, mE), mk("P10", SN, mO)
-    BB16, BBN, B64, B64N, BK = mk("BB16", BB, 16.0), mk("BBN", BB, -1.0), mk("B64", BB, 64.0), mk("B64N", BB, -64.0), mk("BK", BB, -32768.0)
-    N16, K16 = mk("N16", BB, RM(1), 65536.0), mk("K16", ID, kc("k16", -65536, 65536))
+    BB16, BBN, B64, BK = mk("BB16", BB, 16.0), mk("BBN", BB, -1.0), mk("B64", BB, 64.0), mk("BK", BB, -32768.0)
+    N16, K16 = mk("N16", BB, RM(1), 65536.0), mk("K16", ID, kc("k16", -65536, 65536 * 33))
     I23, IPN = mk("I23", ID, 8388608.0), mk("IPN", ID, -16384.0)
     NREP, CREP = mk("NREP", BB, RM(2)), mk("CREP", BB, F("c_c", 1))
-    BIT = [mk("BIT%d" % b, BB, RM(4 + b)) for b in range(4)]
     CLS = [mk("CLS%d" % m, BB, RM(8 + m), 64.0) for m in range(4)]
     D01 = mk("D01", ID, coef("01", [(0, 1), (1, 1)]))
     DH, DL, DH2, DL2 = mk("DH", ID, RM(4)), mk("DL", ID, RM(5)), mk("DH2", ID, coef("06", [(0, 1), (6, 1)])), mk("DL2", ID, coef("17", [(1, 1), (7, 1)]))
@@ -397,7 +403,6 @@ def rank_program(g, core, T, topo):
     ts(c4, F("c64", 64), kcol, O.add)
     lane = sub(c4, 0, 16)
     kneg, kab, k128 = kc("neg", -1, 0), kc("ab", -1, -0.5), kc("128", 128, 0)
-    DK = mk("DK", ID, kc("kt", -2048, 16 * 2048))
     fill(A("mr"), 1)
     fill(A("mr", 0, 256, 16), 0)
     fill(A("mrb"), 0)
@@ -428,8 +433,9 @@ def rank_program(g, core, T, topo):
         TS[w] = [mk("%s%d" % (n, w + 1), m, float(w)) for n, m in zip("abcd", TS[1])]
     dg = LB("dg")
     ts(dg, sub(clo, 0, 256), kcol, O.is_lt, -64.0, O.mult)
-    NB, nbi = S("sb", "NB", 32), S("si", "nbi", 32)
-    ts(nbi, sub(F("i144", 144), 0, 32), coef("pw", [(4, 1), (5, 0.5), (6, 0.25), (7, 0.125)]), O.mult, -0.4375, O.add)
+    NB, nbi = S("sb", "NB", 128), S("si", "nbi", 128)
+    for b in range(4):
+        ts(sub(nbi, 32 * b, 32 * b + 32), sub(F("i144", 144), 0, 32), 0.5 ** b, O.mult, -0.4375, O.add)
     ts(nbi, nbi, 1, O.bitwise_and)
     cp(NB, nbi)
     lims = F("lims", 2)
@@ -532,7 +538,7 @@ def rank_program(g, core, T, topo):
 
     def send(dst, out, src, rs, ls):
         rid, pid, _ = topo.addr(dst)
-        es = topo.engines(core, dst)[:4]
+        es = topo.engines(core, dst)[:ENG]
         m = 0
         for e in es:
             m |= 1 << e
@@ -540,7 +546,7 @@ def rank_program(g, core, T, topo):
                                                   dma_engine_mask=m), [], [src], sem=ls, inc=len(es), busy=300, lat=LINK)
 
     def arrived(buf, rs, src):
-        emit("a", None, [A(buf)], [], sem=rs, inc=len(topo.engines(src, core)[:4]), busy=0, after=[sent[rs]])
+        emit("a", None, [A(buf)], [], sem=rs, inc=len(topo.engines(src, core)[:ENG]), busy=0, after=[sent[rs]])
 
     def payload(lst, n, tag, ps):
         idf, hi, dl = LH("id" + tag, n), LH("hi" + tag, n), LB("dl" + tag, n)
@@ -631,7 +637,7 @@ def rank_program(g, core, T, topo):
         cp(nx, X(A("vs"), U("vL")))
         return nx
 
-    ind, rt0, rt1 = A("at", 0, 1024), A("ML", 0, 1024), A("ML", 2064, 3088)
+    ind, rt0 = A("at", 0, 1024), A("g16", 0, 1024)
     ts(ind, A("li"), 2048.0, O.is_lt)
     ts(A("ML", 1024, 2048), A("li"), -1.0, O.mult, 2048.0, O.add)
     d0 = A("at", 1024, 2048)
@@ -639,28 +645,29 @@ def rank_program(g, core, T, topo):
     for k in range(2):
         mm(bank(k), W012, sub(ind, 512 * k, 512 * k + 512))
     scan(rt0, d0, A("psA", 0, 1024), O.mult, O.add)
-    cp(A("g16", 0, 1024), rt0)
-    gath(bank(4, 0, 64), zst, "g16", 0, 1024)
-    gath(bank(5, 0, 64), zn, "g16", 0, 1024)
-    gath(bank(5, 64, 128), z0, "g16", 0, 1024)
+    vtr(A("g16", 1024, 2048), rt0)
+    lin(bank(4, 0, 64), A("g16", 1024, 2048), [(0, 1), (1, -1)])
+    lin(bank(5, 0, 64), A("g16", 1024, 2048), [(2, 1)])
+    lin(bank(5, 64, 128), A("g16", 1024, 2048), [(0, 1)])
     al, t64, s64 = F("al", 64), F("t64", 64), F("s64", 64)
     ks = A("cx", 0, 3072)
     fill(A("cx", 0, 2048), 0)
     ts(A("prod", 1024, 2048), ccl, kc("8", 1, -8), O.is_equal)
     for k in range(2):
         c = (512 * k, 512 * k + 512)
-        own = [(DH, sub(chi, *c)), (DL, sub(clo, *c)), (ID, A("prod", 1024 + c[0], 1024 + c[1]))]
-        mms(bank(6), own)
+        mms(bank(6), [(DH, sub(chi, *c)), (DL, sub(clo, *c)), (ID, A("prod", 1024 + c[0], 1024 + c[1]))])
         ts(A("xm1", *c), bank(6), 1.0, O.add)
         cp(A("CK", *c), bank(6), "s")
-        mms(bank(7), own + [(DH2, sub(chi, *c)), (DL2, sub(clo, *c)), (zall(2), sub(ind, *c))])
-        act(A("BT", *c), bank(7), AF.Identity, 1.0, coef("64", [(0, 64), (6, 64)]))
+        mms(bank(7), [(DH2, sub(chi, *c)), (DL2, sub(clo, *c))])
+        cp(A("xmb", *c), bank(7))
+        ts(A("xmb", 1024 + c[0], 1024 + c[1]), bank(7), coef("64", [(0, 64), (6, 64)]), O.add)
+        mms(bank(7), [(ID, A("CK", *c)), (ID, A("xmb", 1024 + c[0], 1024 + c[1])), (zall(2), sub(ind, *c))])
+        cp(A("BT", *c), bank(7))
     ts(t64, c4, 2048.0, O.add)
     ts(al, bank(5, 0, 64), 0.5, O.is_gt)
     choose(s64, al, bank(4, 0, 64), t64, "s", 64)
     cp(U("s64", 64), s64)
     cp(X(ks, U("s64", 64)), A("xm1", 0, 1024))
-    cp(U("n64", 64), bank(5, 0, 64))
     ts(s64, bank(5, 64, 128), -2049.0, O.add)
     tt(s64, s64, al, O.mult)
     ts(U("e64", 64), s64, 2048.0, O.add)
@@ -672,22 +679,19 @@ def rank_program(g, core, T, topo):
     scan(A("a1"), A("m0"), A("m0"), O.mult, O.add)
     ts(A("oh"), A("a1"), kcol, O.is_equal)
     ts(A("sel"), A("oh"), 2.0 ** 30, O.mult, -65536.0, O.add)
-    for k in range(4):
-        c = (512 * (k % 2), 512 * (k % 2) + 512)
-        mms(bank(7), [(DH2, sub(chi, *c)), (DL2, sub(clo, *c))])
-        act(ch("xmb", k), bank(7), AF.Identity, 1.0, coef("p%d" % k, [(0, 64 * (k // 2))]))
     PO = U("po", 128)
     for k in range(4):
         tt(ch("px", k), X(A("ML", 1024, 2048), chunks(CP, k, 4)), ch("oh", k), O.mult)
         gath(bank(2 + k % 2, 0, 32), zneg, "px", 512 * k, 512)
         ts(chunks(PO, k, 4), bank(2 + k % 2, 0, 32), 2048.0, O.add)
         cp(ch("xs", k), X(A("xa", 0, 2048), chunks(PO, k, 4)), "s")
-    tt(rt1, X(NB, U("n64", 64)), rt0, O.add)
     ms(A("big", 2048, 2064), 0.0)
-    segscan(sc, [(I23, "oh"), (DK, "oh"), (BBN, "px"), (BK, "xs")], (0, 1))
-    cp(A("KT", 0, 1024), X(sc, U("e64", 64)))
-    segscan(A("usa"), [(zneg(3), "xs"), (z256(3), "oh")], (0, 1))
-    tt(A("RT", 1024, 2048), X(A("usa"), U("e64", 64)), rt1, O.add)
+    segscan(sc, [(I23, "oh"), (BBN, "px"), (BK, "xs")], (0, 1))
+    ts(A("KT", 0, 1024), X(sc, U("e64", 64)), kc("kt", -2048, 16 * 2048), O.add)
+    for k in range(4):
+        act(ch("sq", k), ch("xs", k), AF.Identity, -1.0, 16.0)
+    segscan(A("usa"), [(zall(3), "sq")], (2, 3))
+    tt(A("RT", 1024, 2048), X(A("usa"), U("e64", 64)), rt0, O.add)
     scan(A("usa", 0, 2048), A("m0"), A("xs", 0, 2048), O.mult, O.max)
     cp(A("UT", 1024, 2048), X(A("usa"), U("e64", 64)), "s")
     for k in range(2):
@@ -695,10 +699,10 @@ def rank_program(g, core, T, topo):
     gath(bank(2, 0, 128), zown, "pt", 0, 2048)
     cp(POS, bank(2, 0, 128))
     lb0 = LB("lb0")
-    mms(bank(6, 0, 256), [(DH2, sub(chi, 0, 256)), (DL2, sub(clo, 0, 256))])
-    cp(lb0, bank(6, 0, 256), "s")
+    cp(lb0, A("xmb", 0, 256))
     agents(CP, 1024, False)
     xm = A("xs", 0, 2048)
+    act(A("xm1"), xm, AF.Copy, -1.0)
     zi = None
 
     for t in range(4):
@@ -719,6 +723,8 @@ def rank_program(g, core, T, topo):
         vtr(LH("comb"), rtc)
         lin(bank(4, 32, 48), LH("comb"), [(0, 1), (1, -1)])
         lin(bank(4, 16, 32), LH("comb"), [(0, 1)])
+        lin(bank(4, 160, 176), LH("comb"), [(2, 1)])
+        cp(U("nU"), bank(4, 160, 176))
         ta, tb = best(kt, 256, "s", "mr", O.mult, O.max)
         ki, k4 = S("si", "ki"), S("si", "k4", 64)
         cp(ki, sub(tb, 15, 256, 16))
@@ -753,14 +759,16 @@ def rank_program(g, core, T, topo):
         cp(A("acq"), X(A("act"), U("hU")))
         cp(A("XL", *lanes), xsb)
         for k in range(4):
-            tt(ch("df", k), X(A("XL"), chunks(CP, k, 4)), ch("xs", k), O.subtract)
+            gt(ch("df", k), X(A("XL"), chunks(CP, k, 4)), ch("xs", k), O.subtract, k)
             act(ch("sq", k), ch("df", k), AF.Square)
         byslot(sc)
         dsl, dbl, kb = LF("dsl"), LF("dbl"), LF("kb")
         ts(dsl, X(sc, EU), kneg, O.add)
-        mms(bank(0, 0, 256), [(N16, rtc), (K16, ones)])
+        here, away = LB("here"), LB("away")
+        act(here, kt, AF.Relu, 1.0, -262144.0)
+        act(here, here, AF.Sign)
+        mms(bank(0, 0, 256), [(N16, rtc), (K16, here)])
         tt(kb, bank(0, 0, 256), dsl, O.add)
-        tt(kb, kb, kt, O.min)
         _, bb = best(kb, 256, "b", "mr", O.mult, O.max)
         kj = S("si", "kj")
         ts(kj, sub(bb, 15, 256, 16), 15.0, O.add)
@@ -772,11 +780,9 @@ def rank_program(g, core, T, topo):
         cp(xbb, X(A("xs"), U("bp")))
         cp(A("XB", *lanes), xbb)
         for k in range(4):
-            tt(ch("df", k), X(A("XB"), chunks(CP, k, 4)), ch("xs", k), O.subtract)
+            gt(ch("df", k), X(A("XB"), chunks(CP, k, 4)), ch("xs", k), O.subtract, k)
             act(ch("sq", k), ch("df", k), AF.Square)
         byslot(sc2)
-        here, away = LB("here"), LB("away")
-        act(here, kt, AF.Sign)
         tt(away, X(sub(sc2, 0, 2048), EU), dsl, O.is_lt)
         tt(away, away, here, O.mult)
         mms(bank(0, 0, 256), [(Q1, here), (TW, away)])
@@ -791,13 +797,34 @@ def rank_program(g, core, T, topo):
         nlr, mks = LB("nlr"), LH("mks")
         cp(nlr, bank(1, 0, 256), "s")
         ts(mks, bank(1, 256, 512), kcol, O.is_gt)
-        xn = A("xm%d" % (t % 2))
+        if not last:
+            kta = A("KT", NA - 1024, NA - 768)
+            tt(kta, kt, away, O.mult)
+            _, ba = best(kta, 256, "b", "mr", O.mult, O.max)
+            t2, g2, k2 = kb, dbl, S("si", "k2", 32)
+            ms(sub(t2, 0, 1), 0.0)
+            ms(sub(tb, 15, 256, 16), 0.0)
+            tt(sub(t2, 1, 256), sub(ta, 1, 256), sub(tb, 0, 255), O.min)
+            scan(g2, A("mr", 0, 256), t2, O.mult, O.max)
+            cp(sub(k2, 0, 16), sub(g2, 15, 256, 16))
+            cp(sub(k2, 16, 32), sub(ba, 15, 256, 16))
+            ts(k2, k2, 15, O.arith_shift_right)
+            cp(S("sh", "k2", 32), k2)
+            s2o(S("sh", "k2", 32), bank(4, 128, 160), 32)
+            cp(S("sb", "k2", 32), bank(4, 128, 160))
+            rows(bank(4), S("sb", "k2", 32))
+            m2a = LB("m2a", 512)
+            cp(m2a, bank(4), "s")
+            mms(bank(4, 0, 256), [(D01, rtc), (z0(2), nlr), (z0(3), sub(m2a, 256, 512))])
+            cp(A("RT", NA, NA + 256), bank(4, 0, 256), "s")
+        xn = A("xm0")
         for k in range(4):
-            tt(ch("prod", k), X(A("TAU"), chunks(CP, k, 4)), ch("oh", k), O.mult)
+            gt(ch("prod", k), X(A("TAU"), chunks(CP, k, 4)), ch("oh", k), O.mult, k)
             mm(bank(k % 2), B64, ch("prod", k))
             act(ch("a1", k), bank(k % 2), AF.Abs, 1.0 / 64)
             if not last:
                 tt(sub(xn, 512 * k, 512 * k + 512), bank(k % 2), sub(xm, 512 * k, 512 * k + 512), O.min)
+                tt(ch("xmb", k), bank(k % 2), ch("xm1", k), O.max)
             act(ch("pen", k), ch("a1", k), AF.Abs, 1.0, kab)
         if not last:
             gath(bank(4, 256, 384), zbig, "prod", 0, 2048)
@@ -814,39 +841,15 @@ def rank_program(g, core, T, topo):
         cp(A("ML", NA, NA + 256), bank(0, 0, 256))
         tt(dif, mlc, stay, O.subtract)
         if not last:
-            for k in range(4):
-                mm(bank(k % 2), B64N, ch("prod", k))
-                tt(ch("xmb", k), bank(k % 2), sub(xm, 512 * k, 512 * k + 512), O.min)
             cp(X(A("xmb"), U("sp")), zero)
             scan(A("usa", 0, 2048), A("m0"), xn, O.mult, O.max)
-            scan(A("usb"), A("m0"), A("xmb", 0, 2048), O.mult, O.max)
+            scan(A("usb"), A("m0"), A("xmb", 0, 2048), O.mult, O.min)
             ua, ub = A("UT", NA, NA + 256), LB("ub")
             cp(ua, X(A("usa"), EU), "s")
-            cp(ub, X(A("usb"), EU), "s")
+            ts(ub, X(A("usb"), EU), -1.0, O.mult)
             xm = xn
-            kta = A("KT", NA - 1024, NA - 768)
-            tt(kta, kt, away, O.mult)
-            _, ba = best(kta, 256, "b", "mr", O.mult, O.max)
-            t2, g2, k2 = kb, dbl, S("si", "k2", 32)
-            ms(sub(t2, 0, 1), 0.0)
-            ms(sub(tb, 15, 256, 16), 0.0)
-            tt(sub(t2, 1, 256), sub(ta, 1, 256), sub(tb, 0, 255), O.min)
-            scan(g2, A("mr", 0, 256), t2, O.mult, O.max)
-            cp(sub(k2, 0, 16), sub(g2, 15, 256, 16))
-            cp(sub(k2, 16, 32), sub(ba, 15, 256, 16))
-            ts(k2, k2, 15, O.arith_shift_right)
-            cp(S("sh", "k2", 32), k2)
-            s2o(S("sh", "k2", 32), bank(4, 128, 160), 32)
-            cp(S("sb", "k2", 32), bank(4, 128, 160))
-            rows(bank(0), S("sb", "k2", 32))
-            m2a = LB("m2a", 512)
-            cp(m2a, bank(0), "s")
-            gath(bank(4, 160, 176), zall, "lb", away[1], 256)
-            cp(U("nl"), bank(4, 160, 176))
-            nb = LB("nb")
-            cp(nb, X(NB, U("nl")), "s")
-            mms(bank(1, 0, 256), [(ID, nb), (D01, rtc), (z0(2), nlr), (z0(3), sub(m2a, 256, 512))])
-            cp(A("RT", NA, NA + 256), bank(1, 0, 256), "s")
+            if t < 2:
+                act(A("xm1"), xn, AF.Copy, -1.0)
         for k in range(4):
             mm(bank(2 + k % 2), CLS[cl], ch("at", k))
             act(ch("xc", k), bank(2 + k % 2), AF.Copy)
@@ -862,10 +865,10 @@ def rank_program(g, core, T, topo):
             tt(A("RT", NL + 256, NL + 512), bank(5, 0, 256), LH("r1"), O.max)
         hi, dl = payload(A("acq"), 256, "c", bank(3, 0, 256))
         for i in range(16):
-            if t or i % 2:
+            if i % 2:
                 asel(A("cx", i, 4096, 16), xsb, [[0, 256]], O.is_ge, 0, 0)
             else:
-                cp(A("cx", i, 4096, 16), xsb)
+                ts(A("cx", i, 4096, 16), xsb, 0.0, O.max)
         for k in range(8):
             tt(ch("cx", k), X(A("xc", 0, 2048), A("acq", 32 * k, 32 * k + 32)), ch("cx", k), O.subtract)
             act(ch("cx", k), ch("cx", k), AF.Square)
@@ -898,7 +901,7 @@ def rank_program(g, core, T, topo):
         tt(uv, ud, uc, O.max)
         mm(bank(5, 0, 256), ID, dg, True, False)
         for u in range(16):
-            e0 = 256 * (u % 4)
+            e0 = 256 * u
             ts(A("eq", e0 + 16 * u, e0 + 256), sub(drep, 16 * u, 256), sub(df_, u, u + 1), O.is_equal)
             mm(bank(5, 16 * u, 16 * u + 16), TW, A("eq", e0 + 16 * u, e0 + 16 * u + 16), False, u == 15)
             if u < 15:
@@ -918,10 +921,13 @@ def rank_program(g, core, T, topo):
         ts(sub(de, 0, 256), le, hi4, O.mult, cde, O.add)
         y1 = LH("y1")
         for b in range(4):
-            mm(bank(6, 0, 256), BIT[b], rtc)
-            tt(y1, bank(6, 0, 256), y, O.mult)
+            bit = LB("bit%d" % (b % 2))
+            cp(bit, X(sub(NB, 32 * b, 32 * b + 32), U("nU")))
+            tt(y1, bank(6, 256, 512) if b else y, bit, O.mult)
+            if b:
+                cp(y, bank(6, 256, 512))
             mms(bank(6, 256, 512), [(ID, y), (SH[b], y1)])
-            cp(y, bank(6, 256, 512), "s")
+        cp(y, bank(6, 256, 512))
         gath(bank(3, 272, 288), zall, "lb", uc[1], 256)
         want0, spl, wk = F("want0"), F("spl"), F("wk")
         tt(want0, bank(3, 272, 288), mS, O.add)

@@ -9,9 +9,9 @@ for _n, _w, _d in [
         ("prod", 2048, B2), ("cx", 4096, B2), ("pt", 2048, B2), ("hx", 1536, B2), ("at", 2064, B2),
         ("XL", 1024, B2), ("TAU", 1024, B2), ("CK", 1024, B2), ("el", 256, B2),
         ("px", 2048, H2), ("mr", 256, B2), ("mrb", 512, B2), ("ones", 256, B2), ("orp", 2048, B2),
-        ("wm", 7040, B2), ("zs", 2448, B2), ("lb", 9408, B2), ("lh", 3808, H2), ("lf", 3456, F4), ("li", 1024, I4), ("acq", 256, U2),
+        ("wm", 7040, B2), ("zs", 2448, B2), ("lb", 10176, B2), ("lh", 3808, H2), ("lf", 3456, F4), ("li", 1024, I4), ("acq", 256, U2),
         ("vs", 512, B2), ("yv", 96, B2),
-        ("sm", 2560, F4), ("si", 400, I4), ("su", 1200, U2), ("sh", 144, H2), ("sb", 416, B2), ("lim", 2, I4), ("wtc", 1, I4)]:
+        ("sm", 2560, F4), ("si", 400, I4), ("su", 1200, U2), ("sh", 208, H2), ("sb", 416, B2), ("lim", 2, I4), ("wtc", 1, I4)]:
     SCRATCH[_n] = ("sbuf", [128, _w], _d)
 ALIAS = {"a1": ("df", 0, 2048), "pen": ("sq", 0, 2048), "XB": ("XL", 0, 1024), "g16": ("lh", 0, 2048),
          "hd": ("hx", 0, 1536), "usb": ("df", 0, 2048), "eq": ("cx", 0, 4096)}
@@ -26,8 +26,9 @@ for _t in range(4):
 BIG = 33554432.0
 ENG = 8
 PLAN, PASSES = {}, 6
-BEHIND = 400
-HOP, SLACK, DMA, LINK = 100, 100, 2500, 4000
+OWN = 60
+BEHIND = 500
+HOP, SLACK, DMA, LINK = 100, 0, 2500, 4000
 
 
 def rank_program(g, core, T, topo):
@@ -127,7 +128,7 @@ def rank_program(g, core, T, topo):
                 succ[d].append(i)
 
         def hop(d, i):
-            return 0 if ops[i]["deps"][d] and ops[d]["e"] == ops[i]["e"] == "t" else HOP
+            return 0 if ops[i]["deps"][d] and ops[d]["e"] == ops[i]["e"] == "t" else OWN if ops[d]["e"] == ops[i]["e"] else HOP
         pred = [list(o["deps"]) for o in ops]
 
         def plan(prio, eng):
@@ -217,8 +218,8 @@ def rank_program(g, core, T, topo):
             alt = either(out, a, AF.Identity, s1, s2) if (op0, op1) == (O.mult, O.add) else None
             emit("v", lambda: g.vector.tensor_scalar(ap(out), ap(a), ap(s1), ap(s2), op0, op1), [out], [a, s1, s2], alt=alt)
 
-    def gt(out, x, b, op, k):
-        if k % 2:
+    def gt(out, x, b, op, split):
+        if split:
             act(out, x, AF.Copy)
             tt(out, out, b, op)
         else:
@@ -393,6 +394,8 @@ def rank_program(g, core, T, topo):
     tt(Q1, Q1, TW, O.subtract)
     ts(Q2, ID, 16.0, O.mult)
     tt(Q2, Q2, TW, O.add)
+    TWB = W1("TWB")
+    tt(TWB, TW, BB, O.subtract)
     WC, WD = W1("WC"), W1("WD")
     tt(WC, zms(0), zn(2), O.add)
     tt(WC, WC, znn(3), O.add)
@@ -441,8 +444,9 @@ def rank_program(g, core, T, topo):
     lims = F("lims", 2)
     cp(lims, A("lim"))
     thr0, thr = F("thr0", 1), F("thr", 1)
-    ts(thr0, sub(lims, 0, 1), 256.0, O.add, F("c_01", 1), O.mult)
-    ts(thr0, thr0, coef("t23", [(2, 16), (3, -1)]), O.add, 0.5, O.add)
+    n01 = coef("n01", [(0, -1), (1, -1)])
+    ts(thr0, sub(lims, 0, 1), 256.0, O.add, n01, O.mult)
+    ts(thr0, thr0, coef("t23", [(2, -16), (3, 1)]), O.add, -0.5, O.add)
     lim2 = F("lim2", 1)
     ts(lim2, sub(lims, 1, 2), 256.0, O.add)
     hi4 = coef("hi4", [(r, 1) for r in (4, 5, 6, 7, 8, 9, 10, 11)])
@@ -458,8 +462,9 @@ def rank_program(g, core, T, topo):
             mm(sub(out, w, 16 * n, 16), ors(w), lst)
 
     def s2o(r1, out, n):
-        mms(sub(out, 0, n, 2), [(PE_, sub(r1, 0, n, 2)), (P01, sub(r1, 1, n, 2))])
-        mms(sub(out, 1, n, 2), [(P10, sub(r1, 0, n, 2)), (PO_, sub(r1, 1, n, 2))])
+        ev, od = (r1[0], r1[1], r1[2], 2 * r1[3]), (r1[0], r1[1] + r1[3], r1[2], 2 * r1[3])
+        mms(sub(out, 0, n, 2), [(PE_, ev), (P01, od)])
+        mms(sub(out, 1, n, 2), [(P10, ev), (PO_, od)])
 
     def lin(out, tr, terms):
         n = width(tr)
@@ -563,21 +568,23 @@ def rank_program(g, core, T, topo):
         for w in range(16):
             mm(ps, zall(w), A(src, a + w, a + 16 * n, 16), False, w == 15)
 
-    def nearest(ps, dl, n, tag):
+    def nearest(ps, dl, n, tag, out, far):
         a, b = LF("t" + tag, 2 * n), LF("k" + tag, 2 * n)
         vtr(sub(a, 0, n), ps)
         tt(sub(b, 0, n), ps, dl, O.add)
         vtr(sub(a, n, 2 * n), sub(b, 0, n))
         scan(b, A("mrb", 0, 2 * n), a, O.max, O.min)
         m = n // 16
-        r = S("si", "r" + tag, 2 * m)
+        r, rh = S("si", "r" + tag, 2 * m), S("sh", "r" + tag, 3 * m)
         ts(r, sub(b, 15, 2 * n, 16), 2048.0, O.mult)
-        ts(sub(r, 0, m), sub(r, 0, m), 127, O.bitwise_and)
-        ts(sub(r, m, 2 * m), sub(r, m, 2 * m), 15, O.bitwise_and)
-        ah = F("ah" + tag, m)
-        ts(ah, sub(r, 0, m), 16.0, O.mult, -2048.0, O.add)
-        tt(ah, ah, sub(r, m, 2 * m), O.add)
-        return sub(b, 15, n, 16), ah
+        ts(r, r, 127, O.bitwise_and)
+        cp(sub(rh, 0, 2 * m), r)
+        parts = [(16, 0), (1, m)]
+        if far:
+            ts(sub(rh, 2 * m, 3 * m), sub(b, 15, n, 16), 4096.0, O.is_ge, 2048.0, O.mult)
+            parts.append((1, 2 * m))
+        for h in (0, 1):
+            mms(sub(out, h, m, 2), [(TS[w][2 * h + z], sub(rh, c + z, c + m, 2)) for w, c in parts for z in (0, 1)])
 
     def host(t, h):
         IN = "in%d" % t
@@ -621,9 +628,7 @@ def rank_program(g, core, T, topo):
             act(ch("hd", k, 768), ch("hd", k, 768), AF.Square)
         hi, dl = payload(hl, 96, "h", bank(7, 160, 256))
         sums(bank(7, 32, 128), "hd", 0, hi)
-        _, ah = nearest(bank(7, 32, 128), dl, 96, "h")
-        ts(S("sh", "y6", 6), ah, 2048.0, O.add)
-        s2o(S("sh", "y6", 6), bank(7, 128, 134), 6)
+        nearest(bank(7, 32, 128), dl, 96, "h", bank(7, 128, 134), False)
         cp(U("y6", 6), bank(7, 128, 134))
         cp(A("yv"), X(A("xa", 0, 2049), U("y6", 6)))
         send(h, "ry%d" % t, A("yv"), "rb%d" % t, "lb%d" % t)
@@ -701,8 +706,7 @@ def rank_program(g, core, T, topo):
     lb0 = LB("lb0")
     cp(lb0, A("xmb", 0, 256))
     agents(CP, 1024, False)
-    xm = A("xs", 0, 2048)
-    act(A("xm1"), xm, AF.Copy, -1.0)
+    act(A("xm1"), A("xs", 0, 2048), AF.Identity, 1.0, 32.0)
     zi = None
 
     for t in range(4):
@@ -738,12 +742,11 @@ def rank_program(g, core, T, topo):
         s3 = F("s3", 48)
         cp(s3, bank(4, 64, 112))
         sg, sf, mS = sub(s3, 0, 16), sub(s3, 16, 32), sub(s3, 32, 48)
-        st15, live, lval, tmp = F("st15"), F("live"), F("lval"), F("tmp")
+        st15, live, tmp = F("st15"), F("live"), F("tmp")
         ts(st15, bank(4, 32, 48), 15.0, O.add)
         EU = U("eu")
         ts(EU, bank(4, 16, 32), -1.0, O.add)
         ts(live, mS, 15.5, O.is_gt)
-        ts(lval, sub(k4, 48, 64), 15.5, O.is_gt)
         sp = F("sp")
         tt(sp, st15, sg, O.subtract)
         dead = F("dead")
@@ -751,15 +754,15 @@ def rank_program(g, core, T, topo):
         tt(sp, sp, dead, O.add)
         tt(sp, sp, l2048, O.min)
         cp(U("sp"), sp)
-        tt(dead, dead, sf, O.add)
-        tt(dead, dead, l2064, O.min)
-        cp(U("vA%d" % (t % 2)), dead)
+        tt(tmp, dead, sf, O.add)
+        tt(tmp, tmp, l2064, O.min)
+        cp(U("vA%d" % (t % 2)), tmp)
         xsb, xbb = LB("xsb"), LB("xbb")
         cp(xsb, X(A("xs"), U("sp")))
         cp(A("acq"), X(A("act"), U("hU")))
         cp(A("XL", *lanes), xsb)
         for k in range(4):
-            gt(ch("df", k), X(A("XL"), chunks(CP, k, 4)), ch("xs", k), O.subtract, k)
+            gt(ch("df", k), X(A("XL"), chunks(CP, k, 4)), ch("xs", k), O.subtract, k % 2)
             act(ch("sq", k), ch("df", k), AF.Square)
         byslot(sc)
         dsl, dbl, kb = LF("dsl"), LF("dbl"), LF("kb")
@@ -780,7 +783,7 @@ def rank_program(g, core, T, topo):
         cp(xbb, X(A("xs"), U("bp")))
         cp(A("XB", *lanes), xbb)
         for k in range(4):
-            gt(ch("df", k), X(A("XB"), chunks(CP, k, 4)), ch("xs", k), O.subtract, k)
+            gt(ch("df", k), X(A("XB"), chunks(CP, k, 4)), ch("xs", k), O.subtract, True)
             act(ch("sq", k), ch("df", k), AF.Square)
         byslot(sc2)
         tt(away, X(sub(sc2, 0, 2048), EU), dsl, O.is_lt)
@@ -817,14 +820,13 @@ def rank_program(g, core, T, topo):
             cp(m2a, bank(4), "s")
             mms(bank(4, 0, 256), [(D01, rtc), (z0(2), nlr), (z0(3), sub(m2a, 256, 512))])
             cp(A("RT", NA, NA + 256), bank(4, 0, 256), "s")
-        xn = A("xm0")
         for k in range(4):
-            gt(ch("prod", k), X(A("TAU"), chunks(CP, k, 4)), ch("oh", k), O.mult, k)
+            gt(ch("prod", k), X(A("TAU"), chunks(CP, k, 4)), ch("oh", k), O.mult, True)
             mm(bank(k % 2), B64, ch("prod", k))
             act(ch("a1", k), bank(k % 2), AF.Abs, 1.0 / 64)
             if not last:
-                tt(sub(xn, 512 * k, 512 * k + 512), bank(k % 2), sub(xm, 512 * k, 512 * k + 512), O.min)
-                tt(ch("xmb", k), bank(k % 2), ch("xm1", k), O.max)
+                act(ch("xm0", k), bank(k % 2), AF.Sign)
+                tt(ch("xmb", k), ch("xm0", k), ch("xm1", k), O.mult)
             act(ch("pen", k), ch("a1", k), AF.Abs, 1.0, kab)
         if not last:
             gath(bank(4, 256, 384), zbig, "prod", 0, 2048)
@@ -842,14 +844,13 @@ def rank_program(g, core, T, topo):
         tt(dif, mlc, stay, O.subtract)
         if not last:
             cp(X(A("xmb"), U("sp")), zero)
-            scan(A("usa", 0, 2048), A("m0"), xn, O.mult, O.max)
+            scan(A("usa", 0, 2048), A("m0"), A("xmb", 0, 2048), O.mult, O.max)
             scan(A("usb"), A("m0"), A("xmb", 0, 2048), O.mult, O.min)
             ua, ub = A("UT", NA, NA + 256), LB("ub")
-            cp(ua, X(A("usa"), EU), "s")
-            ts(ub, X(A("usb"), EU), -1.0, O.mult)
-            xm = xn
+            ts(ua, X(A("usa"), EU), -32.0, O.add)
+            ts(ub, X(A("usb"), EU), -1.0, O.mult, -32.0, O.add)
             if t < 2:
-                act(A("xm1"), xn, AF.Copy, -1.0)
+                act(A("xm1"), A("xmb", 0, 2048), AF.Relu)
         for k in range(4):
             mm(bank(2 + k % 2), CLS[cl], ch("at", k))
             act(ch("xc", k), bank(2 + k % 2), AF.Copy)
@@ -870,17 +871,17 @@ def rank_program(g, core, T, topo):
             else:
                 ts(A("cx", i, 4096, 16), xsb, 0.0, O.max)
         for k in range(8):
-            tt(ch("cx", k), X(A("xc", 0, 2048), A("acq", 32 * k, 32 * k + 32)), ch("cx", k), O.subtract)
+            if k % 4:
+                tt(ch("cx", k), X(A("xc", 0, 2048), A("acq", 32 * k, 32 * k + 32)), ch("cx", k), O.subtract)
+            else:
+                act(ch("hx", k // 4), X(A("xc", 0, 2048), A("acq", 32 * k, 32 * k + 32)), AF.Copy)
+                tt(ch("cx", k), ch("hx", k // 4), ch("cx", k), O.subtract)
             act(ch("cx", k), ch("cx", k), AF.Square)
             if k % 2:
                 sums(bank(3, 32 * k - 32, 32 * k + 32), "cx", 512 * k - 512, sub(hi, 32 * k - 32, 32 * k + 32))
-        key, ah = nearest(bank(3, 0, 256), dl, 256, "c")
-        ts(F("fit"), key, 4096.0, O.is_lt)
-        tt(F("fit"), F("fit"), lval, O.mult)
-        tt(ah, ah, F("fit"), O.mult)
-        ts(S("sh", "a16"), ah, 2048.0, O.add)
-        s2o(S("sh", "a16"), bank(2, 0, 16), 16)
-        cp(U("aU"), bank(2, 0, 16))
+        nearest(bank(3, 0, 256), dl, 256, "c", bank(2, 0, 16), True)
+        tt(F("fit"), bank(2, 0, 16), dead, O.max)
+        ts(U("aU"), F("fit"), 2048.0, O.min)
         ag = LB("ag")
         cp(ag, X(A("at", 0, 2049), U("aU")))
         vtr(LB("agt"), ag)
@@ -907,13 +908,15 @@ def rank_program(g, core, T, topo):
             if u < 15:
                 mm(bank(5, 16 * u + 16, 256), BB, A("eq", e0 + 16 * u + 16, e0 + 256), False, False)
         if t:
-            ts(thr, F("c_01", 1), zi, O.mult, thr0, O.add)
+            ts(thr, n01, zi, O.mult, thr0, O.add)
         mms(bank(2, 256, 512), [(W01, uv), (WC, rtc), (WD, rtd)])
         ok1, ok2 = LB("ok1"), LB("ok2")
-        act(ok1, bank(2, 256, 512), AF.Sign, -1.0, thr if t else thr0)
-        act(ok2, bank(5, 0, 256), AF.Sign, -1.0, 0.5)
-        tt(ok1, ok1, ok2, O.min)
-        gath(bank(2, 32, 48), zall, "lb", ok1[1], 256)
+        act(ok1, bank(2, 256, 512), AF.Sign, 1.0, thr if t else thr0)
+        act(ok2, bank(5, 0, 256), AF.Sign, 1.0, -0.5)
+        tt(ok1, ok1, ok2, O.max)
+        vtr(ok2, ok1)
+        scan(ok1, A("mr", 0, 256), ok2, O.mult, O.max)
+        s2o(sub(ok1, 15, 256, 16), bank(2, 32, 48), 16)
         ecnt = empties()
         le, de = LB("le"), LB("de", 512)
         mms(bank(6, 0, 256), [(ID, lb0), (ID, A("CK", *lanes)), (zn(2), rtc)])
@@ -929,28 +932,31 @@ def rank_program(g, core, T, topo):
             mms(bank(6, 256, 512), [(ID, y), (SH[b], y1)])
         cp(y, bank(6, 256, 512))
         gath(bank(3, 272, 288), zall, "lb", uc[1], 256)
-        want0, spl, wk = F("want0"), F("spl"), F("wk")
+        want0, spl = F("want0"), F("spl")
         tt(want0, bank(3, 272, 288), mS, O.add)
         ts(want0, want0, lim2, O.is_gt)
         tt(want0, want0, live, O.mult)
         dec = S("sb", "dec", 32)
-        ts(tmp, bank(2, 32, 48), 15.5, O.is_lt)
-        wb = S("sb", "wb")
-        tt(wb, want0, tmp, O.mult)
-        ts(sub(dec, 0, 16), tmp, -1.0, O.mult, 1.0, O.add)
-        ts(sub(no32, 0, 16), tmp, 2048.0, O.mult)
-        prefix(wb, 16, wk, "pw", bank(2, 48, 80))
+        wb, pk = S("sb", "wb", 32), F("pk", 32)
+        tt(sub(wb, 0, 16), bank(2, 32, 48), want0, O.mult)
+        tt(sub(wb, 16, 32), bank(2, 32, 48), live, O.mult)
+        mm(bank(2, 48, 80), BB, wb)
+        mm(bank(2, 80, 112), TWB, wb)
+        scan(pk, A("mr", 0, 32), bank(2, 48, 80), O.mult, O.add)
+        tt(pk, bank(2, 80, 112), pk, O.add)
+        wk, vk, busy = sub(pk, 0, 16), F("vk"), F("busy")
         ts(spl, wk, ecnt, O.is_lt)
-        tt(spl, spl, wb, O.mult)
-        cp(U("kU"), wk)
-        idle, vk, busy = S("sb", "idle"), F("vk"), F("busy")
-        tt(tmp, tmp, live, O.mult)
-        tt(idle, tmp, spl, O.subtract)
-        prefix(idle, 16, vk, "pv", bank(2, 80, 112))
-        ts(busy, idle, -1000.0, O.mult, 1000.0, O.add)
-        tt(vk, vk, busy, O.add)
-        tt(vk, vk, l256, O.min)
+        ts(vk, wk, ecnt, O.min)
+        tt(spl, spl, sub(wb, 0, 16), O.mult)
+        tt(vk, sub(pk, 16, 32), vk, O.subtract)
+        tt(busy, sub(wb, 16, 32), spl, O.is_gt)
+        tt(vk, vk, l256, O.subtract)
+        tt(vk, vk, busy, O.mult)
+        tt(vk, vk, l256, O.add)
         cp(U("vL"), vk)
+        cp(U("kU"), wk)
+        ts(sub(dec, 0, 16), bank(2, 32, 48), -1.0, O.mult, 1.0, O.add)
+        ts(sub(no32, 0, 16), bank(2, 32, 48), 2048.0, O.mult)
         cp(X(A("vs"), U("vL")), xsb)
         send(q, "in%d" % t, A("vs", 0, 96), "ra%d" % t, "la%d" % t)
         ts(sub(dec, 16, 32), spl, -1.0, O.mult, 1.0, O.add)
@@ -982,13 +988,13 @@ def rank_program(g, core, T, topo):
         cp(A("ML", NL, NL + 256), bank(6, 0, 256))
         if not last:
             u1, u2, u4, p1, n1 = LB("u1"), LB("u2"), LB("u4"), LH("p1"), LB("n1")
+            act(n1, bank(6, 0, 256), AF.Sign)
             tt(u1, ns_, ua, O.mult)
             tt(u2, mr_, uv, O.mult)
             tt(p1, mr_, rtd, O.mult)
-            tt(n1, ns_, nlr, O.mult)
             tt(u1, u1, u2, O.max)
             tt(u4, u1, ub, O.max)
-            mms(bank(5, 256, 512), [(zn(2), rtc), (zn(2), p1), (z0n(2), nlr), (z0(2), n1), (z0(3), sub(m2a, 0, 256))])
+            mms(bank(5, 256, 512), [(zall(2), n1), (z0(3), sub(m2a, 0, 256))])
             tt(LH("r1"), bank(5, 256, 512), p1, O.max)
             mm(bank(2, 128, 144), o128, sub(dec, 0, 16))
             emit("v", lambda: g.vector.tensor_reduce(ap(F("zz", 1)), ap(bank(2, 128, 144)), AX.X, O.add), [F("zz", 1)], [bank(2, 128, 144)])

from concourse.mybir import AluOpType as O, ActivationFunctionType as AF, AxisListType as AX

F4, B2, H2, I4, U2 = "float32", "bfloat16", "float16", "int32", "uint16"
SCRATCH = {}
for _n, _w, _d in [
        ("ML", 3088, F4), ("RT", 3088, F4), ("KT", 1808, F4), ("UT", 3088, B2), ("BT", 1792, B2), ("big", 4128, F4),
        ("act", 1024, I4), ("xa", 2320, B2), ("xc", 2320, B2), ("xs", 2304, B2), ("xm0", 2048, B2), ("xm1", 2048, B2), ("xmb", 2304, B2),
        ("usa", 2064, B2), ("atp", 2048, B2), ("oh", 2048, B2), ("sel", 2048, B2), ("m0", 2048, B2), ("df", 2048, B2), ("sq", 2048, B2),
        ("prod", 2048, B2), ("cx", 4096, B2), ("pt", 2048, B2), ("hx", 1536, B2), ("at", 2064, B2),
        ("XL", 1024, B2), ("TAU", 1024, B2), ("CK", 1024, B2), ("el", 256, B2),
        ("px", 2048, H2), ("mr", 256, B2), ("mrb", 512, B2), ("ones", 256, B2), ("orp", 2048, B2),
        ("wm", 7040, B2), ("zs", 2448, B2), ("lb", 10176, B2), ("lh", 3808, H2), ("lf", 3456, F4), ("li", 1024, I4), ("acq", 256, U2),
        ("vs", 512, B2), ("yv", 96, B2),
        ("sm", 2560, F4), ("si", 400, I4), ("su", 1200, U2), ("sh", 208, H2), ("sb", 416, B2), ("lim", 2, I4), ("wtc", 1, I4)]:
    SCRATCH[_n] = ("sbuf", [128, _w], _d)
ALIAS = {"a1": ("df", 0, 2048), "pen": ("sq", 0, 2048), "XB": ("XL", 0, 1024), "g16": ("lh", 0, 2048),
         "hd": ("hx", 0, 1536), "usb": ("df", 0, 2048), "eq": ("cx", 0, 4096)}
for _t in range(4):
    SCRATCH["in%d" % _t] = ("sbuf", [128, 96], B2)
    SCRATCH["ry%d" % _t] = ("sbuf", [128, 96], B2)
SCRATCH["psA"] = ("psum", [128, 2048], F4)
SCRATCH["psB"] = ("psum", [128, 2048], F4)
SEMAPHORES = ["sv", "ss", "st", "sg"] + ["d%d" % i for i in range(16)]
for _t in range(4):
    SEMAPHORES += ["ra%d" % _t, "rb%d" % _t, "la%d" % _t, "lb%d" % _t]
BIG = 33554432.0
ENG = 8
PLAN, PASSES = {}, 6
OWN = 60
BEHIND = 500
HOP, SLACK, DMA, LINK = 100, 0, 2500, 4000


def rank_program(g, core, T, topo):
    rank = T.rank_of(core)
    if rank is None:
        return
    Q = {"v": g.vector, "s": g.scalar, "t": g.tensor, "g": g, "y": g.sync}
    SEM = {"v": "sv", "s": "ss", "t": "st", "g": "sg"}
    cnt = {"v": 0, "s": 0, "t": 0, "g": 0}
    know = {e: {} for e in Q}
    hist = {}
    recs = {}
    ops = []
    fin = []
    sent = {}

    def A(n, a=0, b=None, s=1):
        if n in ALIAS:
            m, o, w = ALIAS[n]
            return (m, o + a, o + (w if b is None else b), s)
        return (n, a, SCRATCH[n][1][1] if b is None else b, s)

    def X(w, o):
        return ("X", w, o, 0)

    def ap(x):
        if not isinstance(x, tuple):
            return x
        if x[0] == "X":
            return ap(x[1]).indirect(ap(x[2]))
        n, a, b, s = x
        return T[n][:, a:b] if s == 1 else T[n][:, a:b:s]

    def sub(x, a, b, s=1):
        return (x[0], x[1] + a, x[1] + b, s)

    def touch(outs, ins):
        acc = []
        for x, w in [(o, True) for o in outs] + [(i, False) for i in ins]:
            if not isinstance(x, tuple):
                continue
            for y, ww in ([(x[1], w), (x[2], False)] if x[0] == "X" else [(x, w)]):
                n, a, b, s = y
                if n[:2] == "ps":
                    for k in range(a // 512, (b - 1) // 512 + 1):
                        acc.append((n, 512 * k, 512 * k + 512, True, True, 1))
                else:
                    acc.append((n, a, b, ww, False, s))
        me = len(ops)
        deps = {}
        for n, a, b, w, ps, s in acc:
            for r in recs.get((n, True), []) + (recs.get((n, False), []) if w else []):
                if r[0] < b and a < r[1] and r[2] != me and not (s == r[3] and (a - r[0]) % s):
                    deps[r[2]] = deps.get(r[2], True) and ps
        for n, a, b, w, ps, s in acc:
            if w:
                for k in ((n, True), (n, False)):
                    recs[k] = [r for r in recs.get(k, []) if not (a <= r[0] and r[1] <= b and (s == 1 or (s == r[3] and (a - r[0]) % s == 0)))]
            recs.setdefault((n, w), []).append((a, b, me, s))
        return deps

    def width(x):
        return 16 * width(x[2]) if x[0] == "X" else len(range(x[1], x[2], x[3]))

    def narrow(xs):
        return all(SCRATCH[x[0]][2] in (B2, H2, U2) for x in xs)

    def cycles(e, kind, outs, ins):
        big = [x for x in ins if isinstance(x, tuple) and width(x) > 1] or outs
        n = width(big[-1] if e == "t" else big[0])
        if outs[0][0] == "X":
            return 60 + 3 * n
        if big[0][0] == "X":
            return 60 + 1.5 * n
        if e == "g":
            return 180 + 2 * n
        if e == "t":
            return max(64, n) * (1 if narrow(big) else 4)
        if e == "s":
            return max(64, n)
        per = 2 if kind == "tt" and all(x[0][:2] != "ps" for x in big) else 1
        return max(64, n * per * (0.5 if narrow(big + outs) else 1))

    def emit(e, fn, outs, ins, kind="", sem=None, inc=1, busy=None, lat=0, after=(), alt=None):
        deps = touch(outs, ins)
        for d in after:
            deps[d] = False
        ops.append({"e": e, "fn": fn, "deps": deps, "sem": sem, "inc": inc, "busy": cycles(e, kind, outs, ins) if busy is None else busy, "lat": lat,
                    "alt": (alt, cycles("s", kind, outs, ins)) if alt else None})
        return len(ops) - 1

    def issue():
        n = len(ops)
        succ = [[] for _ in ops]
        for i, o in enumerate(ops):
            for d in o["deps"]:
                succ[d].append(i)

        def hop(d, i):
            return 0 if ops[i]["deps"][d] and ops[d]["e"] == ops[i]["e"] == "t" else OWN if ops[d]["e"] == ops[i]["e"] else HOP
        pred = [list(o["deps"]) for o in ops]

        def plan(prio, eng):
            nxt, left = (pred, [len(x) for x in succ]) if eng else (succ, [len(x) for x in pred])
            home = eng or [o["e"] for o in ops]
            at, end, got, order = [0.0] * n, [0.0] * n, list(home), []
            ready = {e: [] for e in "vstgya"}
            free = {e: 0.0 for e in "vstgya"}
            for i in range(n):
                if not left[i]:
                    ready[home[i]].append(i)
            while len(order) < n:
                can = dict(ready)
                if not eng:
                    can["s"] = ready["s"] + [i for i in ready["v"] if ops[i]["alt"]]
                    can["v"] = [i for i in ready["v"] if not ops[i]["alt"] or free["s"] > max(free["v"], at[i]) + BEHIND]
                t, e = min((max(free[x], min(at[i] for i in can[x])), x) for x in can if can[x])
                i = max((i for i in can[e] if at[i] <= t + SLACK), key=lambda i: (prio[i], -i))
                ready[home[i]].remove(i)
                got[i] = e
                order.append(i)
                free[e] = end[i] = max(t, at[i]) + (ops[i]["busy"] if e == ops[i]["e"] else ops[i]["alt"][1])
                for j in nxt[i]:
                    at[j] = max(at[j], end[i] + (ops[j]["lat"] + hop(j, i) if eng else ops[i]["lat"] + hop(i, j)))
                    left[j] -= 1
                    if not left[j]:
                        ready[home[j]].append(j)
            return max(end[i] + ops[i]["lat"] for i in range(n)), order, got, end
        if n not in PLAN:
            tail = [0.0] * n
            for i in range(n - 1, -1, -1):
                tail[i] = ops[i]["busy"] + ops[i]["lat"] + max([tail[j] + hop(i, j) for j in succ[i]] + [0])
            plans = [plan(tail, None)]
            for _ in range(PASSES):
                plans.append(plan(plan(plans[-1][3], plans[-1][2])[3], None))
            PLAN[n] = min(plans, key=lambda p: p[0])
        order = PLAN[n][1]
        for i, e in enumerate(PLAN[n][2]):
            if e != ops[i]["e"]:
                ops[i].update({"e": e, "fn": ops[i]["alt"][0]})
        mark = {}
        for i in order:
            o = ops[i]
            e = o["e"]
            if e == "a":
                mark[i] = (o["sem"], o["inc"])
                hist[mark[i]] = {}
                fin.append(mark[i])
                continue
            need = {}
            for d, ps in o["deps"].items():
                if not (ps and ops[d]["e"] == e == "t"):
                    need[mark[d][0]] = max(need.get(mark[d][0], 0), mark[d][1])
            for x in sorted(need):
                if know[e].get(x, 0) < need[x]:
                    Q[e].wait_ge(T.sem[x], need[x])
                    for k, v in hist[(x, need[x])].items():
                        know[e][k] = max(know[e].get(k, 0), v)
                    know[e][x] = need[x]
            if o["sem"]:
                mark[i] = (o["sem"], o["inc"])
                fin.append(mark[i])
                o["fn"]()
            else:
                cnt[e] += 1
                mark[i] = (SEM[e], cnt[e])
                o["fn"]().then_inc(T.sem[SEM[e]], 1)
            hist[mark[i]] = dict(know[e])
        for who, v in fin + [(SEM[e], cnt[e]) for e in ("v", "s", "t", "g")]:
            g.wait_ge(T.sem[who], v)

    def either(out, i, f, scale=1.0, bias=0.0):
        if out[0] != "X" and all(SCRATCH[x[0]][2] in (F4, B2, H2) for x in (out, i[1] if i[0] == "X" else i)):
            return lambda: g.scalar.activation(ap(out), ap(i), f, bias=ap(bias), scale=ap(scale))

    def cp(out, i, e="v"):
        emit("v", lambda: g.vector.tensor_copy(ap(out), ap(i)), [out], [i], alt=either(out, i, AF.Copy))

    def tt(out, a, b, op):
        emit("v", lambda: g.vector.tensor_tensor(ap(out), ap(a), ap(b), op), [out], [a, b], "tt")

    def ts(out, a, s1, op0, s2=None, op1=None):
        if op1 is None:
            alt = either(out, a, AF.Identity, 1.0, s1) if op0 == O.add else either(out, a, AF.Copy, s1) if op0 == O.mult else None
            emit("v", lambda: g.vector.tensor_scalar(ap(out), ap(a), ap(s1), None, op0), [out], [a, s1], alt=alt)
        else:
            alt = either(out, a, AF.Identity, s1, s2) if (op0, op1) == (O.mult, O.add) else None
            emit("v", lambda: g.vector.tensor_scalar(ap(out), ap(a), ap(s1), ap(s2), op0, op1), [out], [a, s1, s2], alt=alt)

    def gt(out, x, b, op, split):
        if split:
            act(out, x, AF.Copy)
            tt(out, out, b, op)
        else:
            tt(out, x, b, op)

    def scan(out, d0, d1, op0, op1, init=0.0):
        emit("v", lambda: g.vector.tensor_tensor_scan(ap(out), ap(d0), ap(d1), ap(init), op0, op1), [out], [d0, d1, init])

    def vtr(out, i):
        emit("v", lambda: g.vector.transpose(ap(out), ap(i)), [out], [i])

    def ms(out, c):
        emit("v", lambda: g.vector.memset(ap(out), c), [out], [])

    def fill(out, c):
        iota(out, [[0, width(out)]], c, 0)

    def act(out, i, f, scale=1.0, bias=0.0):
        emit("s", lambda: g.scalar.activation(ap(out), ap(i), f, bias=ap(bias), scale=ap(scale)), [out], [i, scale, bias])

    def mm(out, l, r, start=True, stop=True):
        emit("t", lambda: g.tensor.matmul(ap(out), ap(l), ap(r), start, stop), [out], [l, r])

    def mms(out, pairs):
        for k, (l, r) in enumerate(pairs):
            mm(out, l, r, k == 0, k == len(pairs) - 1)

    def asel(out, i, pat, op, base, cm):
        emit("g", lambda: g.affine_select(ap(out), ap(i), pat, op, 0.0, base, cm), [out], [i])

    def iota(out, pat, base, cm):
        emit("g", lambda: g.iota(ap(out), pat, base, cm, allow_small_or_imprecise_dtypes=True), [out], [])

    nd = [0]

    def dma(e, o, i, oa, ia, add=False):
        who = "d%d" % nd[0]
        nd[0] += 1
        how = {"accum_op": O.add} if add else {}
        emit(e, lambda: Q[e].dma_start(oa, ia, **how).then_inc(T.sem[who], 16), [o] if o else [], [i] if i else [], sem=who, inc=16,
             busy=1000 if e == "g" else 60, lat=DMA + (2000 if add else 0))

    slots = {}
    used = {}

    def S(buf, name, w=16):
        if (buf, name) not in slots:
            u = used.get(buf, 0)
            slots[(buf, name)] = A(buf, u, u + w)
            used[buf] = u + (w + 15) // 16 * 16
        return slots[(buf, name)]

    def F(name, w=16):
        return S("sm", name, w)

    def U(name, w=16):
        return S("su", name, w)

    def LB(name, w=256):
        return S("lb", name, w)

    def LH(name, w=256):
        return S("lh", name, w)

    def LF(name, w=256):
        return S("lf", name, w)

    def bank(k, a=0, b=512):
        return A("psA" if k < 4 else "psB", 512 * (k % 4) + a, 512 * (k % 4) + b)

    def ch(n, k, w=512, o=0):
        return A(n, o + w * k, o + w * k + w)

    def chunks(off, k, n):
        w = (off[2] - off[1]) // n
        return sub(off, k * w, k * w + w)

    for n, src in (("li", T.ml), ("xa", T.x0), ("act", T.ac), ("lim", T.lims), ("wtc", T.wt)):
        w = src.shape[1]
        dma("y", A(n, 0, w), None if n == "li" else A("li", 0, 1), T[n][:, 0:w], src[:, 0:w])

    ones = A("ones")
    ms(ones, 1.0)
    o128 = A("ones", 0, 128)
    iota(F("i144", 144), [[1, 144]], 0, 0)
    i16 = sub(F("i144", 144), 0, 16)
    iota(F("pi", 1), [[0, 1]], 0, 1)
    iota(F("c64", 64), [[16, 64]], 0, 0)

    def W1(name):
        return S("wm", name, 128)
    BB, ID, SP, SN, TW, REV = W1("BB"), W1("ID"), W1("SP"), W1("SN"), W1("TW"), W1("REV")
    asel(BB, o128, [[-16, 8], [0, 16]], O.is_ge, 0, 1)
    asel(BB, BB, [[16, 8], [0, 16]], O.is_ge, 15, -1)
    asel(ID, o128, [[-1, 128]], O.is_equal, 0, 1)
    chi, clo, ccl = A("xm0", 0, 1024), A("xm0", 1024, 2048), A("prod", 0, 1024)
    iota(chi, [[1, 64], [0, 16]], 0, 0)
    iota(clo, [[0, 64], [1, 16]], 0, 0)
    iota(ccl, [[0, 256], [1, 4]], 0, 0)
    asel(SP, o128, [[-1, 128]], O.is_equal, 16, 1)
    asel(SN, o128, [[-1, 128]], O.is_equal, -16, 1)
    asel(TW, BB, [[1, 128]], O.is_gt, 0, -1)
    asel(REV, o128, [[-16, 8], [1, 16]], O.is_equal, -15, 1)
    SH = [W1("SH%d" % b) for b in range(4)]
    for b in range(4):
        asel(SH[b], BB, [[-1, 128]], O.is_equal, 1 << b, 1)
        tt(SH[b], SH[b], ID, O.subtract)
    pi, p2 = S("si", "pi", 1), S("si", "p2", 1)
    kcol, mO, mE, g15 = F("kcol", 1), F("mO", 1), F("mE", 1), F("g15", 1)
    cp(pi, F("pi", 1))
    ts(p2, pi, 15, O.bitwise_and)
    cp(kcol, p2)
    ts(S("si", "p3", 1), pi, 4, O.arith_shift_right, 1, O.bitwise_and)
    cp(mO, S("si", "p3", 1))
    ts(mE, mO, -1.0, O.mult, 1.0, O.add)
    ts(g15, F("pi", 1), kcol, O.subtract, 15.0, O.add)
    rm = F("rm")
    ts(rm, i16, kcol, O.is_equal)

    def RM(r):
        return sub(rm, r, r + 1)

    def coef(name, terms):
        c = F("c_" + name, 1)
        ts(c, RM(terms[0][0]), float(terms[0][1]), O.mult)
        for r, w in terms[1:]:
            ts(c, RM(r), float(w), O.mult, c, O.add)
        return c

    def kc(name, a, b):
        c = F("k_" + name, 1)
        ts(c, kcol, float(a), O.mult, float(b), O.add)
        return c

    def zset(name, col):
        z = S("zs", name, 144)
        ts(z, F("i144", 144), g15, O.is_equal, col, O.mult)
        return lambda w: sub(z, 15 - w, 143 - w)

    def mk(name, src, col, w=1.0):
        m = W1(name)
        ts(m, src, col, O.mult, float(w), O.mult)
        return m

    cE = RM(0)
    zall, zneg = zset("all", 1.0), zset("neg", -1.0)
    z0, z0n, zn, zms = zset("0", RM(0)), zset("0n", coef("0n", [(0, -1)])), zset("n", RM(2)), zset("ms", RM(3))
    zown, zc = zset("own", coef("own", [(0, 16), (1, 1)])), zset("c", coef("c", [(4, 16), (5, 1)]))
    znn = zset("nn", coef("nn", [(2, -1)]))
    wf = F("wf", 1)
    cp(wf, A("wtc"))
    zw = zset("w", wf)
    Z16 = zset("16", 16.0)

    def ors(w):
        return A("orp", 128 * w, 128 * w + 128)
    W012 = W1("W012")
    tt(W012, zall(0), zall(1), O.add)
    W01 = W1("W01")
    cp(W01, W012)
    tt(W012, W012, zall(2), O.add)
    PE_, PO_, P01, P10 = mk("PE", ID, mE), mk("PO", ID, mO), mk("P01", SP, mE), mk("P10", SN, mO)
    BB16, BBN, B64, BK = mk("BB16", BB, 16.0), mk("BBN", BB, -1.0), mk("B64", BB, 64.0), mk("BK", BB, -32768.0)
    N16, K16 = mk("N16", BB, RM(1), 65536.0), mk("K16", ID, kc("k16", -65536, 65536 * 33))
    I23, IPN = mk("I23", ID, 8388608.0), mk("IPN", ID, -16384.0)
    NREP, CREP = mk("NREP", BB, RM(2)), mk("CREP", BB, F("c_c", 1))
    CLS = [mk("CLS%d" % m, BB, RM(8 + m), 64.0) for m in range(4)]
    D01 = mk("D01", ID, coef("01", [(0, 1), (1, 1)]))
    DH, DL, DH2, DL2 = mk("DH", ID, RM(4)), mk("DL", ID, RM(5)), mk("DH2", ID, coef("06", [(0, 1), (6, 1)])), mk("DL2", ID, coef("17", [(1, 1), (7, 1)]))
    Q1, Q2, TW2, IDN = W1("Q1"), W1("Q2"), mk("TW2", TW, -2.0), mk("IDN", ID, -1.0)
    ts(Q1, ID, -0.5, O.mult)
    tt(Q1, Q1, TW, O.subtract)
    ts(Q2, ID, 16.0, O.mult)
    tt(Q2, Q2, TW, O.add)
    TWB = W1("TWB")
    tt(TWB, TW, BB, O.subtract)
    WC, WD = W1("WC"), W1("WD")
    tt(WC, zms(0), zn(2), O.add)
    tt(WC, WC, znn(3), O.add)
    tt(WD, zms(1), zn(2), O.add)
    for w in range(16):
        ts(ors(w), BB, RM(w), O.mult)
    lane, c4 = F("lane"), F("c4", 64)
    ts(c4, F("c64", 64), kcol, O.add)
    lane = sub(c4, 0, 16)
    kneg, kab, k128 = kc("neg", -1, 0), kc("ab", -1, -0.5), kc("128", 128, 0)
    fill(A("mr"), 1)
    fill(A("mr", 0, 256, 16), 0)
    fill(A("mrb"), 0)
    ms(A("mrb", 0, 512, 16), BIG)
    fill(A("XL"), 0)
    ts(A("TAU"), A("XL"), 0.25, O.add)
    zbig = zset("big", 16384.0)
    I11, I17N, DK16, REVN = mk("I11", ID, 1.0 / 2048), mk("I17N", ID, -17.0), mk("DK16", ID, kc("16", 0.0625, -0.75)), mk("REVN", REV, -1.0)
    fill(A("vs"), 0)
    fill(A("xs", 2048, 2304), 0)
    fill(A("xa", 2048, 2064), 64)
    fill(A("usa", 2048, 2064), 0)
    fill(A("UT", 2048, 2064), 0)
    fill(A("ML", 2048, 2064), 0)
    fill(A("RT", 2048, 2064), 0)
    fill(A("KT", 1024, 1040), 0)
    ts(A("RT", 2049, 2050), RM(2), 99.0, O.mult)
    cp(A("at", 2048, 2049), coef("far", [(4, 127), (5, 15), (6, 128), (7, 1)]))
    zero, i256 = LB("zero"), LB("i256")
    fill(zero, 0)
    iota(i256, [[1, 256]], 0, 0)
    zk = zset("k", kcol)
    l05, l2048, l2064, l256, l32 = F("l05"), F("l2048"), F("l2064"), F("l256"), F("l32", 32)
    for c, v in ((l05, 0.5), (l2048, 2048.0), (l2064, 2064.0), (l256, 256.0), (sub(l32, 0, 16), 1280.0), (sub(l32, 16, 32), 1536.0)):
        ts(c, lane, v, O.add)
    TS = {1: (PE_, P01, P10, PO_)}
    for w in (16, -1):
        TS[w] = [mk("%s%d" % (n, w + 1), m, float(w)) for n, m in zip("abcd", TS[1])]
    dg = LB("dg")
    ts(dg, sub(clo, 0, 256), kcol, O.is_lt, -64.0, O.mult)
    NB, nbi = S("sb", "NB", 128), S("si", "nbi", 128)
    for b in range(4):
        ts(sub(nbi, 32 * b, 32 * b + 32), sub(F("i144", 144), 0, 32), 0.5 ** b, O.mult, -0.4375, O.add)
    ts(nbi, nbi, 1, O.bitwise_and)
    cp(NB, nbi)
    lims = F("lims", 2)
    cp(lims, A("lim"))
    thr0, thr = F("thr0", 1), F("thr", 1)
    n01 = coef("n01", [(0, -1), (1, -1)])
    ts(thr0, sub(lims, 0, 1), 256.0, O.add, n01, O.mult)
    ts(thr0, thr0, coef("t23", [(2, -16), (3, 1)]), O.add, -0.5, O.add)
    lim2 = F("lim2", 1)
    ts(lim2, sub(lims, 1, 2), 256.0, O.add)
    hi4 = coef("hi4", [(r, 1) for r in (4, 5, 6, 7, 8, 9, 10, 11)])
    cde = coef("de", [(0, 128)])

    def gath(out, st, src, a, n, step=1):
        for w in range(16):
            mm(out, st(w), A(src, a + step * w, a + step * n, 16 * step), w == 0, w == 15)

    def rows(out, lst):
        n = width(lst)
        for w in range(16):
            mm(sub(out, w, 16 * n, 16), ors(w), lst)

    def s2o(r1, out, n):
        ev, od = (r1[0], r1[1], r1[2], 2 * r1[3]), (r1[0], r1[1] + r1[3], r1[2], 2 * r1[3])
        mms(sub(out, 0, n, 2), [(PE_, ev), (P01, od)])
        mms(sub(out, 1, n, 2), [(P10, ev), (PO_, od)])

    def lin(out, tr, terms):
        n = width(tr)
        for h in (0, 1):
            mms(sub(out, h, n // 16, 2), [(TS[w][2 * h + z], sub(tr, 16 * z + r, n, 32)) for r, w in terms for z in (0, 1)][::1 - 2 * h])

    def prefix(ind, n, out, tag, ps):
        mm(sub(ps, 0, n), TW, ind)
        mm(sub(ps, n, 2 * n), BB, ind)
        inc = F(tag + "inc", n + 1)
        if tag not in used:
            used[tag] = 0
            ms(sub(inc, 0, 1), 0.0)
        scan(sub(inc, 1, n + 1), A("ones", 0, n), sub(ps, n, 2 * n), O.mult, O.add)
        tt(out, sub(ps, 0, n), sub(inc, 0, n), O.add)
        return sub(inc, n, n + 1)

    def choose(out, cond, a, b, tag, w=16):
        d = F("ch" + tag, w)
        tt(d, a, b, O.subtract)
        tt(d, d, cond, O.mult)
        tt(out, d, b, O.add)

    def best(src, n, tag, mask, op0, op1):
        a, b = LF("t" + tag, n), LF(("k" if mask == "mrb" else "g") + tag, n)
        vtr(a, src)
        scan(b, A(mask, 0, n), a, op0, op1)
        return a, b

    def segscan(out, passes, banks):
        for k in range(4):
            ps = bank(banks[k % 2])
            mms(ps, [(m, ch(n, k)) for m, n in passes])
            scan(sub(out, 512 * k, 512 * k + 512), ch("m0", k), ps, O.mult, O.max, sub(out, 512 * k - 1, 512 * k) if k else 0.0)

    def byslot(out):
        for k in range(4):
            mm(bank(k % 2), BB16, ch("sq", k))
            scan(sub(out, 512 * k, 512 * k + 512), ch("sel", k), bank(k % 2), O.add, O.min, sub(out, 512 * k - 1, 512 * k) if k else 0.0)

    CP, CPF, POS, IX = U("cp", 128), F("cpf", 128), U("pos", 128), U("ix", 128)
    sc, sc2 = A("big", 0, 2064), A("big", 2064, 4128)

    def agents(lst, hi, last):
        for k in range(4):
            cp(ch("atp", k), X(A("BT", 0, hi), chunks(lst, k, 4)))
        for k in range(0 if last else 4):
            cp(ch("at", k), X(A("atp"), chunks(POS, k, 4)))
        if hi > 1024 and not last:
            for k in range(2):
                gath(bank(k, 0, 64), zc, "atp", 1024 * k, 1024)
                cp(chunks(CP, k, 2), bank(k, 0, 64))
                ts(chunks(CPF, k, 2), bank(k, 0, 64), 4096.0, O.add)

    def empties():
        gath(bank(6, 0, 64), zn, "BT", 0, 1024)
        e64, r64, eb = F("e64", 64), F("r64", 64), S("sb", "e64", 64)
        ts(eb, bank(6, 0, 64), 0.5, O.is_lt)
        e = prefix(eb, 64, r64, "pe", bank(6, 64, 192))
        inc, acc, rb = sub(F("peinc"), 1, 65), F("acc"), S("sb", "rb", 64)
        for u in range(16):
            emit("s", lambda u=u: g.scalar.activation(ap(e64), ap(inc), AF.Sign, bias=ap(sub(l05, u, u + 1)), scale=-1.0, accum_out=ap(sub(acc, u, u + 1))),
                 [e64, sub(acc, u, u + 1)], [inc, l05], busy=90)
        ts(acc, acc, 8.0, O.mult, 512.0, O.add)
        ts(acc, acc, 1008.0, O.min)
        ts(U("ub"), acc, 0.0625, O.mult)
        ts(rb, eb, 1000.0, O.mult, -1000.0, O.add)
        tt(rb, r64, rb, O.subtract)
        ek = LB("ek")
        tt(ek, X(rb, U("ub")), i256, O.is_equal)
        gath(bank(6, 192, 208), zk, "lb", ek[1], 256)
        tt(acc, bank(6, 192, 208), acc, O.add)
        cp(U("ec"), acc)
        cp(A("el"), X(A("CK"), U("ec")))
        return e

    def send(dst, out, src, rs, ls):
        rid, pid, _ = topo.addr(dst)
        es = topo.engines(core, dst)[:ENG]
        m = 0
        for e in es:
            m |= 1 << e
        sent[rs] = emit("g", lambda: g.remote_dma(out_ap=T[out][:], in_ap=ap(src), remote_sem=T.sem[rs], local_sem=T.sem[ls], pid=pid, routing_id=rid,
                                                  dma_engine_mask=m), [], [src], sem=ls, inc=len(es), busy=300, lat=LINK)

    def arrived(buf, rs, src):
        emit("a", None, [A(buf)], [], sem=rs, inc=len(topo.engines(src, core)[:ENG]), busy=0, after=[sent[rs]])

    def payload(lst, n, tag, ps):
        idf, hi, dl = LH("id" + tag, n), LH("hi" + tag, n), LB("dl" + tag, n)
        cp(idf, lst)
        ts(hi, idf, 0.0625, O.mult, 1535.53125, O.add)
        mms(ps, [(ID, idf), (I17N, hi)])
        ts(dl, ps, 1.0 / 2048, O.mult, 12.75, O.add)
        return hi, dl

    def sums(ps, src, a, hi):
        n = width(ps)
        mm(ps, I11, hi, True, False)
        mm(ps, DK16, A("ones", 0, n), False, False)
        for w in range(16):
            mm(ps, zall(w), A(src, a + w, a + 16 * n, 16), False, w == 15)

    def nearest(ps, dl, n, tag, out, far):
        a, b = LF("t" + tag, 2 * n), LF("k" + tag, 2 * n)
        vtr(sub(a, 0, n), ps)
        tt(sub(b, 0, n), ps, dl, O.add)
        vtr(sub(a, n, 2 * n), sub(b, 0, n))
        scan(b, A("mrb", 0, 2 * n), a, O.max, O.min)
        m = n // 16
        r, rh = S("si", "r" + tag, 2 * m), S("sh", "r" + tag, 3 * m)
        ts(r, sub(b, 15, 2 * n, 16), 2048.0, O.mult)
        ts(r, r, 127, O.bitwise_and)
        cp(sub(rh, 0, 2 * m), r)
        parts = [(16, 0), (1, m)]
        if far:
            ts(sub(rh, 2 * m, 3 * m), sub(b, 15, n, 16), 4096.0, O.is_ge, 2048.0, O.mult)
            parts.append((1, 2 * m))
        for h in (0, 1):
            mms(sub(out, h, m, 2), [(TS[w][2 * h + z], sub(rh, c + z, c + m, 2)) for w, c in parts for z in (0, 1)])

    def host(t, h):
        IN = "in%d" % t
        arrived(IN, "ra%d" % t, h)
        gath(bank(7, 0, 6), zw, IN, 0, 96)
        vi = S("si", "vi", 6)
        cp(vi, bank(7, 0, 6))
        ts(vi, vi, 2047, O.bitwise_and)
        cp(U("vi", 6), vi)
        vag = LB("vag", 96)
        cp(vag, X(A("pt"), U("vi", 6)))
        vtr(LB("vagt", 96), vag)
        lin(bank(7, 8, 14), LB("vagt", 96), [(0, 16), (1, 1)])
        cp(U("vp", 6), bank(7, 8, 14))
        cp(vag, X(A("atp"), U("vp", 6)))
        if t == 3:
            vt, vc, vw = LB("vt", 96), F("vc", 6), F("vw", 6)
            cp(vt, X(A("prod"), U("vp", 6)))
            vtr(LB("vagt", 96), vag)
            lin(bank(7, 8, 14), LB("vagt", 96), [(4, 16), (5, 1)])
            ts(vc, bank(7, 8, 14), 4096.0, O.add)
            gath(bank(7, 0, 6), zbig, "lb", vt[1], 96)
            ts(vw, vc, 0.25, O.mult, 4096.0 - t / 4.0, O.add)
            tt(vw, bank(7, 0, 6), vw, O.min)
            tt(vw, vw, vc, O.max)
            ts(U("vx", 6), vw, -4096.0, O.add)
            cp(vag, X(A("BT", 0, 1280), U("vx", 6)))
        vtr(LB("vagt", 96), vag)
        lin(bank(7, 16, 22), LB("vagt", 96), [(6, 16), (7, 1)])
        lo = 768 - 256 * t
        ts(U("hp", 6), bank(7, 16, 22), float(-lo), O.add)
        hl = U("hl", 96)
        ts(hl, X(A("ML", lo, 2320 + 256 * t), U("hp", 6)), -1.0, O.mult, 2048.0, O.add)
        for i in range(16):
            if i % 2:
                asel(A("hx", i, 1536, 16), A(IN), [[0, 96]], O.is_ge, 0, 0)
            else:
                cp(A("hx", i, 1536, 16), A(IN))
        for k in range(2):
            tt(ch("hd", k, 768), X(A("xa", 0, 2049), chunks(hl, k, 2)), ch("hx", k, 768), O.subtract)
            act(ch("hd", k, 768), ch("hd", k, 768), AF.Square)
        hi, dl = payload(hl, 96, "h", bank(7, 160, 256))
        sums(bank(7, 32, 128), "hd", 0, hi)
        nearest(bank(7, 32, 128), dl, 96, "h", bank(7, 128, 134), False)
        cp(U("y6", 6), bank(7, 128, 134))
        cp(A("yv"), X(A("xa", 0, 2049), U("y6", 6)))
        send(h, "ry%d" % t, A("yv"), "rb%d" % t, "lb%d" % t)

    def answer(t, q):
        arrived("ry%d" % t, "rb%d" % t, q)
        ri, nx = S("li", "ri", 96), LB("nx")
        tt(ri, A("ry%d" % t), A("vs", 0, 96), O.add)
        ts(ri, ri, 1, O.arith_shift_right)
        cp(A("vs", 0, 96), ri)
        cp(nx, X(A("vs"), U("vL")))
        return nx

    ind, rt0 = A("at", 0, 1024), A("g16", 0, 1024)
    ts(ind, A("li"), 2048.0, O.is_lt)
    ts(A("ML", 1024, 2048), A("li"), -1.0, O.mult, 2048.0, O.add)
    d0 = A("at", 1024, 2048)
    act(d0, chi, AF.Identity, 0.0, RM(0))
    for k in range(2):
        mm(bank(k), W012, sub(ind, 512 * k, 512 * k + 512))
    scan(rt0, d0, A("psA", 0, 1024), O.mult, O.add)
    vtr(A("g16", 1024, 2048), rt0)
    lin(bank(4, 0, 64), A("g16", 1024, 2048), [(0, 1), (1, -1)])
    lin(bank(5, 0, 64), A("g16", 1024, 2048), [(2, 1)])
    lin(bank(5, 64, 128), A("g16", 1024, 2048), [(0, 1)])
    al, t64, s64 = F("al", 64), F("t64", 64), F("s64", 64)
    ks = A("cx", 0, 3072)
    fill(A("cx", 0, 2048), 0)
    ts(A("prod", 1024, 2048), ccl, kc("8", 1, -8), O.is_equal)
    for k in range(2):
        c = (512 * k, 512 * k + 512)
        mms(bank(6), [(DH, sub(chi, *c)), (DL, sub(clo, *c)), (ID, A("prod", 1024 + c[0], 1024 + c[1]))])
        ts(A("xm1", *c), bank(6), 1.0, O.add)
        cp(A("CK", *c), bank(6), "s")
        mms(bank(7), [(DH2, sub(chi, *c)), (DL2, sub(clo, *c))])
        cp(A("xmb", *c), bank(7))
        ts(A("xmb", 1024 + c[0], 1024 + c[1]), bank(7), coef("64", [(0, 64), (6, 64)]), O.add)
        mms(bank(7), [(ID, A("CK", *c)), (ID, A("xmb", 1024 + c[0], 1024 + c[1])), (zall(2), sub(ind, *c))])
        cp(A("BT", *c), bank(7))
    ts(t64, c4, 2048.0, O.add)
    ts(al, bank(5, 0, 64), 0.5, O.is_gt)
    choose(s64, al, bank(4, 0, 64), t64, "s", 64)
    cp(U("s64", 64), s64)
    cp(X(ks, U("s64", 64)), A("xm1", 0, 1024))
    ts(s64, bank(5, 64, 128), -2049.0, O.add)
    tt(s64, s64, al, O.mult)
    ts(U("e64", 64), s64, 2048.0, O.add)
    ts(A("m0"), A("cx", 0, 2048), 0.0, O.is_equal)
    scan(A("sq"), A("m0"), A("cx", 0, 2048), O.mult, O.add)
    gath(bank(4, 384, 512), zc, "sq", 0, 2048)
    ts(CP, bank(4, 384, 512), -17.0, O.add)
    ts(CPF, bank(4, 384, 512), 4096.0 - 17.0, O.add)
    scan(A("a1"), A("m0"), A("m0"), O.mult, O.add)
    ts(A("oh"), A("a1"), kcol, O.is_equal)
    ts(A("sel"), A("oh"), 2.0 ** 30, O.mult, -65536.0, O.add)
    PO = U("po", 128)
    for k in range(4):
        tt(ch("px", k), X(A("ML", 1024, 2048), chunks(CP, k, 4)), ch("oh", k), O.mult)
        gath(bank(2 + k % 2, 0, 32), zneg, "px", 512 * k, 512)
        ts(chunks(PO, k, 4), bank(2 + k % 2, 0, 32), 2048.0, O.add)
        cp(ch("xs", k), X(A("xa", 0, 2048), chunks(PO, k, 4)), "s")
    ms(A("big", 2048, 2064), 0.0)
    segscan(sc, [(I23, "oh"), (BBN, "px"), (BK, "xs")], (0, 1))
    ts(A("KT", 0, 1024), X(sc, U("e64", 64)), kc("kt", -2048, 16 * 2048), O.add)
    for k in range(4):
        act(ch("sq", k), ch("xs", k), AF.Identity, -1.0, 16.0)
    segscan(A("usa"), [(zall(3), "sq")], (2, 3))
    tt(A("RT", 1024, 2048), X(A("usa"), U("e64", 64)), rt0, O.add)
    scan(A("usa", 0, 2048), A("m0"), A("xs", 0, 2048), O.mult, O.max)
    cp(A("UT", 1024, 2048), X(A("usa"), U("e64", 64)), "s")
    for k in range(2):
        cp(X(A("pt"), chunks(PO, k, 2)), ch("xmb", k, 1024))
    gath(bank(2, 0, 128), zown, "pt", 0, 2048)
    cp(POS, bank(2, 0, 128))
    lb0 = LB("lb0")
    cp(lb0, A("xmb", 0, 256))
    agents(CP, 1024, False)
    act(A("xm1"), A("xs", 0, 2048), AF.Identity, 1.0, 32.0)
    zi = None

    for t in range(4):
        cl, last = t, t == 3
        lanes = (cl, 1024, 4)
        NA, NL = 2064 + 256 * t, 768 - 256 * t
        q = T.cores[(rank + 1 + t % 7) % 8]
        h = T.cores[(rank - 1 - t % 7) % 8]
        vtr(LB("ek"), A("BT", *lanes))
        lin(bank(4, 0, 16), LB("ek"), [(0, 16), (1, 1)])
        LP = U("lp")
        ts(LP, bank(4, 0, 16), -1024.0, O.add)
        kt, mlc, rtc, uc, uv = LF("kt"), LH("mlc"), LH("rtc"), LB("uc"), LB("uv")
        cp(kt, X(A("KT", 0, NA - 1024), LP))
        cp(rtc, X(A("RT", 1024, NA), LP), "s")
        cp(mlc, X(A("ML", 1024, NA), LP), "s")
        cp(uc, X(A("UT", 1024, NA), LP), "s")
        vtr(LH("comb"), rtc)
        lin(bank(4, 32, 48), LH("comb"), [(0, 1), (1, -1)])
        lin(bank(4, 16, 32), LH("comb"), [(0, 1)])
        lin(bank(4, 160, 176), LH("comb"), [(2, 1)])
        cp(U("nU"), bank(4, 160, 176))
        ta, tb = best(kt, 256, "s", "mr", O.mult, O.max)
        ki, k4 = S("si", "ki"), S("si", "k4", 64)
        cp(ki, sub(tb, 15, 256, 16))
        ts(sub(k4, 0, 16), ki, 1023, O.bitwise_and)
        ts(sub(k4, 16, 32), ki, 11, O.arith_shift_right, 15, O.bitwise_and)
        ts(sub(k4, 32, 48), ki, 2047, O.bitwise_and)
        ts(sub(k4, 48, 64), ki, 15, O.arith_shift_right)
        cp(S("sh", "k4", 64), k4)
        s2o(S("sh", "k4", 64), bank(4, 48, 112), 64)
        cp(U("hU"), bank(4, 48, 64))
        s3 = F("s3", 48)
        cp(s3, bank(4, 64, 112))
        sg, sf, mS = sub(s3, 0, 16), sub(s3, 16, 32), sub(s3, 32, 48)
        st15, live, tmp = F("st15"), F("live"), F("tmp")
        ts(st15, bank(4, 32, 48), 15.0, O.add)
        EU = U("eu")
        ts(EU, bank(4, 16, 32), -1.0, O.add)
        ts(live, mS, 15.5, O.is_gt)
        sp = F("sp")
        tt(sp, st15, sg, O.subtract)
        dead = F("dead")
        ts(dead, mS, 15.5, O.is_lt, 4096.0, O.mult)
        tt(sp, sp, dead, O.add)
        tt(sp, sp, l2048, O.min)
        cp(U("sp"), sp)
        tt(tmp, dead, sf, O.add)
        tt(tmp, tmp, l2064, O.min)
        cp(U("vA%d" % (t % 2)), tmp)
        xsb, xbb = LB("xsb"), LB("xbb")
        cp(xsb, X(A("xs"), U("sp")))
        cp(A("acq"), X(A("act"), U("hU")))
        cp(A("XL", *lanes), xsb)
        for k in range(4):
            gt(ch("df", k), X(A("XL"), chunks(CP, k, 4)), ch("xs", k), O.subtract, k % 2)
            act(ch("sq", k), ch("df", k), AF.Square)
        byslot(sc)
        dsl, dbl, kb = LF("dsl"), LF("dbl"), LF("kb")
        ts(dsl, X(sc, EU), kneg, O.add)
        here, away = LB("here"), LB("away")
        act(here, kt, AF.Relu, 1.0, -262144.0)
        act(here, here, AF.Sign)
        mms(bank(0, 0, 256), [(N16, rtc), (K16, here)])
        tt(kb, bank(0, 0, 256), dsl, O.add)
        _, bb = best(kb, 256, "b", "mr", O.mult, O.max)
        kj = S("si", "kj")
        ts(kj, sub(bb, 15, 256, 16), 15.0, O.add)
        ts(kj, kj, 15, O.bitwise_and)
        cp(S("sh", "kj"), kj)
        s2o(S("sh", "kj"), bank(4, 112, 128), 16)
        tt(F("bp"), st15, bank(4, 112, 128), O.subtract)
        cp(U("bp"), F("bp"))
        cp(xbb, X(A("xs"), U("bp")))
        cp(A("XB", *lanes), xbb)
        for k in range(4):
            gt(ch("df", k), X(A("XB"), chunks(CP, k, 4)), ch("xs", k), O.subtract, True)
            act(ch("sq", k), ch("df", k), AF.Square)
        byslot(sc2)
        tt(away, X(sub(sc2, 0, 2048), EU), dsl, O.is_lt)
        tt(away, away, here, O.mult)
        mms(bank(0, 0, 256), [(Q1, here), (TW, away)])
        mms(bank(0, 256, 512), [(Q2, here), (TW2, away)])
        tq = LB("tq")
        tt(tq, bank(0, 256, 512), away, O.mult)
        if t:
            ts(A("TAU", cl - 1, 1024, 4), zero, 0.25, O.add)
        tt(A("TAU", *lanes), bank(0, 0, 256), tq, O.add)
        mm(bank(1, 0, 256), BB, away)
        mms(bank(1, 256, 512), [(NREP, rtc), (BBN, away)])
        nlr, mks = LB("nlr"), LH("mks")
        cp(nlr, bank(1, 0, 256), "s")
        ts(mks, bank(1, 256, 512), kcol, O.is_gt)
        if not last:
            kta = A("KT", NA - 1024, NA - 768)
            tt(kta, kt, away, O.mult)
            _, ba = best(kta, 256, "b", "mr", O.mult, O.max)
            t2, g2, k2 = kb, dbl, S("si", "k2", 32)
            ms(sub(t2, 0, 1), 0.0)
            ms(sub(tb, 15, 256, 16), 0.0)
            tt(sub(t2, 1, 256), sub(ta, 1, 256), sub(tb, 0, 255), O.min)
            scan(g2, A("mr", 0, 256), t2, O.mult, O.max)
            cp(sub(k2, 0, 16), sub(g2, 15, 256, 16))
            cp(sub(k2, 16, 32), sub(ba, 15, 256, 16))
            ts(k2, k2, 15, O.arith_shift_right)
            cp(S("sh", "k2", 32), k2)
            s2o(S("sh", "k2", 32), bank(4, 128, 160), 32)
            cp(S("sb", "k2", 32), bank(4, 128, 160))
            rows(bank(4), S("sb", "k2", 32))
            m2a = LB("m2a", 512)
            cp(m2a, bank(4), "s")
            mms(bank(4, 0, 256), [(D01, rtc), (z0(2), nlr), (z0(3), sub(m2a, 256, 512))])
            cp(A("RT", NA, NA + 256), bank(4, 0, 256), "s")
        for k in range(4):
            gt(ch("prod", k), X(A("TAU"), chunks(CP, k, 4)), ch("oh", k), O.mult, True)
            mm(bank(k % 2), B64, ch("prod", k))
            act(ch("a1", k), bank(k % 2), AF.Abs, 1.0 / 64)
            if not last:
                act(ch("xm0", k), bank(k % 2), AF.Sign)
                tt(ch("xmb", k), ch("xm0", k), ch("xm1", k), O.mult)
            act(ch("pen", k), ch("a1", k), AF.Abs, 1.0, kab)
        if not last:
            gath(bank(4, 256, 384), zbig, "prod", 0, 2048)
            cv = F("cv", 128)
            ts(cv, CPF, 0.25, O.mult, 4096.0 - cl / 4.0, O.add)
            tt(cv, bank(4, 256, 384), cv, O.min)
            tt(cv, cv, CPF, O.max)
            ts(IX, cv, -4096.0, O.add)
        segscan(sc, [(BB, "px"), (IPN, "pen")], (0, 1))
        comb, stay, dif = LH("comb"), LH("stay"), LH("dif")
        cp(comb, X(sc, EU), "s")
        tt(stay, comb, mks, O.mult)
        mms(bank(0, 0, 256), [(REV, comb), (REVN, stay)])
        cp(A("ML", NA, NA + 256), bank(0, 0, 256))
        tt(dif, mlc, stay, O.subtract)
        if not last:
            cp(X(A("xmb"), U("sp")), zero)
            scan(A("usa", 0, 2048), A("m0"), A("xmb", 0, 2048), O.mult, O.max)
            scan(A("usb"), A("m0"), A("xmb", 0, 2048), O.mult, O.min)
            ua, ub = A("UT", NA, NA + 256), LB("ub")
            ts(ua, X(A("usa"), EU), -32.0, O.add)
            ts(ub, X(A("usb"), EU), -1.0, O.mult, -32.0, O.add)
            if t < 2:
                act(A("xm1"), A("xmb", 0, 2048), AF.Relu)
        for k in range(4):
            mm(bank(2 + k % 2), CLS[cl], ch("at", k))
            act(ch("xc", k), bank(2 + k % 2), AF.Copy)
            if k % 2:
                c = (512 * k - 512, 512 * k + 512)
                dma("g", A("xc", *c), A("xa", *c), T["xc"][:, c[0]:c[1]], T["xa"][:, c[0]:c[1]], True)
        if t:
            nx = answer(t - 1, T.cores[(rank + t) % 8])
            cp(X(A("xc"), U("vA%d" % (1 - t % 2))), nx)
            cp(X(A("xa"), U("vA%d" % (1 - t % 2))), nx)
            tt(A("UT", NL + 256, NL + 512), LB("u4"), nx, O.max)
            mms(bank(5, 0, 256), [(zneg(3), nx), (Z16(3), ones)])
            tt(A("RT", NL + 256, NL + 512), bank(5, 0, 256), LH("r1"), O.max)
        hi, dl = payload(A("acq"), 256, "c", bank(3, 0, 256))
        for i in range(16):
            if i % 2:
                asel(A("cx", i, 4096, 16), xsb, [[0, 256]], O.is_ge, 0, 0)
            else:
                ts(A("cx", i, 4096, 16), xsb, 0.0, O.max)
        for k in range(8):
            if k % 4:
                tt(ch("cx", k), X(A("xc", 0, 2048), A("acq", 32 * k, 32 * k + 32)), ch("cx", k), O.subtract)
            else:
                act(ch("hx", k // 4), X(A("xc", 0, 2048), A("acq", 32 * k, 32 * k + 32)), AF.Copy)
                tt(ch("cx", k), ch("hx", k // 4), ch("cx", k), O.subtract)
            act(ch("cx", k), ch("cx", k), AF.Square)
            if k % 2:
                sums(bank(3, 32 * k - 32, 32 * k + 32), "cx", 512 * k - 512, sub(hi, 32 * k - 32, 32 * k + 32))
        nearest(bank(3, 0, 256), dl, 256, "c", bank(2, 0, 16), True)
        tt(F("fit"), bank(2, 0, 16), dead, O.max)
        ts(U("aU"), F("fit"), 2048.0, O.min)
        ag = LB("ag")
        cp(ag, X(A("at", 0, 2049), U("aU")))
        vtr(LB("agt"), ag)
        lin(bank(2, 16, 32), LB("agt"), [(6, 16), (7, 1)])
        DP, plo = U("dp"), NL + 256
        ts(DP, bank(2, 16, 32), float(-plo), O.add)
        mm(bank(5, 0, 256), CREP, ag)
        drep = LH("drep")
        cp(drep, bank(5, 0, 256), "s")
        lin(bank(3, 256, 272), LB("agt"), [(4, 16), (5, 1)])
        de32, no32 = F("de32", 32), F("no32", 32)
        df_ = sub(de32, 0, 16)
        cp(df_, bank(3, 256, 272))
        ud, rtd, y = LB("ud"), LH("rtd"), LH("y")
        cp(ud, X(A("UT", plo, NA), DP))
        cp(rtd, X(A("RT", plo, NA), DP), "s")
        cp(y, X(A("ML", plo, NA), DP), "s")
        tt(uv, ud, uc, O.max)
        mm(bank(5, 0, 256), ID, dg, True, False)
        for u in range(16):
            e0 = 256 * u
            ts(A("eq", e0 + 16 * u, e0 + 256), sub(drep, 16 * u, 256), sub(df_, u, u + 1), O.is_equal)
            mm(bank(5, 16 * u, 16 * u + 16), TW, A("eq", e0 + 16 * u, e0 + 16 * u + 16), False, u == 15)
            if u < 15:
                mm(bank(5, 16 * u + 16, 256), BB, A("eq", e0 + 16 * u + 16, e0 + 256), False, False)
        if t:
            ts(thr, n01, zi, O.mult, thr0, O.add)
        mms(bank(2, 256, 512), [(W01, uv), (WC, rtc), (WD, rtd)])
        ok1, ok2 = LB("ok1"), LB("ok2")
        act(ok1, bank(2, 256, 512), AF.Sign, 1.0, thr if t else thr0)
        act(ok2, bank(5, 0, 256), AF.Sign, 1.0, -0.5)
        tt(ok1, ok1, ok2, O.max)
        vtr(ok2, ok1)
        scan(ok1, A("mr", 0, 256), ok2, O.mult, O.max)
        s2o(sub(ok1, 15, 256, 16), bank(2, 32, 48), 16)
        ecnt = empties()
        le, de = LB("le"), LB("de", 512)
        mms(bank(6, 0, 256), [(ID, lb0), (ID, A("CK", *lanes)), (zn(2), rtc)])
        ts(le, bank(6, 0, 256), coef("nl%d" % t, [(0, NL // 16), (6, NL // 16)]), O.add)
        ts(sub(de, 0, 256), le, hi4, O.mult, cde, O.add)
        y1 = LH("y1")
        for b in range(4):
            bit = LB("bit%d" % (b % 2))
            cp(bit, X(sub(NB, 32 * b, 32 * b + 32), U("nU")))
            tt(y1, bank(6, 256, 512) if b else y, bit, O.mult)
            if b:
                cp(y, bank(6, 256, 512))
            mms(bank(6, 256, 512), [(ID, y), (SH[b], y1)])
        cp(y, bank(6, 256, 512))
        gath(bank(3, 272, 288), zall, "lb", uc[1], 256)
        want0, spl = F("want0"), F("spl")
        tt(want0, bank(3, 272, 288), mS, O.add)
        ts(want0, want0, lim2, O.is_gt)
        tt(want0, want0, live, O.mult)
        dec = S("sb", "dec", 32)
        wb, pk = S("sb", "wb", 32), F("pk", 32)
        tt(sub(wb, 0, 16), bank(2, 32, 48), want0, O.mult)
        tt(sub(wb, 16, 32), bank(2, 32, 48), live, O.mult)
        mm(bank(2, 48, 80), BB, wb)
        mm(bank(2, 80, 112), TWB, wb)
        scan(pk, A("mr", 0, 32), bank(2, 48, 80), O.mult, O.add)
        tt(pk, bank(2, 80, 112), pk, O.add)
        wk, vk, busy = sub(pk, 0, 16), F("vk"), F("busy")
        ts(spl, wk, ecnt, O.is_lt)
        ts(vk, wk, ecnt, O.min)
        tt(spl, spl, sub(wb, 0, 16), O.mult)
        tt(vk, sub(pk, 16, 32), vk, O.subtract)
        tt(busy, sub(wb, 16, 32), spl, O.is_gt)
        tt(vk, vk, l256, O.subtract)
        tt(vk, vk, busy, O.mult)
        tt(vk, vk, l256, O.add)
        cp(U("vL"), vk)
        cp(U("kU"), wk)
        ts(sub(dec, 0, 16), bank(2, 32, 48), -1.0, O.mult, 1.0, O.add)
        ts(sub(no32, 0, 16), bank(2, 32, 48), 2048.0, O.mult)
        cp(X(A("vs"), U("vL")), xsb)
        send(q, "in%d" % t, A("vs", 0, 96), "ra%d" % t, "la%d" % t)
        ts(sub(dec, 16, 32), spl, -1.0, O.mult, 1.0, O.add)
        rows(bank(3), dec)
        mr_, ns_ = bank(3, 0, 256), bank(3, 256, 512)
        eg = LB("eg")
        cp(eg, X(A("el"), U("kU")), "s")
        vtr(LB("agt"), eg)
        lin(bank(2, 112, 128), LB("agt"), [(4, 16), (5, 1)])
        DE = U("de", 32)
        cp(sub(de32, 16, 32), bank(2, 112, 128))
        ts(sub(no32, 16, 32), spl, -2048.0, O.mult, 2048.0, O.add)
        tt(no32, no32, de32, O.add)
        tt(no32, no32, l32, O.min)
        cp(DE, no32)
        ee, sd = sub(de, 256, 512), LB("sd")
        mms(bank(5, 256, 512), [(ID, lb0), (ID, eg)])
        ts(ee, bank(5, 256, 512), coef("na%d" % t, [(0, NA // 16), (6, NA // 16), (2, 1)]), O.add)
        cp(A("BT", *lanes), le)
        tt(sd, le, ee, O.subtract)
        tt(sd, ns_, sd, O.mult)
        tt(A("BT", 1024, 1280), sd, ee, O.add)
        cp(X(A("BT"), DE), de)
        if not last:
            agents(IX, 1280, last)
        tt(dif, ns_, dif, O.mult)
        tt(y1, mr_, y, O.mult)
        mms(bank(6, 0, 256), [(ID, stay), (ID, dif), (ID, y1)])
        cp(A("ML", NL, NL + 256), bank(6, 0, 256))
        if not last:
            u1, u2, u4, p1, n1 = LB("u1"), LB("u2"), LB("u4"), LH("p1"), LB("n1")
            act(n1, bank(6, 0, 256), AF.Sign)
            tt(u1, ns_, ua, O.mult)
            tt(u2, mr_, uv, O.mult)
            tt(p1, mr_, rtd, O.mult)
            tt(u1, u1, u2, O.max)
            tt(u4, u1, ub, O.max)
            mms(bank(5, 256, 512), [(zall(2), n1), (z0(3), sub(m2a, 0, 256))])
            tt(LH("r1"), bank(5, 256, 512), p1, O.max)
            mm(bank(2, 128, 144), o128, sub(dec, 0, 16))
            emit("v", lambda: g.vector.tensor_reduce(ap(F("zz", 1)), ap(bank(2, 128, 144)), AX.X, O.add), [F("zz", 1)], [bank(2, 128, 144)])
            zj, zi = S("si", "zj", 1), F("zi", 1)
            cp(zj, F("zz", 1))
            ts(zj, zj, 15, O.bitwise_and)
            cp(zi, zj)
        host(t, h)
    gath(bank(6, 0, 64), zown, "BT", 0, 1024)
    cp(U("l64", 64), bank(6, 0, 64))
    ts(A("RT", 0, 1024), X(A("ML"), U("l64", 64)), -1.0, O.mult, 2048.0, O.add)
    dma("y", None, A("RT", 0, 1024), T.ym[:, 0:1024], T["RT"][:, 0:1024])
    nx = answer(3, T.cores[(rank + 4) % 8])
    cp(X(A("xa"), U("vA1")), nx)
    dma("y", None, A("xa", 0, 2048), T.yx[:, 0:2048], T["xa"][:, 0:2048])
    issue()
